import numpy as np
import ml_dtypes


def mxq(x, axis, fmt="e4m3"):
    dtype, down = {"e4m3": (ml_dtypes.float8_e4m3fn, 7), "e5m2": (ml_dtypes.float8_e5m2, 14)}[fmt]
    v = np.moveaxis(np.asarray(x, np.float32).astype(ml_dtypes.bfloat16).astype(np.float64), axis, -1)
    blocks = v.reshape(v.shape[:-1] + (-1, 32))
    amax = np.abs(blocks).max(-1, keepdims=True)
    byte = np.maximum(np.where(amax > 0, np.frexp(amax)[1] - 1 + 127, 0) - down, 1)
    scale = np.exp2(byte - 127.0)
    codes = (blocks / scale).astype(np.float32).astype(dtype).astype(np.float64)
    return np.moveaxis((codes * scale).reshape(v.shape), -1, axis)


WIDE = False


def mx_kscale(k):
    if not WIDE:
        return np.ones(k)
    levels = np.array([10, -10, 5, -5, 0])
    if k % 512:
        return np.exp2(np.random.permutation(np.resize(levels, k // 32))).repeat(32)
    a = np.empty((k // 512, 16))
    for p in range(k // 512):
        a[p, :8] = np.random.permutation(np.resize(levels, 8))
        for g in range(8):
            far = levels[np.abs(levels - a[p, g]) >= 10]
            a[p, g + 8] = far[np.random.randint(len(far))]
    return np.exp2(a.ravel()).repeat(32)


def f64(x):
    return np.asarray(x).astype(np.float64)


def striped(idx):
    return np.tile(idx.reshape(-1, 16).T, (8, 1)).astype(np.uint16)


def unstriped(offs):
    return offs[:16].T.reshape(-1).astype(np.int64)


E2M1 = np.array([0.0, 0.5, 1.0, 1.5, 2.0, 3.0, 4.0, 6.0, -0.0, -0.5, -1.0, -1.5, -2.0, -3.0, -4.0, -6.0])


def pack_weight(w, fmt):
    k, n = w.shape
    w = f64(np.asarray(w, np.float32).astype(ml_dtypes.bfloat16)).reshape(k // 32, 32, n)
    amax = np.abs(w).max(1)
    if fmt == "e4m3":
        byte = np.frexp(amax)[1] - 1 + 127 - 7
    else:
        mant, ex = np.frexp(amax / 6.0)
        byte = np.where(mant > 0.5, ex, ex - 1) + 127
    byte = np.clip(np.where(amax > 0, byte, 1), 1, 254)
    scaled = (w * np.exp2(127.0 - byte)[:, None, :]).reshape(k, n).astype(np.float32)
    by_word = np.ascontiguousarray(scaled.reshape(k // 512, 128, 4, n).transpose(0, 1, 3, 2))
    if fmt == "e4m3":
        words = by_word.astype(ml_dtypes.float8_e4m3fn).view(np.uint8)
    else:
        c = by_word.astype(ml_dtypes.float4_e2m1fn).view(np.uint8) & 0xF
        words = (c[..., 0::2] | (c[..., 1::2] << 4)).reshape(k // 512, 128, 2 * n)
    return np.ascontiguousarray(words), np.ascontiguousarray(byte.astype(np.uint8).reshape(k // 512, 16, n))


def unpack_weight(words, scales, fmt):
    g, _, n = scales.shape
    words = np.ascontiguousarray(words).reshape(g, 128, n, -1)
    if fmt == "e4m3":
        vals = words.view(ml_dtypes.float8_e4m3fn).astype(np.float64)
    else:
        nib = np.empty((g, 128, n, 4), np.uint8)
        nib[..., 0::2] = words & 0xF
        nib[..., 1::2] = words >> 4
        vals = E2M1[nib]
    vals = vals * np.repeat(np.exp2(scales.astype(np.float64) - 127.0), 8, axis=1)[..., None]
    return vals.transpose(0, 1, 3, 2).reshape(g * 512, n)


def gelu(v):
    return 0.5 * v * (1.0 + np.tanh(np.sqrt(2.0 / np.pi) * (v + 0.044715 * v**3)))


def often(T, S):
    return np.random.permutation(T)[(T * np.random.uniform(0, 1, S) ** 4).astype(np.int64)]


K, H, N, T, S, T2, P = 1024, 1024, 512, 4096, 1024, 2048, 512

def setup_inputs():
    n = np.random.standard_normal
    s = mx_kscale(K)[:, None]
    u = mx_kscale(H)[:, None]
    tab_words, tab_scales = pack_weight(n((K, T)) * s, "e4m3")
    tab2_words, tab2_scales = pack_weight(n((K, T2)) * s, "e4m3")
    wsire_words, wsire_scales = pack_weight(n((K, H)) / np.sqrt(K) / s * u.T, "e2m1")
    return {
        "tab_words": tab_words, "tab_scales": tab_scales,
        "offs": striped(np.random.permutation(T)[:S]),
        "pos1": striped(often(S, P)),
        "tab2_words": tab2_words, "tab2_scales": tab2_scales,
        "offs2": striped(np.random.permutation(T2)[:P]),
        "wsire_words": wsire_words, "wsire_scales": wsire_scales,
        "wcalf": (n((K, H)) / np.sqrt(K) / s * u.T).astype(np.float32),
        "gain": (0.3 * n(H) / u[:, 0]).astype(np.float32),
        "wmerit": (n((H, N)) / np.sqrt(H) / u).astype(np.float32),
    }

def reference(tab_words, tab_scales, offs, pos1, tab2_words, tab2_scales, offs2,
              wsire_words, wsire_scales, wcalf, gain, wmerit):
    v = unpack_weight(tab_words, tab_scales, "e4m3")[:, unstriped(offs)]
    v2 = unpack_weight(tab2_words, tab2_scales, "e4m3")[:, unstriped(offs2)]
    ws = unpack_weight(wsire_words, wsire_scales, "e2m1")
    h = ws.T @ v
    a = h[:, unstriped(pos1)]
    b = mxq(f64(wcalf), 0, "e4m3").T @ v2
    x = a + b
    z = x + f64(gain)[:, None] * np.square(x)
    out = mxq(f64(wmerit), 0, "e4m3").T @ mxq(z, 0, "e4m3")
    return out

@@ -1,0 +1,266 @@
+from contextlib import ExitStack
+
+import concourse.mybir as mybir
+
+K, H, N, T, S, T2, C = 1024, 1024, 512, 4096, 1024, 2048, 512
+FLOPS = 2 * K * H * S + 2 * K * H * C + 2 * H * N * C
+
+F32 = mybir.dt.float32
+BF16 = mybir.dt.bfloat16
+I32 = mybir.dt.int32
+U32 = mybir.dt.uint32
+U16 = mybir.dt.uint16
+U8 = mybir.dt.uint8
+FP8X4 = mybir.dt.float8_e4m3fn_x4
+FP4X4 = mybir.dt.float4_e2m1fn_x4
+ADD = mybir.AluOpType.add
+MULT = mybir.AluOpType.mult
+COPY = mybir.ActivationFunctionType.Copy
+
+P = 128
+PACK = 4
+KP = P * PACK
+BANK = 512
+HALF = C // 2
+
+
+def tile_list_sire_calf_merit_kernel(
+    tc, tab_words, tab_scales, offs, pos1, tab2_words, tab2_scales, offs2,
+    wsire_words, wsire_scales, wcalf, gain, wmerit, out,
+):
+    nc = tc.nc
+    with ExitStack() as ctx:
+        keep = ctx.enter_context(tc.tile_pool(name="keep", bufs=1))
+        raws = ctx.enter_context(tc.tile_pool(name="raws", bufs=4))
+        stage = ctx.enter_context(tc.tile_pool(name="stage", bufs=3))
+        psum = ctx.enter_context(tc.psum_pool(name="psum", bufs=8))
+
+        def held(name, shape, dtype):
+            return keep.tile(shape, dtype, name=name, align_bytes=64)
+
+        def bank(width):
+            return psum.tile([P, width], F32, name="bank")
+
+        sire_list = held("sire_list", [P, S // 16], U16)
+        calf_list = held("calf_list", [P, C // 16], U16)
+        pick_list = held("pick_list", [P, C // 16], U16)
+
+        tab_sc = held("tab_sc", [P, T], U8)
+        ws_sc_raw = held("ws_sc_raw", [P, 2 * H], U8)
+        v_sc1 = held("v_sc1", [P, S], U8)
+        tab2_sc = held("tab2_sc", [P, T2], U8)
+        for plane in (tab_sc, ws_sc_raw, v_sc1, tab2_sc):
+            nc.vector.memset(plane[:].bitcast(I32), 0)
+
+        def load_words(name, words, a, width):
+            win = held(name, [P, width], I32)
+            nc.sync.dma_start(win[:], words[a].rearrange("p t i -> p (t i)").bitcast(I32))
+            return win
+
+        def load_rows(src):
+            raw = raws.tile([P, PACK, BANK], F32, name="raw")
+            nc.sync.dma_start(raw[:], src.rearrange("(p j) c -> p j c", j=PACK))
+            return raw
+
+        nc.sync.dma_start(sire_list[:], offs)
+        tab_w = [load_words("tab_w0", tab_words, 0, T)]
+        ws_raw = held("ws_raw", [P, 2, H // 2], I32)
+        nc.sync.dma_start(ws_raw[:], wsire_words.bitcast(I32).rearrange("a p c -> p a c"))
+        tab_w.append(load_words("tab_w1", tab_words, 1, T))
+        for q in range(4):
+            nc.gpsimd.dma_start(tab_sc[32 * q : 32 * q + 8, :].bitcast(I32), tab_scales[:, 4 * q : 4 * q + 4, :].bitcast(I32))
+        for q in range(4):
+            nc.gpsimd.dma_start(
+                ws_sc_raw[32 * q : 32 * q + 4, :].bitcast(I32).rearrange("r (a c) -> r a c", a=2),
+                wsire_scales[:, 4 * q : 4 * q + 4, :].bitcast(I32).rearrange("a r c -> r a c"),
+            )
+        wc_raw = {}
+        for a in range(2):
+            wc_raw[a, 0] = load_rows(wcalf[KP * a : KP * (a + 1), 0:KP])
+        nc.sync.dma_start(pick_list[:], pos1)
+        nc.sync.dma_start(calf_list[:], offs2)
+        tab2_w = [load_words("tab2_w%d" % a, tab2_words, a, T2) for a in range(2)]
+        g = held("g", [P, 2, PACK], F32)
+        nc.sync.dma_start(g[:], gain.rearrange("(b p t) -> p b t", b=2, t=PACK))
+        for a in range(2):
+            wc_raw[a, 1] = load_rows(wcalf[KP * a : KP * (a + 1), KP : 2 * KP])
+
+        def gather(name, win, offsets, count, dtype):
+            got = held(name, [P, count], dtype)
+            nc.vector.tensor_copy(got[:], win[:].bitcast(dtype).indirect(offsets))
+            return got
+
+        v_sc = held("v_sc", [P, S], U8)
+        nc.vector.tensor_copy(v_sc[:], tab_sc[:].indirect(sire_list[:]))
+        nc.gpsimd.dma_start(v_sc1[0:100, :].bitcast(I32), v_sc[4:104, :].bitcast(I32))
+        for q in range(4):
+            nc.gpsimd.dma_start(tab2_sc[32 * q : 32 * q + 8, :].bitcast(I32), tab2_scales[:, 4 * q : 4 * q + 4, :].bitcast(I32))
+        v0 = gather("v0", tab_w[0], sire_list[:], S, U32)
+
+        ws = held("ws", [P, 2 * H], U16)
+        nc.vector.tensor_copy(
+            ws[:].rearrange("p (g t m) -> p g t m", t=PACK, m=P),
+            ws_raw[:].rearrange("p a c -> p (a c)").bitcast(U16).rearrange("p (g m t) -> p g t m", t=PACK, m=P),
+        )
+        ws_sc = held("ws_sc", [P, 2 * H], U8)
+        nc.vector.tensor_copy(
+            ws_sc[:].rearrange("p (g t m) -> p g t m", t=PACK, m=P),
+            ws_sc_raw[:].rearrange("p (g m t) -> p g t m", t=PACK, m=P),
+        )
+        v1 = [gather("v1_%d" % u, tab_w[1], sire_list[:, 32 * u : 32 * (u + 1)], BANK, U32) for u in range(2)]
+
+        def sire_pass(acc, s, u, a):
+            cols = slice(H * a + P * s, H * a + P * (s + 1))
+            rhs = v0[:, BANK * u : BANK * (u + 1)] if a == 0 else v1[u][:]
+            nc.tensor.matmul_mx(
+                out=acc[:],
+                lhsT=ws[:, cols].bitcast(U8).bitcast(FP4X4),
+                lhsT_scale=ws_sc[:, cols],
+                rhs=rhs.bitcast(FP8X4),
+                rhs_scale=(v_sc, v_sc1)[a][:, BANK * u : BANK * (u + 1)],
+                start=(a == 0),
+                stop=(a == 1),
+            )
+
+        h = [held("h%d" % s, [P, S], F32) for s in range(8)]
+
+        def sire_slices(slices):
+            accs = {}
+            for s in slices:
+                for u in range(2):
+                    accs[s, u] = bank(BANK)
+                    sire_pass(accs[s, u], s, u, 0)
+            for s in slices:
+                for u in range(2):
+                    sire_pass(accs[s, u], s, u, 1)
+                    nc.scalar.activation(h[s][:, BANK * u : BANK * (u + 1)], accs[s, u][:], COPY)
+
+        def cast(engine, dst, src):
+            if engine == "vector":
+                nc.vector.tensor_copy(dst, src)
+            else:
+                nc.scalar.activation(dst, src, COPY)
+
+        def cast_wcalf(engine, raw):
+            grouped = stage.tile([P, PACK * BANK], BF16, name="grouped", align_bytes=64)
+            cast(engine, grouped[:].rearrange("p (t m j) -> p m j t", t=PACK, j=PACK), raw[:].rearrange("p j (m t) -> p m j t", t=PACK))
+            return grouped
+
+        def cast_wmerit(engine, raw):
+            grouped = stage.tile([P, PACK * BANK], BF16, name="grouped", align_bytes=64)
+            cast(engine, grouped[:].rearrange("p (c i j) -> p c j i", i=4, j=PACK), raw[:].rearrange("p j (c i) -> p c j i", i=4))
+            return grouped
+
+        def quantise(name, grouped, width):
+            codes = held(name + "_codes", [P, width], U32)
+            scales = held(name + "_scales", [P, width], U8)
+            nc.vector.quantize_mx(out=codes[:].bitcast(FP8X4), scales=scales[:], in_=grouped[:])
+            return codes, scales
+
+        sire_slices(range(0, 4))
+        wc = {}
+        picked = held("picked", [P, PACK, C], F32)
+        grp = cast_wcalf("vector", wc_raw[0, 0])
+        nc.vector.tensor_copy(picked[:, 0, :], h[0][:].indirect(pick_list[:]))
+        wc[0, 0] = quantise("wc00", grp, BANK)
+        grp = cast_wcalf("vector", wc_raw[1, 0])
+        nc.vector.tensor_copy(picked[:, 1, :], h[1][:].indirect(pick_list[:]))
+        wc[1, 0] = quantise("wc10", grp, BANK)
+        for s in range(4, 8):
+            sire_slices([s])
+        v2_sc = held("v2_sc", [P, C], U8)
+        nc.vector.tensor_copy(v2_sc[:], tab2_sc[:].indirect(calf_list[:]))
+        v2 = [gather("v2_0", tab2_w[0], calf_list[:], C, U32)]
+        nc.vector.tensor_copy(picked[:, 2, :], h[2][:].indirect(pick_list[:]))
+        v2.append(gather("v2_1", tab2_w[1], calf_list[:], C, U32))
+        nc.vector.tensor_copy(picked[:, 3, :], h[3][:].indirect(pick_list[:]))
+
+        def calf_slice(b, t):
+            acc = bank(C)
+            for a in range(2):
+                codes, scales = wc[a, b]
+                nc.tensor.matmul_mx(
+                    out=acc[:],
+                    lhsT=codes[:, P * t : P * (t + 1)].bitcast(FP8X4),
+                    lhsT_scale=scales[:, P * t : P * (t + 1)],
+                    rhs=v2[a][:].bitcast(FP8X4),
+                    rhs_scale=v2_sc[4 * a : P, :],
+                    start=(a == 0),
+                    stop=(a == 1),
+                )
+            return acc
+
+        def factor(dst, x, b, t):
+            nc.scalar.activation(dst, x, COPY, bias=1.0, scale=g[:, b, t : t + 1])
+
+        def make_z(name, x, f, width):
+            z = held(name, [P, PACK * width], BF16)
+            order = "p t (c i) -> p c t i"
+            nc.vector.tensor_tensor(
+                z[:].rearrange("p (c i t) -> p c t i", i=4, t=PACK), x[:].rearrange(order, i=4), f[:].rearrange(order, i=4), MULT
+            )
+            return z
+
+        wm_raw = [load_rows(wmerit[KP * b : KP * (b + 1), :]) for b in range(2)]
+
+        x0 = picked
+        f0 = held("f0", [P, PACK, C], F32)
+        for t in range(PACK):
+            acc = calf_slice(0, t)
+            nc.vector.tensor_tensor(x0[:, t, :], picked[:, t, :], acc[:], ADD)
+            factor(f0[:, t, :], x0[:, t, :], 0, t)
+        grp01 = cast_wcalf("vector", wc_raw[0, 1])
+        grp11 = cast_wcalf("scalar", wc_raw[1, 1])
+        wc[0, 1] = quantise("wc01", grp01, BANK)
+        z0 = make_z("z0", x0, f0, C)
+        wc[1, 1] = quantise("wc11", grp11, BANK)
+        own = held("own", [P, PACK, C], F32)
+        for t in range(PACK):
+            acc = calf_slice(1, t)
+            nc.scalar.activation(own[:, t, :], acc[:], COPY)
+        zq0 = quantise("zq0", z0, C)
+        grp = cast_wmerit("scalar", wm_raw[0])
+        x1 = [held("x1_%d" % u, [P, PACK, HALF], F32) for u in range(2)]
+        f1 = [held("f1_%d" % u, [P, PACK, HALF], F32) for u in range(2)]
+
+        def second_block(u):
+            for t in range(PACK):
+                nc.vector.tensor_tensor(
+                    x1[u][:, t, :], h[PACK + t][:].indirect(pick_list[:, 16 * u : 16 * (u + 1)]),
+                    own[:, t, HALF * u : HALF * (u + 1)], ADD,
+                )
+                factor(f1[u][:, t, :], x1[u][:, t, :], 1, t)
+
+        second_block(0)
+        wm = [quantise("wm0", grp, N)]
+        grp = cast_wmerit("scalar", wm_raw[1])
+        second_block(1)
+        wm.append(quantise("wm1", grp, N))
+
+        def merit_pass(acc, n, b, codes, scales):
+            nc.tensor.matmul_mx(
+                out=acc[:],
+                lhsT=wm[b][0][:, P * n : P * (n + 1)].bitcast(FP8X4),
+                lhsT_scale=wm[b][1][:, P * n : P * (n + 1)],
+                rhs=codes.bitcast(FP8X4),
+                rhs_scale=scales,
+                start=(b == 0),
+                stop=(b == 1),
+            )
+
+        accs = {}
+        for u in range(2):
+            cols = slice(HALF * u, HALF * (u + 1))
+            for n in range(4):
+                accs[u, n] = bank(HALF)
+                merit_pass(accs[u, n], n, 0, zq0[0][:, cols], zq0[1][:, cols])
+        z1 = [make_z("z1_%d" % u, x1[u], f1[u], HALF) for u in range(2)]
+        for u in range(2):
+            codes, scales = quantise("zq1_%d" % u, z1[u], HALF)
+            for n in range(4):
+                merit_pass(accs[u, n], n, 1, codes[:], scales[:])
+        for u in range(2):
+            for n in range(4):
+                res = held("res%d%d" % (u, n), [P, HALF], F32)
+                cast("scalar" if (u == 0 or n % 2 == 0) else "vector", res[:], accs[u, n][:])
+                nc.sync.dma_start(out[P * n : P * (n + 1), HALF * u : HALF * (u + 1)], res[:])

@@ -22,6 +22,7 @@ PACK = 4
 KP = P * PACK
 BANK = 512
 HALF = C // 2
+FIRST = "vector"
 
 
 def tile_list_sire_calf_merit_kernel(
@@ -31,7 +32,6 @@ def tile_list_sire_calf_merit_kernel(
     nc = tc.nc
     with ExitStack() as ctx:
         keep = ctx.enter_context(tc.tile_pool(name="keep", bufs=1))
-        raws = ctx.enter_context(tc.tile_pool(name="raws", bufs=4))
         stage = ctx.enter_context(tc.tile_pool(name="stage", bufs=3))
         psum = ctx.enter_context(tc.psum_pool(name="psum", bufs=8))
 
@@ -46,62 +46,66 @@ def tile_list_sire_calf_merit_kernel(
         pick_list = held("pick_list", [P, C // 16], U16)
 
         tab_sc = held("tab_sc", [P, T], U8)
-        ws_sc_raw = held("ws_sc_raw", [P, 2 * H], U8)
         v_sc1 = held("v_sc1", [P, S], U8)
+        ws_sc_raw = held("ws_sc_raw", [P, 2 * H], U8)
         tab2_sc = held("tab2_sc", [P, T2], U8)
         for plane in (tab_sc, ws_sc_raw, v_sc1, tab2_sc):
-            nc.vector.memset(plane[:].bitcast(I32), 0)
+            nc.gpsimd.memset(plane[:].bitcast(I32), 0)
 
         def load_words(name, words, a, width):
             win = held(name, [P, width], I32)
             nc.sync.dma_start(win[:], words[a].rearrange("p t i -> p (t i)").bitcast(I32))
             return win
 
-        def load_rows(src):
-            raw = raws.tile([P, PACK, BANK], F32, name="raw")
+        def load_rows(name, src):
+            raw = held(name, [P, PACK, BANK], F32)
             nc.sync.dma_start(raw[:], src.rearrange("(p j) c -> p j c", j=PACK))
             return raw
 
-        nc.sync.dma_start(sire_list[:], offs)
-        tab_w = [load_words("tab_w0", tab_words, 0, T)]
+        def load_planes(plane, scales):
+            for q in range(4):
+                nc.sync.dma_start(
+                    plane[32 * q : 32 * q + 4, :].bitcast(I32).rearrange("r (a c) -> r a c", a=2),
+                    scales[:, 4 * q : 4 * q + 4, :].bitcast(I32).rearrange("a r c -> r a c"),
+                )
+
         ws_raw = held("ws_raw", [P, 2, H // 2], I32)
         nc.sync.dma_start(ws_raw[:], wsire_words.bitcast(I32).rearrange("a p c -> p a c"))
+        nc.sync.dma_start(sire_list[:], offs)
+        for r in range(4):
+            nc.sync.dma_start(tab_sc[r:P:16, :].bitcast(I32), tab_scales[:, r:16:4, :].bitcast(I32).rearrange("a q c -> q a c"))
+        tab_w = [load_words("tab_w0", tab_words, 0, T)]
+        load_planes(ws_sc_raw, wsire_scales)
         tab_w.append(load_words("tab_w1", tab_words, 1, T))
-        for q in range(4):
-            nc.gpsimd.dma_start(tab_sc[32 * q : 32 * q + 8, :].bitcast(I32), tab_scales[:, 4 * q : 4 * q + 4, :].bitcast(I32))
-        for q in range(4):
-            nc.gpsimd.dma_start(
-                ws_sc_raw[32 * q : 32 * q + 4, :].bitcast(I32).rearrange("r (a c) -> r a c", a=2),
-                wsire_scales[:, 4 * q : 4 * q + 4, :].bitcast(I32).rearrange("a r c -> r a c"),
-            )
+        v_sc0 = held("v_sc0", [P, S], U8)
+        nc.vector.tensor_copy(v_sc0[:], tab_sc[:].indirect(sire_list[:]))
+        nc.sync.dma_start(v_sc1[0:100, :].bitcast(I32), v_sc0[16:116, :].bitcast(I32))
+        v_sc = [v_sc0, v_sc1]
         wc_raw = {}
         for a in range(2):
-            wc_raw[a, 0] = load_rows(wcalf[KP * a : KP * (a + 1), 0:KP])
-        nc.sync.dma_start(pick_list[:], pos1)
+            wc_raw[a, 0] = load_rows("raw%d0" % a, wcalf[KP * a : KP * (a + 1), 0:KP])
         nc.sync.dma_start(calf_list[:], offs2)
+        nc.sync.dma_start(pick_list[:], pos1)
+        for q in range(4):
+            nc.sync.dma_start(tab2_sc[32 * q : 32 * q + 8, :].bitcast(I32), tab2_scales[:, 4 * q : 4 * q + 4, :].bitcast(I32))
         tab2_w = [load_words("tab2_w%d" % a, tab2_words, a, T2) for a in range(2)]
         g = held("g", [P, 2, PACK], F32)
         nc.sync.dma_start(g[:], gain.rearrange("(b p t) -> p b t", b=2, t=PACK))
         for a in range(2):
-            wc_raw[a, 1] = load_rows(wcalf[KP * a : KP * (a + 1), KP : 2 * KP])
+            wc_raw[a, 1] = load_rows("raw%d1" % a, wcalf[KP * a : KP * (a + 1), KP : 2 * KP])
 
         def gather(name, win, offsets, count, dtype):
             got = held(name, [P, count], dtype)
             nc.vector.tensor_copy(got[:], win[:].bitcast(dtype).indirect(offsets))
             return got
 
-        v_sc = held("v_sc", [P, S], U8)
-        nc.vector.tensor_copy(v_sc[:], tab_sc[:].indirect(sire_list[:]))
-        nc.gpsimd.dma_start(v_sc1[0:100, :].bitcast(I32), v_sc[4:104, :].bitcast(I32))
-        for q in range(4):
-            nc.gpsimd.dma_start(tab2_sc[32 * q : 32 * q + 8, :].bitcast(I32), tab2_scales[:, 4 * q : 4 * q + 4, :].bitcast(I32))
-        v0 = gather("v0", tab_w[0], sire_list[:], S, U32)
-
         ws = held("ws", [P, 2 * H], U16)
         nc.vector.tensor_copy(
             ws[:].rearrange("p (g t m) -> p g t m", t=PACK, m=P),
             ws_raw[:].rearrange("p a c -> p (a c)").bitcast(U16).rearrange("p (g m t) -> p g t m", t=PACK, m=P),
         )
+        v0 = gather("v0", tab_w[0], sire_list[:], S, U32)
+
         ws_sc = held("ws_sc", [P, 2 * H], U8)
         nc.vector.tensor_copy(
             ws_sc[:].rearrange("p (g t m) -> p g t m", t=PACK, m=P),
@@ -117,7 +121,7 @@ def tile_list_sire_calf_merit_kernel(
                 lhsT=ws[:, cols].bitcast(U8).bitcast(FP4X4),
                 lhsT_scale=ws_sc[:, cols],
                 rhs=rhs.bitcast(FP8X4),
-                rhs_scale=(v_sc, v_sc1)[a][:, BANK * u : BANK * (u + 1)],
+                rhs_scale=v_sc[a][:, BANK * u : BANK * (u + 1)],
                 start=(a == 0),
                 stop=(a == 1),
             )
@@ -138,57 +142,63 @@ def tile_list_sire_calf_merit_kernel(
         def cast(engine, dst, src):
             if engine == "vector":
                 nc.vector.tensor_copy(dst, src)
+            elif engine == "gpsimd":
+                nc.gpsimd.tensor_scalar(dst, src, 1.0, 0.0, MULT, ADD)
             else:
                 nc.scalar.activation(dst, src, COPY)
 
-        def cast_wcalf(engine, raw):
-            grouped = stage.tile([P, PACK * BANK], BF16, name="grouped", align_bytes=64)
-            cast(engine, grouped[:].rearrange("p (t m j) -> p m j t", t=PACK, j=PACK), raw[:].rearrange("p j (m t) -> p m j t", t=PACK))
+        def staged():
+            return stage.tile([P, PACK * BANK], BF16, name="grouped", align_bytes=64)[:]
+
+        def cast_wcalf(engine, raw, grouped):
+            cast(engine, grouped.rearrange("p (t m j) -> p m j t", t=PACK, j=PACK), raw[:].rearrange("p j (m t) -> p m j t", t=PACK))
             return grouped
 
-        def cast_wmerit(engine, raw):
-            grouped = stage.tile([P, PACK * BANK], BF16, name="grouped", align_bytes=64)
-            cast(engine, grouped[:].rearrange("p (c i j) -> p c j i", i=4, j=PACK), raw[:].rearrange("p j (c i) -> p c j i", i=4))
+        def cast_wmerit(engine, raw, grouped):
+            cast(engine, grouped.rearrange("p (c i j) -> p c j i", i=4, j=PACK), raw[:].rearrange("p j (c i) -> p c j i", i=4))
             return grouped
 
         def quantise(name, grouped, width):
             codes = held(name + "_codes", [P, width], U32)
             scales = held(name + "_scales", [P, width], U8)
-            nc.vector.quantize_mx(out=codes[:].bitcast(FP8X4), scales=scales[:], in_=grouped[:])
-            return codes, scales
+            nc.vector.quantize_mx(out=codes[:].bitcast(FP8X4), scales=scales[:], in_=grouped)
+            return codes[:], scales[:]
 
         sire_slices(range(0, 4))
-        wc = {}
-        picked = held("picked", [P, PACK, C], F32)
-        grp = cast_wcalf("vector", wc_raw[0, 0])
-        nc.vector.tensor_copy(picked[:, 0, :], h[0][:].indirect(pick_list[:]))
-        wc[0, 0] = quantise("wc00", grp, BANK)
-        grp = cast_wcalf("vector", wc_raw[1, 0])
-        nc.vector.tensor_copy(picked[:, 1, :], h[1][:].indirect(pick_list[:]))
-        wc[1, 0] = quantise("wc10", grp, BANK)
         for s in range(4, 8):
             sire_slices([s])
+        both = held("both", [P, 2 * PACK * BANK], BF16)
+        for a in range(2):
+            cast_wcalf(FIRST, wc_raw[a, 0], both[:, PACK * BANK * a : PACK * BANK * (a + 1)])
+        picked = held("raw00", [P, PACK, C], F32)
+        for t in range(3):
+            nc.vector.tensor_copy(picked[:, t, :], h[t][:].indirect(pick_list[:]))
         v2_sc = held("v2_sc", [P, C], U8)
         nc.vector.tensor_copy(v2_sc[:], tab2_sc[:].indirect(calf_list[:]))
         v2 = [gather("v2_0", tab2_w[0], calf_list[:], C, U32)]
-        nc.vector.tensor_copy(picked[:, 2, :], h[2][:].indirect(pick_list[:]))
+        codes, scales = quantise("wc0", both[:], 2 * BANK)
+        wc = {(a, 0): (codes[:, BANK * a : BANK * (a + 1)], scales[:, BANK * a : BANK * (a + 1)]) for a in range(2)}
         v2.append(gather("v2_1", tab2_w[1], calf_list[:], C, U32))
-        nc.vector.tensor_copy(picked[:, 3, :], h[3][:].indirect(pick_list[:]))
+        picked_last = held("tab2_w1", [P, C], F32)
+        nc.vector.tensor_copy(picked_last[:], h[3][:].indirect(pick_list[:]))
 
-        def calf_slice(b, t):
-            acc = bank(C)
-            for a in range(2):
-                codes, scales = wc[a, b]
-                nc.tensor.matmul_mx(
-                    out=acc[:],
-                    lhsT=codes[:, P * t : P * (t + 1)].bitcast(FP8X4),
-                    lhsT_scale=scales[:, P * t : P * (t + 1)],
-                    rhs=v2[a][:].bitcast(FP8X4),
-                    rhs_scale=v2_sc[4 * a : P, :],
-                    start=(a == 0),
-                    stop=(a == 1),
-                )
-            return acc
+        def calf_pass(acc, b, t, a):
+            codes, scales = wc[a, b]
+            nc.tensor.matmul_mx(
+                out=acc[:],
+                lhsT=codes[:, P * t : P * (t + 1)].bitcast(FP8X4),
+                lhsT_scale=scales[:, P * t : P * (t + 1)],
+                rhs=v2[a][:].bitcast(FP8X4),
+                rhs_scale=v2_sc[4 * a : P, :],
+                start=(a == 0),
+                stop=(a == 1),
+            )
+
+        def open_calf(b):
+            accs = [bank(C) for t in range(PACK)]
+            for t in range(PACK):
+                calf_pass(accs[t], b, t, 0)
+            return accs
 
         def factor(dst, x, b, t):
             nc.scalar.activation(dst, x, COPY, bias=1.0, scale=g[:, b, t : t + 1])
@@ -199,27 +209,30 @@ def tile_list_sire_calf_merit_kernel(
             nc.vector.tensor_tensor(
                 z[:].rearrange("p (c i t) -> p c t i", i=4, t=PACK), x[:].rearrange(order, i=4), f[:].rearrange(order, i=4), MULT
             )
-            return z
+            return z[:]
 
-        wm_raw = [load_rows(wmerit[KP * b : KP * (b + 1), :]) for b in range(2)]
+        wm_raw = [load_rows(("raw10", "raw_wm1")[b], wmerit[KP * b : KP * (b + 1), :]) for b in range(2)]
 
         x0 = picked
-        f0 = held("f0", [P, PACK, C], F32)
+        f0 = held("raw11", [P, PACK, C], F32)
+        accs0 = open_calf(0)
+        grp01 = cast_wcalf("scalar", wc_raw[0, 1], staged())
+        grp11 = cast_wcalf("scalar", wc_raw[1, 1], staged())
         for t in range(PACK):
-            acc = calf_slice(0, t)
-            nc.vector.tensor_tensor(x0[:, t, :], picked[:, t, :], acc[:], ADD)
-            factor(f0[:, t, :], x0[:, t, :], 0, t)
-        grp01 = cast_wcalf("vector", wc_raw[0, 1])
-        grp11 = cast_wcalf("scalar", wc_raw[1, 1])
+            calf_pass(accs0[t], 0, t, 1)
+            nc.vector.tensor_tensor(x0[:, t, :], picked[:, t, :] if t < 3 else picked_last[:], accs0[t][:], ADD)
         wc[0, 1] = quantise("wc01", grp01, BANK)
-        z0 = make_z("z0", x0, f0, C)
+        accs1 = open_calf(1)
         wc[1, 1] = quantise("wc11", grp11, BANK)
+        for t in range(PACK):
+            factor(f0[:, t, :], x0[:, t, :], 0, t)
+        grpm0 = cast_wmerit("scalar", wm_raw[0], staged())
         own = held("own", [P, PACK, C], F32)
         for t in range(PACK):
-            acc = calf_slice(1, t)
-            nc.scalar.activation(own[:, t, :], acc[:], COPY)
-        zq0 = quantise("zq0", z0, C)
-        grp = cast_wmerit("scalar", wm_raw[0])
+            calf_pass(accs1[t], 1, t, 1)
+            nc.scalar.activation(own[:, t, :], accs1[t][:], COPY)
+        grpm1 = cast_wmerit("scalar", wm_raw[1], staged())
+        z0 = make_z("z0", x0, f0, C)
         x1 = [held("x1_%d" % u, [P, PACK, HALF], F32) for u in range(2)]
         f1 = [held("f1_%d" % u, [P, PACK, HALF], F32) for u in range(2)]
 
@@ -232,10 +245,10 @@ def tile_list_sire_calf_merit_kernel(
                 factor(f1[u][:, t, :], x1[u][:, t, :], 1, t)
 
         second_block(0)
-        wm = [quantise("wm0", grp, N)]
-        grp = cast_wmerit("scalar", wm_raw[1])
         second_block(1)
-        wm.append(quantise("wm1", grp, N))
+        wm = [quantise("wm0", grpm0, N)]
+        zq0 = quantise("zq0", z0, C)
+        wm.append(quantise("wm1", grpm1, N))
 
         def merit_pass(acc, n, b, codes, scales):
             nc.tensor.matmul_mx(
@@ -258,7 +271,7 @@ def tile_list_sire_calf_merit_kernel(
         for u in range(2):
             codes, scales = quantise("zq1_%d" % u, z1[u], HALF)
             for n in range(4):
-                merit_pass(accs[u, n], n, 1, codes[:], scales[:])
+                merit_pass(accs[u, n], n, 1, codes, scales)
         for u in range(2):
             for n in range(4):
                 res = held("res%d%d" % (u, n), [P, HALF], F32)

@@ -22,7 +22,10 @@ PACK = 4
 KP = P * PACK
 BANK = 512
 HALF = C // 2
-FIRST = "vector"
+LIST_ROWS = 16
+SHIFT = 16
+LIVE = 100
+RUN = 2
 
 
 def tile_list_sire_calf_merit_kernel(
@@ -41,45 +44,42 @@ def tile_list_sire_calf_merit_kernel(
         def bank(width):
             return psum.tile([P, width], F32, name="bank")
 
-        sire_list = held("sire_list", [P, S // 16], U16)
-        calf_list = held("calf_list", [P, C // 16], U16)
-        pick_list = held("pick_list", [P, C // 16], U16)
+        sire_list = held("sire_list", [P, S // LIST_ROWS], U16)
+        calf_list = held("calf_list", [P, C // LIST_ROWS], U16)
+        pick_list = held("pick_list", [P, C // LIST_ROWS], U16)
 
         tab_sc = held("tab_sc", [P, T], U8)
         v_sc1 = held("v_sc1", [P, S], U8)
         ws_sc_raw = held("ws_sc_raw", [P, 2 * H], U8)
         tab2_sc = held("tab2_sc", [P, T2], U8)
-        for plane in (tab_sc, ws_sc_raw, v_sc1, tab2_sc):
-            nc.gpsimd.memset(plane[:].bitcast(I32), 0)
+        for scale_tile in (tab_sc, ws_sc_raw, v_sc1, tab2_sc):
+            nc.gpsimd.memset(scale_tile[:].bitcast(I32), 0)
 
         def load_words(name, words, a, width):
-            win = held(name, [P, width], I32)
-            nc.sync.dma_start(win[:], words[a].rearrange("p t i -> p (t i)").bitcast(I32))
-            return win
+            window = held(name, [P, width], I32)
+            nc.sync.dma_start(window[:], words[a].rearrange("p t i -> p (t i)").bitcast(I32))
+            return window
 
-        def load_rows(name, src):
+        def load_rows(name, rows):
             raw = held(name, [P, PACK, BANK], F32)
-            nc.sync.dma_start(raw[:], src.rearrange("(p j) c -> p j c", j=PACK))
+            nc.sync.dma_start(raw[:], rows.rearrange("(p j) c -> p j c", j=PACK))
             return raw
-
-        def load_planes(plane, scales):
-            for q in range(4):
-                nc.sync.dma_start(
-                    plane[32 * q : 32 * q + 4, :].bitcast(I32).rearrange("r (a c) -> r a c", a=2),
-                    scales[:, 4 * q : 4 * q + 4, :].bitcast(I32).rearrange("a r c -> r a c"),
-                )
 
         ws_raw = held("ws_raw", [P, 2, H // 2], I32)
         nc.sync.dma_start(ws_raw[:], wsire_words.bitcast(I32).rearrange("a p c -> p a c"))
         nc.sync.dma_start(sire_list[:], offs)
         for r in range(4):
-            nc.sync.dma_start(tab_sc[r:P:16, :].bitcast(I32), tab_scales[:, r:16:4, :].bitcast(I32).rearrange("a q c -> q a c"))
+            nc.sync.dma_start(tab_sc[r:P:SHIFT, :].bitcast(I32), tab_scales[:, r:16:4, :].bitcast(I32).rearrange("a q c -> q a c"))
         tab_w = [load_words("tab_w0", tab_words, 0, T)]
-        load_planes(ws_sc_raw, wsire_scales)
+        for q in range(4):
+            nc.sync.dma_start(
+                ws_sc_raw[32 * q : 32 * q + 4, :].bitcast(I32).rearrange("r (a c) -> r a c", a=2),
+                wsire_scales[:, 4 * q : 4 * q + 4, :].bitcast(I32).rearrange("a r c -> r a c"),
+            )
         tab_w.append(load_words("tab_w1", tab_words, 1, T))
         v_sc0 = held("v_sc0", [P, S], U8)
         nc.vector.tensor_copy(v_sc0[:], tab_sc[:].indirect(sire_list[:]))
-        nc.sync.dma_start(v_sc1[0:100, :].bitcast(I32), v_sc0[16:116, :].bitcast(I32))
+        nc.sync.dma_start(v_sc1[0:LIVE, :].bitcast(I32), v_sc0[SHIFT : SHIFT + LIVE, :].bitcast(I32))
         v_sc = [v_sc0, v_sc1]
         wc_raw = {}
         for a in range(2):
@@ -89,73 +89,71 @@ def tile_list_sire_calf_merit_kernel(
         for q in range(4):
             nc.sync.dma_start(tab2_sc[32 * q : 32 * q + 8, :].bitcast(I32), tab2_scales[:, 4 * q : 4 * q + 4, :].bitcast(I32))
         tab2_w = [load_words("tab2_w%d" % a, tab2_words, a, T2) for a in range(2)]
-        g = held("g", [P, 2, PACK], F32)
-        nc.sync.dma_start(g[:], gain.rearrange("(b p t) -> p b t", b=2, t=PACK))
+        gains = held("g", [P, 2, PACK], F32)
+        nc.sync.dma_start(gains[:], gain.rearrange("(b p t) -> p b t", b=2, t=PACK))
         for a in range(2):
             wc_raw[a, 1] = load_rows("raw%d1" % a, wcalf[KP * a : KP * (a + 1), KP : 2 * KP])
 
-        def gather(name, win, offsets, count, dtype):
-            got = held(name, [P, count], dtype)
-            nc.vector.tensor_copy(got[:], win[:].bitcast(dtype).indirect(offsets))
-            return got
+        def gather_words(name, window, offsets, count):
+            gathered = held(name, [P, count], U32)
+            nc.vector.tensor_copy(gathered[:], window[:].bitcast(U32).indirect(offsets))
+            return gathered
 
         ws = held("ws", [P, 2 * H], U16)
         nc.vector.tensor_copy(
-            ws[:].rearrange("p (g t m) -> p g t m", t=PACK, m=P),
-            ws_raw[:].rearrange("p a c -> p (a c)").bitcast(U16).rearrange("p (g m t) -> p g t m", t=PACK, m=P),
+            ws[:].rearrange("p (e t m) -> p e t m", t=PACK, m=P),
+            ws_raw[:].rearrange("p a c -> p (a c)").bitcast(U16).rearrange("p (e m t) -> p e t m", t=PACK, m=P),
         )
-        v0 = gather("v0", tab_w[0], sire_list[:], S, U32)
-
+        v0 = gather_words("v0", tab_w[0], sire_list[:], S)
         ws_sc = held("ws_sc", [P, 2 * H], U8)
         nc.vector.tensor_copy(
-            ws_sc[:].rearrange("p (g t m) -> p g t m", t=PACK, m=P),
-            ws_sc_raw[:].rearrange("p (g m t) -> p g t m", t=PACK, m=P),
+            ws_sc[:].rearrange("p (e t m) -> p e t m", t=PACK, m=P),
+            ws_sc_raw[:].rearrange("p (e m t) -> p e t m", t=PACK, m=P),
         )
-        v1 = [gather("v1_%d" % u, tab_w[1], sire_list[:, 32 * u : 32 * (u + 1)], BANK, U32) for u in range(2)]
+        part = BANK // LIST_ROWS
+        v1 = [gather_words("v1_%d" % u, tab_w[1], sire_list[:, part * u : part * (u + 1)], BANK) for u in range(2)]
 
         def sire_pass(acc, s, u, a):
             cols = slice(H * a + P * s, H * a + P * (s + 1))
-            rhs = v0[:, BANK * u : BANK * (u + 1)] if a == 0 else v1[u][:]
+            moving = v0[:, BANK * u : BANK * (u + 1)] if a == 0 else v1[u][:]
             nc.tensor.matmul_mx(
                 out=acc[:],
                 lhsT=ws[:, cols].bitcast(U8).bitcast(FP4X4),
                 lhsT_scale=ws_sc[:, cols],
-                rhs=rhs.bitcast(FP8X4),
+                rhs=moving.bitcast(FP8X4),
                 rhs_scale=v_sc[a][:, BANK * u : BANK * (u + 1)],
                 start=(a == 0),
                 stop=(a == 1),
             )
 
-        h = [held("h%d" % s, [P, S], F32) for s in range(8)]
+        h = [held("h%d" % s, [P, S], F32) for s in range(2 * PACK)]
 
         def sire_slices(slices):
-            accs = {}
+            sums = {}
             for s in slices:
                 for u in range(2):
-                    accs[s, u] = bank(BANK)
-                    sire_pass(accs[s, u], s, u, 0)
+                    sums[s, u] = bank(BANK)
+                    sire_pass(sums[s, u], s, u, 0)
             for s in slices:
                 for u in range(2):
-                    sire_pass(accs[s, u], s, u, 1)
-                    nc.scalar.activation(h[s][:, BANK * u : BANK * (u + 1)], accs[s, u][:], COPY)
+                    sire_pass(sums[s, u], s, u, 1)
+                    nc.scalar.activation(h[s][:, BANK * u : BANK * (u + 1)], sums[s, u][:], COPY)
 
-        def cast(engine, dst, src):
-            if engine == "vector":
-                nc.vector.tensor_copy(dst, src)
-            elif engine == "gpsimd":
-                nc.gpsimd.tensor_scalar(dst, src, 1.0, 0.0, MULT, ADD)
-            else:
-                nc.scalar.activation(dst, src, COPY)
+        def on_vector(dst, src):
+            nc.vector.tensor_copy(dst, src)
+
+        def on_scalar(dst, src):
+            nc.scalar.activation(dst, src, COPY)
 
         def staged():
             return stage.tile([P, PACK * BANK], BF16, name="grouped", align_bytes=64)[:]
 
-        def cast_wcalf(engine, raw, grouped):
-            cast(engine, grouped.rearrange("p (t m j) -> p m j t", t=PACK, j=PACK), raw[:].rearrange("p j (m t) -> p m j t", t=PACK))
+        def cast_wcalf(copy, raw, grouped):
+            copy(grouped.rearrange("p (t m j) -> p m j t", t=PACK, j=PACK), raw[:].rearrange("p j (m t) -> p m j t", t=PACK))
             return grouped
 
-        def cast_wmerit(engine, raw, grouped):
-            cast(engine, grouped.rearrange("p (c i j) -> p c j i", i=4, j=PACK), raw[:].rearrange("p j (c i) -> p c j i", i=4))
+        def cast_wmerit(raw, grouped):
+            on_scalar(grouped.rearrange("p (c i j) -> p c j i", i=RUN, j=PACK), raw[:].rearrange("p j (c i) -> p c j i", i=RUN))
             return grouped
 
         def quantise(name, grouped, width):
@@ -164,26 +162,28 @@ def tile_list_sire_calf_merit_kernel(
             nc.vector.quantize_mx(out=codes[:].bitcast(FP8X4), scales=scales[:], in_=grouped)
             return codes[:], scales[:]
 
-        sire_slices(range(0, 4))
-        for s in range(4, 8):
+        sire_slices(range(0, PACK))
+        for s in range(PACK, 2 * PACK):
             sire_slices([s])
+
         both = held("both", [P, 2 * PACK * BANK], BF16)
         for a in range(2):
-            cast_wcalf(FIRST, wc_raw[a, 0], both[:, PACK * BANK * a : PACK * BANK * (a + 1)])
-        picked = held("raw00", [P, PACK, C], F32)
-        for t in range(3):
-            nc.vector.tensor_copy(picked[:, t, :], h[t][:].indirect(pick_list[:]))
+            cast_wcalf(on_vector, wc_raw[a, 0], both[:, PACK * BANK * a : PACK * BANK * (a + 1)])
+        last = PACK - 1
+        x0 = held("raw00", [P, PACK, C], F32)
+        for t in range(last):
+            nc.vector.tensor_copy(x0[:, t, :], h[t][:].indirect(pick_list[:]))
         v2_sc = held("v2_sc", [P, C], U8)
         nc.vector.tensor_copy(v2_sc[:], tab2_sc[:].indirect(calf_list[:]))
-        v2 = [gather("v2_0", tab2_w[0], calf_list[:], C, U32)]
-        codes, scales = quantise("wc0", both[:], 2 * BANK)
-        wc = {(a, 0): (codes[:, BANK * a : BANK * (a + 1)], scales[:, BANK * a : BANK * (a + 1)]) for a in range(2)}
-        v2.append(gather("v2_1", tab2_w[1], calf_list[:], C, U32))
+        v2 = [gather_words("v2_0", tab2_w[0], calf_list[:], C)]
+        both_codes, both_scales = quantise("wc0", both[:], 2 * BANK)
+        wc = {(a, 0): (both_codes[:, BANK * a : BANK * (a + 1)], both_scales[:, BANK * a : BANK * (a + 1)]) for a in range(2)}
+        v2.append(gather_words("v2_1", tab2_w[1], calf_list[:], C))
         picked_last = held("tab2_w1", [P, C], F32)
-        nc.vector.tensor_copy(picked_last[:], h[3][:].indirect(pick_list[:]))
+        nc.vector.tensor_copy(picked_last[:], h[last][:].indirect(pick_list[:]))
 
-        def calf_pass(acc, b, t, a):
-            codes, scales = wc[a, b]
+        def calf_pass(acc, rb, t, a):
+            codes, scales = wc[a, rb]
             nc.tensor.matmul_mx(
                 out=acc[:],
                 lhsT=codes[:, P * t : P * (t + 1)].bitcast(FP8X4),
@@ -194,86 +194,84 @@ def tile_list_sire_calf_merit_kernel(
                 stop=(a == 1),
             )
 
-        def open_calf(b):
-            accs = [bank(C) for t in range(PACK)]
+        def open_calf(rb):
+            sums = [bank(C) for t in range(PACK)]
             for t in range(PACK):
-                calf_pass(accs[t], b, t, 0)
-            return accs
+                calf_pass(sums[t], rb, t, 0)
+            return sums
 
-        def factor(dst, x, b, t):
-            nc.scalar.activation(dst, x, COPY, bias=1.0, scale=g[:, b, t : t + 1])
+        def factor(dst, x, rb, t):
+            nc.scalar.activation(dst, x, COPY, bias=1.0, scale=gains[:, rb, t : t + 1])
 
         def make_z(name, x, f, width):
             z = held(name, [P, PACK * width], BF16)
             order = "p t (c i) -> p c t i"
             nc.vector.tensor_tensor(
-                z[:].rearrange("p (c i t) -> p c t i", i=4, t=PACK), x[:].rearrange(order, i=4), f[:].rearrange(order, i=4), MULT
+                z[:].rearrange("p (c i t) -> p c t i", i=RUN, t=PACK), x[:].rearrange(order, i=RUN), f[:].rearrange(order, i=RUN), MULT
             )
             return z[:]
 
-        wm_raw = [load_rows(("raw10", "raw_wm1")[b], wmerit[KP * b : KP * (b + 1), :]) for b in range(2)]
+        wm_raw = [load_rows(("raw10", "raw_wm1")[rb], wmerit[KP * rb : KP * (rb + 1), :]) for rb in range(2)]
 
-        x0 = picked
         f0 = held("raw11", [P, PACK, C], F32)
-        accs0 = open_calf(0)
-        grp01 = cast_wcalf("scalar", wc_raw[0, 1], staged())
-        grp11 = cast_wcalf("scalar", wc_raw[1, 1], staged())
+        b0 = open_calf(0)
+        wc01_bf16 = cast_wcalf(on_scalar, wc_raw[0, 1], staged())
+        wc11_bf16 = cast_wcalf(on_scalar, wc_raw[1, 1], staged())
         for t in range(PACK):
-            calf_pass(accs0[t], 0, t, 1)
-            nc.vector.tensor_tensor(x0[:, t, :], picked[:, t, :] if t < 3 else picked_last[:], accs0[t][:], ADD)
-        wc[0, 1] = quantise("wc01", grp01, BANK)
-        accs1 = open_calf(1)
-        wc[1, 1] = quantise("wc11", grp11, BANK)
+            calf_pass(b0[t], 0, t, 1)
+            nc.vector.tensor_tensor(x0[:, t, :], x0[:, t, :] if t < last else picked_last[:], b0[t][:], ADD)
+        wc[0, 1] = quantise("wc01", wc01_bf16, BANK)
+        b1 = open_calf(1)
+        wc[1, 1] = quantise("wc11", wc11_bf16, BANK)
         for t in range(PACK):
             factor(f0[:, t, :], x0[:, t, :], 0, t)
-        grpm0 = cast_wmerit("scalar", wm_raw[0], staged())
+        wm0_bf16 = cast_wmerit(wm_raw[0], staged())
+
         own = held("own", [P, PACK, C], F32)
         for t in range(PACK):
-            calf_pass(accs1[t], 1, t, 1)
-            nc.scalar.activation(own[:, t, :], accs1[t][:], COPY)
-        grpm1 = cast_wmerit("scalar", wm_raw[1], staged())
+            calf_pass(b1[t], 1, t, 1)
+            on_scalar(own[:, t, :], b1[t][:])
+        wm1_bf16 = cast_wmerit(wm_raw[1], staged())
         z0 = make_z("z0", x0, f0, C)
         x1 = [held("x1_%d" % u, [P, PACK, HALF], F32) for u in range(2)]
         f1 = [held("f1_%d" % u, [P, PACK, HALF], F32) for u in range(2)]
-
-        def second_block(u):
+        half_list = HALF // LIST_ROWS
+        for u in range(2):
             for t in range(PACK):
                 nc.vector.tensor_tensor(
-                    x1[u][:, t, :], h[PACK + t][:].indirect(pick_list[:, 16 * u : 16 * (u + 1)]),
+                    x1[u][:, t, :], h[PACK + t][:].indirect(pick_list[:, half_list * u : half_list * (u + 1)]),
                     own[:, t, HALF * u : HALF * (u + 1)], ADD,
                 )
                 factor(f1[u][:, t, :], x1[u][:, t, :], 1, t)
+        wm = [quantise("wm0", wm0_bf16, N)]
+        z0_codes, z0_scales = quantise("zq0", z0, C)
+        wm.append(quantise("wm1", wm1_bf16, N))
 
-        second_block(0)
-        second_block(1)
-        wm = [quantise("wm0", grpm0, N)]
-        zq0 = quantise("zq0", z0, C)
-        wm.append(quantise("wm1", grpm1, N))
-
-        def merit_pass(acc, n, b, codes, scales):
+        def merit_pass(acc, n, rb, z_codes, z_scales):
             nc.tensor.matmul_mx(
                 out=acc[:],
-                lhsT=wm[b][0][:, P * n : P * (n + 1)].bitcast(FP8X4),
-                lhsT_scale=wm[b][1][:, P * n : P * (n + 1)],
-                rhs=codes.bitcast(FP8X4),
-                rhs_scale=scales,
-                start=(b == 0),
-                stop=(b == 1),
+                lhsT=wm[rb][0][:, P * n : P * (n + 1)].bitcast(FP8X4),
+                lhsT_scale=wm[rb][1][:, P * n : P * (n + 1)],
+                rhs=z_codes.bitcast(FP8X4),
+                rhs_scale=z_scales,
+                start=(rb == 0),
+                stop=(rb == 1),
             )
 
-        accs = {}
+        merits = {}
         for u in range(2):
-            cols = slice(HALF * u, HALF * (u + 1))
-            for n in range(4):
-                accs[u, n] = bank(HALF)
-                merit_pass(accs[u, n], n, 0, zq0[0][:, cols], zq0[1][:, cols])
+            calves = slice(HALF * u, HALF * (u + 1))
+            for n in range(N // P):
+                merits[u, n] = bank(HALF)
+                merit_pass(merits[u, n], n, 0, z0_codes[:, calves], z0_scales[:, calves])
         z1 = [make_z("z1_%d" % u, x1[u], f1[u], HALF) for u in range(2)]
         for u in range(2):
-            codes, scales = quantise("zq1_%d" % u, z1[u], HALF)
-            for n in range(4):
-                merit_pass(accs[u, n], n, 1, codes, scales)
+            z1_codes, z1_scales = quantise("zq1_%d" % u, z1[u], HALF)
+            for n in range(N // P):
+                merit_pass(merits[u, n], n, 1, z1_codes, z1_scales)
         for u in range(2):
-            for n in range(4):
+            for n in range(N // P):
                 res = held("res%d%d" % (u, n), [P, HALF], F32)
-                cast("scalar" if (u == 0 or n % 2 == 0) else "vector", res[:], accs[u, n][:])
+                copy_out = on_vector if (n % 2 == 0 and u + n > 0) else on_scalar
+                copy_out(res[:], merits[u, n][:])
                 nc.sync.dma_start(out[P * n : P * (n + 1), HALF * u : HALF * (u + 1)], res[:])

@@ -35,14 +35,13 @@ def tile_list_sire_calf_merit_kernel(
     nc = tc.nc
     with ExitStack() as ctx:
         keep = ctx.enter_context(tc.tile_pool(name="keep", bufs=1))
-        stage = ctx.enter_context(tc.tile_pool(name="stage", bufs=3))
-        psum = ctx.enter_context(tc.psum_pool(name="psum", bufs=8))
+        psum = ctx.enter_context(tc.psum_pool(name="psum", bufs=4))
 
         def held(name, shape, dtype):
             return keep.tile(shape, dtype, name=name, align_bytes=64)
 
-        def bank(width):
-            return psum.tile([P, width], F32, name="bank")
+        def bank(width, ring=0):
+            return psum.tile([P, width], F32, name="ring%d" % ring)
 
         sire_list = held("sire_list", [P, S // LIST_ROWS], U16)
         calf_list = held("calf_list", [P, C // LIST_ROWS], U16)
@@ -76,23 +75,30 @@ def tile_list_sire_calf_merit_kernel(
                 ws_sc_raw[32 * q : 32 * q + 4, :].bitcast(I32).rearrange("r (a c) -> r a c", a=2),
                 wsire_scales[:, 4 * q : 4 * q + 4, :].bitcast(I32).rearrange("a r c -> r a c"),
             )
+        nc.sync.dma_start(calf_list[:], offs2)
+        nc.sync.dma_start(pick_list[:], pos1)
         tab_w.append(load_words("tab_w1", tab_words, 1, T))
         v_sc0 = held("v_sc0", [P, S], U8)
         nc.vector.tensor_copy(v_sc0[:], tab_sc[:].indirect(sire_list[:]))
         nc.sync.dma_start(v_sc1[0:LIVE, :].bitcast(I32), v_sc0[SHIFT : SHIFT + LIVE, :].bitcast(I32))
         v_sc = [v_sc0, v_sc1]
+
+        def load_tab2_scales(a):
+            for r in range(4):
+                nc.sync.dma_start(tab2_sc[4 * a + r : P : 32, :].bitcast(I32), tab2_scales[a, r:16:4, :].bitcast(I32))
+
+        tab2_w = []
+        for a in range(2):
+            tab2_w.append(load_words("tab2_w%d" % a, tab2_words, a, T2))
+            load_tab2_scales(a)
         wc_raw = {}
-        for a in range(2):
-            wc_raw[a, 0] = load_rows("raw%d0" % a, wcalf[KP * a : KP * (a + 1), 0:KP])
-        nc.sync.dma_start(calf_list[:], offs2)
-        nc.sync.dma_start(pick_list[:], pos1)
-        for q in range(4):
-            nc.sync.dma_start(tab2_sc[32 * q : 32 * q + 8, :].bitcast(I32), tab2_scales[:, 4 * q : 4 * q + 4, :].bitcast(I32))
-        tab2_w = [load_words("tab2_w%d" % a, tab2_words, a, T2) for a in range(2)]
-        gains = held("g", [P, 2, PACK], F32)
-        nc.sync.dma_start(gains[:], gain.rearrange("(b p t) -> p b t", b=2, t=PACK))
-        for a in range(2):
-            wc_raw[a, 1] = load_rows("raw%d1" % a, wcalf[KP * a : KP * (a + 1), KP : 2 * KP])
+        for rb in range(2):
+            for a in range(2):
+                wc_raw[a, rb] = load_rows("raw%d%d" % (a, rb), wcalf[KP * a : KP * (a + 1), KP * rb : KP * (rb + 1)])
+        gains = [held(("gain0", "stage_wm1")[rb], [P, PACK], F32) for rb in range(2)]
+        for rb in range(2):
+            nc.sync.dma_start(gains[rb][:], gain[KP * rb : KP * (rb + 1)].rearrange("(p t) -> p t", t=PACK))
+        wm_raw = [load_rows("tab_w%d" % rb, wmerit[KP * rb : KP * (rb + 1), :]) for rb in range(2)]
 
         def gather_words(name, window, offsets, count):
             gathered = held(name, [P, count], U32)
@@ -105,21 +111,22 @@ def tile_list_sire_calf_merit_kernel(
             ws_raw[:].rearrange("p a c -> p (a c)").bitcast(U16).rearrange("p (e m t) -> p e t m", t=PACK, m=P),
         )
         v0 = gather_words("v0", tab_w[0], sire_list[:], S)
-        ws_sc = held("ws_sc", [P, 2 * H], U8)
-        nc.vector.tensor_copy(
-            ws_sc[:].rearrange("p (e t m) -> p e t m", t=PACK, m=P),
-            ws_sc_raw[:].rearrange("p (e m t) -> p e t m", t=PACK, m=P),
-        )
+        ws_sc = [held("ws_sc%d" % rb, [P, H], U8) for rb in range(2)]
+        for rb in range(2):
+            nc.vector.tensor_copy(
+                ws_sc[rb][:].rearrange("p (a t m) -> p a t m", t=PACK, m=P),
+                ws_sc_raw[:].rearrange("p (a b m t) -> p b a t m", a=2, t=PACK, m=P)[:, rb],
+            )
         part = BANK // LIST_ROWS
         v1 = [gather_words("v1_%d" % u, tab_w[1], sire_list[:, part * u : part * (u + 1)], BANK) for u in range(2)]
 
         def sire_pass(acc, s, u, a):
-            cols = slice(H * a + P * s, H * a + P * (s + 1))
+            rb, t = divmod(s, PACK)
             moving = v0[:, BANK * u : BANK * (u + 1)] if a == 0 else v1[u][:]
             nc.tensor.matmul_mx(
                 out=acc[:],
-                lhsT=ws[:, cols].bitcast(U8).bitcast(FP4X4),
-                lhsT_scale=ws_sc[:, cols],
+                lhsT=ws[:, H * a + P * s : H * a + P * (s + 1)].bitcast(U8).bitcast(FP4X4),
+                lhsT_scale=ws_sc[rb][:, KP * a + P * t : KP * a + P * (t + 1)],
                 rhs=moving.bitcast(FP8X4),
                 rhs_scale=v_sc[a][:, BANK * u : BANK * (u + 1)],
                 start=(a == 0),
@@ -128,16 +135,13 @@ def tile_list_sire_calf_merit_kernel(
 
         h = [held("h%d" % s, [P, S], F32) for s in range(2 * PACK)]
 
-        def sire_slices(slices):
-            sums = {}
-            for s in slices:
-                for u in range(2):
-                    sums[s, u] = bank(BANK)
-                    sire_pass(sums[s, u], s, u, 0)
-            for s in slices:
-                for u in range(2):
-                    sire_pass(sums[s, u], s, u, 1)
-                    nc.scalar.activation(h[s][:, BANK * u : BANK * (u + 1)], sums[s, u][:], COPY)
+        def sire_sums(sums):
+            banks = [bank(BANK) for s, u in sums]
+            for acc, (s, u) in zip(banks, sums):
+                sire_pass(acc, s, u, 0)
+            for acc, (s, u) in zip(banks, sums):
+                sire_pass(acc, s, u, 1)
+                nc.scalar.activation(h[s][:, BANK * u : BANK * (u + 1)], acc[:], COPY)
 
         def on_vector(dst, src):
             nc.vector.tensor_copy(dst, src)
@@ -145,15 +149,17 @@ def tile_list_sire_calf_merit_kernel(
         def on_scalar(dst, src):
             nc.scalar.activation(dst, src, COPY)
 
-        def staged():
-            return stage.tile([P, PACK * BANK], BF16, name="grouped", align_bytes=64)[:]
+        def staged(name):
+            return held(name, [P, PACK * BANK], BF16)[:]
 
-        def cast_wcalf(copy, raw, grouped):
-            copy(grouped.rearrange("p (t m j) -> p m j t", t=PACK, j=PACK), raw[:].rearrange("p j (m t) -> p m j t", t=PACK))
+        def cast_wcalf(copy, a, rb):
+            grouped = staged("stage%d%d" % (a, rb))
+            copy(grouped.rearrange("p (t m j) -> p m j t", t=PACK, j=PACK), wc_raw[a, rb][:].rearrange("p j (m t) -> p m j t", t=PACK))
             return grouped
 
-        def cast_wmerit(raw, grouped):
-            on_scalar(grouped.rearrange("p (c i j) -> p c j i", i=RUN, j=PACK), raw[:].rearrange("p j (c i) -> p c j i", i=RUN))
+        def cast_wmerit(rb):
+            grouped = staged("stage_wm%d" % rb)
+            on_scalar(grouped.rearrange("p (c i j) -> p c j i", i=RUN, j=PACK), wm_raw[rb][:].rearrange("p j (c i) -> p c j i", i=RUN))
             return grouped
 
         def quantise(name, grouped, width):
@@ -162,25 +168,24 @@ def tile_list_sire_calf_merit_kernel(
             nc.vector.quantize_mx(out=codes[:].bitcast(FP8X4), scales=scales[:], in_=grouped)
             return codes[:], scales[:]
 
-        sire_slices(range(0, PACK))
-        for s in range(PACK, 2 * PACK):
-            sire_slices([s])
+        sire_sums([(0, 0), (1, 0), (0, 1), (1, 1)])
+        for s in range(2, 2 * PACK):
+            sire_sums([(s, 0), (s, 1)])
 
-        both = held("both", [P, 2 * PACK * BANK], BF16)
-        for a in range(2):
-            cast_wcalf(on_vector, wc_raw[a, 0], both[:, PACK * BANK * a : PACK * BANK * (a + 1)])
-        last = PACK - 1
-        x0 = held("raw00", [P, PACK, C], F32)
-        for t in range(last):
-            nc.vector.tensor_copy(x0[:, t, :], h[t][:].indirect(pick_list[:]))
+        v2 = [gather_words("v2_%d" % a, tab2_w[a], calf_list[:], C) for a in range(2)]
         v2_sc = held("v2_sc", [P, C], U8)
         nc.vector.tensor_copy(v2_sc[:], tab2_sc[:].indirect(calf_list[:]))
-        v2 = [gather_words("v2_0", tab2_w[0], calf_list[:], C)]
-        both_codes, both_scales = quantise("wc0", both[:], 2 * BANK)
-        wc = {(a, 0): (both_codes[:, BANK * a : BANK * (a + 1)], both_scales[:, BANK * a : BANK * (a + 1)]) for a in range(2)}
-        v2.append(gather_words("v2_1", tab2_w[1], calf_list[:], C))
-        picked_last = held("tab2_w1", [P, C], F32)
-        nc.vector.tensor_copy(picked_last[:], h[last][:].indirect(pick_list[:]))
+        wc = {}
+        wc[0, 0] = quantise("wc00", cast_wcalf(on_vector, 0, 0), BANK)
+        x = [held("x%d" % rb, [P, PACK, C], F32) for rb in range(2)]
+        picked = {}
+
+        def pick(s, dst):
+            nc.vector.tensor_copy(dst, h[s][:].indirect(pick_list[:]))
+            picked[s] = dst
+
+        for s in range(6):
+            pick(s, x[s // PACK][:, s % PACK, :])
 
         def calf_pass(acc, rb, t, a):
             codes, scales = wc[a, rb]
@@ -195,57 +200,49 @@ def tile_list_sire_calf_merit_kernel(
             )
 
         def open_calf(rb):
-            sums = [bank(C) for t in range(PACK)]
+            sums = [bank(C, 1 - rb) for t in range(PACK)]
             for t in range(PACK):
                 calf_pass(sums[t], rb, t, 0)
             return sums
 
-        def factor(dst, x, rb, t):
-            nc.scalar.activation(dst, x, COPY, bias=1.0, scale=gains[:, rb, t : t + 1])
+        def close_calf(rb, sums):
+            for t in range(PACK):
+                calf_pass(sums[t], rb, t, 1)
+                nc.vector.tensor_tensor(x[rb][:, t, :], picked[PACK * rb + t], sums[t][:], ADD)
 
-        def make_z(name, x, f, width):
-            z = held(name, [P, PACK * width], BF16)
+        def factors(name, rb):
+            f = held(name, [P, PACK, C], F32)
+            for t in range(PACK):
+                nc.scalar.activation(f[:, t, :], x[rb][:, t, :], COPY, bias=1.0, scale=gains[rb][:, t : t + 1])
+            return f
+
+        def make_z(name, rb, f, calves):
+            z = held(name, [P, PACK * (calves.stop - calves.start)], BF16)
             order = "p t (c i) -> p c t i"
             nc.vector.tensor_tensor(
-                z[:].rearrange("p (c i t) -> p c t i", i=RUN, t=PACK), x[:].rearrange(order, i=RUN), f[:].rearrange(order, i=RUN), MULT
+                z[:].rearrange("p (c i t) -> p c t i", i=RUN, t=PACK),
+                x[rb][:, :, calves].rearrange(order, i=RUN), f[:, :, calves].rearrange(order, i=RUN), MULT,
             )
             return z[:]
 
-        wm_raw = [load_rows(("raw10", "raw_wm1")[rb], wmerit[KP * rb : KP * (rb + 1), :]) for rb in range(2)]
-
-        f0 = held("raw11", [P, PACK, C], F32)
         b0 = open_calf(0)
-        wc01_bf16 = cast_wcalf(on_scalar, wc_raw[0, 1], staged())
-        wc11_bf16 = cast_wcalf(on_scalar, wc_raw[1, 1], staged())
-        for t in range(PACK):
-            calf_pass(b0[t], 0, t, 1)
-            nc.vector.tensor_tensor(x0[:, t, :], x0[:, t, :] if t < last else picked_last[:], b0[t][:], ADD)
+        wc[1, 0] = quantise("wc10", cast_wcalf(on_scalar, 1, 0), BANK)
+        pick(7, held("stage10", [P, C], F32)[:])
+        wc01_bf16 = cast_wcalf(on_scalar, 0, 1)
+        wc11_bf16 = cast_wcalf(on_scalar, 1, 1)
+        close_calf(0, b0)
         wc[0, 1] = quantise("wc01", wc01_bf16, BANK)
         b1 = open_calf(1)
         wc[1, 1] = quantise("wc11", wc11_bf16, BANK)
-        for t in range(PACK):
-            factor(f0[:, t, :], x0[:, t, :], 0, t)
-        wm0_bf16 = cast_wmerit(wm_raw[0], staged())
-
-        own = held("own", [P, PACK, C], F32)
-        for t in range(PACK):
-            calf_pass(b1[t], 1, t, 1)
-            on_scalar(own[:, t, :], b1[t][:])
-        wm1_bf16 = cast_wmerit(wm_raw[1], staged())
-        z0 = make_z("z0", x0, f0, C)
-        x1 = [held("x1_%d" % u, [P, PACK, HALF], F32) for u in range(2)]
-        f1 = [held("f1_%d" % u, [P, PACK, HALF], F32) for u in range(2)]
-        half_list = HALF // LIST_ROWS
-        for u in range(2):
-            for t in range(PACK):
-                nc.vector.tensor_tensor(
-                    x1[u][:, t, :], h[PACK + t][:].indirect(pick_list[:, half_list * u : half_list * (u + 1)]),
-                    own[:, t, HALF * u : HALF * (u + 1)], ADD,
-                )
-                factor(f1[u][:, t, :], x1[u][:, t, :], 1, t)
+        pick(6, held("stage11", [P, C], F32)[:])
+        f0 = factors("raw11", 0)
+        wm0_bf16 = cast_wmerit(0)
+        close_calf(1, b1)
+        f1 = factors("tab_w0", 1)
+        wm1_bf16 = cast_wmerit(1)
+        z0 = make_z("z0", 0, f0, slice(0, C))
         wm = [quantise("wm0", wm0_bf16, N)]
         z0_codes, z0_scales = quantise("zq0", z0, C)
-        wm.append(quantise("wm1", wm1_bf16, N))
 
         def merit_pass(acc, n, rb, z_codes, z_scales):
             nc.tensor.matmul_mx(
@@ -258,13 +255,14 @@ def tile_list_sire_calf_merit_kernel(
                 stop=(rb == 1),
             )
 
+        halves = [slice(HALF * u, HALF * (u + 1)) for u in range(2)]
         merits = {}
         for u in range(2):
-            calves = slice(HALF * u, HALF * (u + 1))
             for n in range(N // P):
-                merits[u, n] = bank(HALF)
-                merit_pass(merits[u, n], n, 0, z0_codes[:, calves], z0_scales[:, calves])
-        z1 = [make_z("z1_%d" % u, x1[u], f1[u], HALF) for u in range(2)]
+                merits[u, n] = bank(HALF, 1 - u)
+                merit_pass(merits[u, n], n, 0, z0_codes[:, halves[u]], z0_scales[:, halves[u]])
+        z1 = [make_z("z1_%d" % u, 1, f1, halves[u]) for u in range(2)]
+        wm.append(quantise("wm1", wm1_bf16, N))
         for u in range(2):
             z1_codes, z1_scales = quantise("zq1_%d" % u, z1[u], HALF)
             for n in range(N // P):
@@ -274,4 +272,4 @@ def tile_list_sire_calf_merit_kernel(
                 res = held("res%d%d" % (u, n), [P, HALF], F32)
                 copy_out = on_vector if (n % 2 == 0 and u + n > 0) else on_scalar
                 copy_out(res[:], merits[u, n][:])
-                nc.sync.dma_start(out[P * n : P * (n + 1), HALF * u : HALF * (u + 1)], res[:])
+                nc.sync.dma_start(out[P * n : P * (n + 1), halves[u]], res[:])

@@ -157,6 +157,14 @@ def tile_list_sire_calf_merit_kernel(
             copy(grouped.rearrange("p (t m j) -> p m j t", t=PACK, j=PACK), wc_raw[a, rb][:].rearrange("p j (m t) -> p m j t", t=PACK))
             return grouped
 
+        def cast_wcalf_gpsimd(a, rb):
+            grouped = staged("stage%d%d" % (a, rb))
+            dst = grouped.rearrange("p (t m j) -> p m t j", t=PACK, j=PACK)
+            src = wc_raw[a, rb][:].rearrange("p j (m t) -> p m t j", t=PACK)
+            for m in range(0, P, 32):
+                nc.gpsimd.tensor_scalar(dst[:, m : m + 32], src[:, m : m + 32], 1.0, 0.0, MULT, ADD)
+            return grouped
+
         def cast_wmerit(rb):
             grouped = staged("stage_wm%d" % rb)
             on_scalar(grouped.rearrange("p (c i j) -> p c j i", i=RUN, j=PACK), wm_raw[rb][:].rearrange("p j (c i) -> p c j i", i=RUN))
@@ -176,7 +184,7 @@ def tile_list_sire_calf_merit_kernel(
         v2_sc = held("v2_sc", [P, C], U8)
         nc.vector.tensor_copy(v2_sc[:], tab2_sc[:].indirect(calf_list[:]))
         wc = {}
-        wc[0, 0] = quantise("wc00", cast_wcalf(on_vector, 0, 0), BANK)
+        wc[0, 0] = quantise("wc00", cast_wcalf_gpsimd(0, 0), BANK)
         x = [held("x%d" % rb, [P, PACK, C], F32) for rb in range(2)]
         picked = {}
 
@@ -184,7 +192,7 @@ def tile_list_sire_calf_merit_kernel(
             nc.vector.tensor_copy(dst, h[s][:].indirect(pick_list[:]))
             picked[s] = dst
 
-        for s in range(6):
+        for s in range(5):
             pick(s, x[s // PACK][:, s % PACK, :])
 
         def calf_pass(acc, rb, t, a):
@@ -227,20 +235,28 @@ def tile_list_sire_calf_merit_kernel(
 
         b0 = open_calf(0)
         wc[1, 0] = quantise("wc10", cast_wcalf(on_scalar, 1, 0), BANK)
-        pick(7, held("stage10", [P, C], F32)[:])
-        wc01_bf16 = cast_wcalf(on_scalar, 0, 1)
+        pick(5, held("stage10", [P, C], F32)[:])
+        wc01_bf16 = cast_wcalf_gpsimd(0, 1)
         wc11_bf16 = cast_wcalf(on_scalar, 1, 1)
         close_calf(0, b0)
         wc[0, 1] = quantise("wc01", wc01_bf16, BANK)
         b1 = open_calf(1)
         wc[1, 1] = quantise("wc11", wc11_bf16, BANK)
-        pick(6, held("stage11", [P, C], F32)[:])
+        late = held("stage11", [P, 2, C], F32)
+        pick(6, late[:, 0, :])
+        pick(7, late[:, 1, :])
         f0 = factors("raw11", 0)
+        z0 = held("z0", [P, PACK * C], BF16)[:]
+        order = "p t (c i) -> p c t i"
+        for c in range(0, C, P):
+            nc.gpsimd.tensor_tensor(
+                z0[:, PACK * c : PACK * (c + P)].rearrange("p (c i t) -> p c t i", i=RUN, t=PACK),
+                x[0][:, :, c : c + P].rearrange(order, i=RUN), f0[:, :, c : c + P].rearrange(order, i=RUN), MULT,
+            )
         wm0_bf16 = cast_wmerit(0)
         close_calf(1, b1)
         f1 = factors("tab_w0", 1)
         wm1_bf16 = cast_wmerit(1)
-        z0 = make_z("z0", 0, f0, slice(0, C))
         wm = [quantise("wm0", wm0_bf16, N)]
         z0_codes, z0_scales = quantise("zq0", z0, C)
 

@@ -66,15 +66,15 @@ def tile_list_sire_calf_merit_kernel(
 
         ws_raw = held("ws_raw", [P, 2, H // 2], I32)
         nc.sync.dma_start(ws_raw[:], wsire_words.bitcast(I32).rearrange("a p c -> p a c"))
-        nc.sync.dma_start(sire_list[:], offs)
         for r in range(4):
             nc.sync.dma_start(tab_sc[r:P:SHIFT, :].bitcast(I32), tab_scales[:, r:16:4, :].bitcast(I32).rearrange("a q c -> q a c"))
-        tab_w = [load_words("tab_w0", tab_words, 0, T)]
         for q in range(4):
             nc.sync.dma_start(
                 ws_sc_raw[32 * q : 32 * q + 4, :].bitcast(I32).rearrange("r (a c) -> r a c", a=2),
                 wsire_scales[:, 4 * q : 4 * q + 4, :].bitcast(I32).rearrange("a r c -> r a c"),
             )
+        nc.sync.dma_start(sire_list[:], offs)
+        tab_w = [load_words("tab_w0", tab_words, 0, T)]
         nc.sync.dma_start(calf_list[:], offs2)
         nc.sync.dma_start(pick_list[:], pos1)
         tab_w.append(load_words("tab_w1", tab_words, 1, T))
@@ -110,13 +110,13 @@ def tile_list_sire_calf_merit_kernel(
             ws[:].rearrange("p (e t m) -> p e t m", t=PACK, m=P),
             ws_raw[:].rearrange("p a c -> p (a c)").bitcast(U16).rearrange("p (e m t) -> p e t m", t=PACK, m=P),
         )
-        v0 = gather_words("v0", tab_w[0], sire_list[:], S)
         ws_sc = [held("ws_sc%d" % rb, [P, H], U8) for rb in range(2)]
         for rb in range(2):
             nc.vector.tensor_copy(
                 ws_sc[rb][:].rearrange("p (a t m) -> p a t m", t=PACK, m=P),
                 ws_sc_raw[:].rearrange("p (a b m t) -> p b a t m", a=2, t=PACK, m=P)[:, rb],
             )
+        v0 = gather_words("v0", tab_w[0], sire_list[:], S)
         part = BANK // LIST_ROWS
         v1 = [gather_words("v1_%d" % u, tab_w[1], sire_list[:, part * u : part * (u + 1)], BANK) for u in range(2)]
 

@@ -23,8 +23,7 @@ KP = P * PACK
 BANK = 512
 HALF = C // 2
 LIST_ROWS = 16
-SHIFT = 16
-LIVE = 100
+SPREAD = 4
 RUN = 2
 
 
@@ -48,10 +47,11 @@ def tile_list_sire_calf_merit_kernel(
         pick_list = held("pick_list", [P, C // LIST_ROWS], U16)
 
         tab_sc = held("tab_sc", [P, T], U8)
-        v_sc1 = held("v_sc1", [P, S], U8)
         ws_sc_raw = held("ws_sc_raw", [P, 2 * H], U8)
         tab2_sc = held("tab2_sc", [P, T2], U8)
-        for scale_tile in (tab_sc, ws_sc_raw, v_sc1, tab2_sc):
+        v_sc = [held("v_sc%d" % a, [P, S], U8) for a in range(2)]
+        v2_sc = held("v2_sc", [P, C], U8)
+        for scale_tile in (tab_sc, ws_sc_raw, tab2_sc, v_sc[0], v_sc[1], v2_sc):
             nc.gpsimd.memset(scale_tile[:].bitcast(I32), 0)
 
         def load_words(name, words, a, width):
@@ -66,39 +66,38 @@ def tile_list_sire_calf_merit_kernel(
 
         ws_raw = held("ws_raw", [P, 2, H // 2], I32)
         nc.sync.dma_start(ws_raw[:], wsire_words.bitcast(I32).rearrange("a p c -> p a c"))
-        for r in range(4):
-            nc.sync.dma_start(tab_sc[r:P:SHIFT, :].bitcast(I32), tab_scales[:, r:16:4, :].bitcast(I32).rearrange("a q c -> q a c"))
+        nc.sync.dma_start(sire_list[:], offs)
+
+        def load_scale_rows(window, scales):
+            nc.sync.dma_start(window[0:P:SPREAD, :].bitcast(I32), scales.bitcast(I32).rearrange("a q c -> (a q) c"))
+
+        def deal_scale_rows(plane, first, gathered, a):
+            for r in range(4):
+                start = 64 * a + SPREAD * r
+                nc.sync.dma_start(plane[first + r : P : 32, :].bitcast(I32), gathered[start : 64 * (a + 1) : 16, :].bitcast(I32))
+
+        load_scale_rows(tab_sc, tab_scales)
         for q in range(4):
             nc.sync.dma_start(
                 ws_sc_raw[32 * q : 32 * q + 4, :].bitcast(I32).rearrange("r (a c) -> r a c", a=2),
                 wsire_scales[:, 4 * q : 4 * q + 4, :].bitcast(I32).rearrange("a r c -> r a c"),
             )
-        nc.sync.dma_start(sire_list[:], offs)
         tab_w = [load_words("tab_w0", tab_words, 0, T)]
         nc.sync.dma_start(calf_list[:], offs2)
-        nc.sync.dma_start(pick_list[:], pos1)
-        tab_w.append(load_words("tab_w1", tab_words, 1, T))
-        v_sc0 = held("v_sc0", [P, S], U8)
-        nc.vector.tensor_copy(v_sc0[:], tab_sc[:].indirect(sire_list[:]))
-        nc.sync.dma_start(v_sc1[0:LIVE, :].bitcast(I32), v_sc0[SHIFT : SHIFT + LIVE, :].bitcast(I32))
-        v_sc = [v_sc0, v_sc1]
-
-        def load_tab2_scales(a):
-            for r in range(4):
-                nc.sync.dma_start(tab2_sc[4 * a + r : P : 32, :].bitcast(I32), tab2_scales[a, r:16:4, :].bitcast(I32))
-
-        tab2_w = []
+        load_scale_rows(tab2_sc, tab2_scales)
+        sire_rows = held("sire_rows", [P, S], U8)
+        nc.vector.tensor_copy(sire_rows[:], tab_sc[:].indirect(sire_list[:]))
+        tab_w.append(held("tab_w1", [P, T], I32))
+        second_words = tab_words[1].rearrange("p t i -> p (t i)").bitcast(I32)
         for a in range(2):
-            tab2_w.append(load_words("tab2_w%d" % a, tab2_words, a, T2))
-            load_tab2_scales(a)
-        wc_raw = {}
-        for rb in range(2):
-            for a in range(2):
-                wc_raw[a, rb] = load_rows("raw%d%d" % (a, rb), wcalf[KP * a : KP * (a + 1), KP * rb : KP * (rb + 1)])
-        gains = [held(("gain0", "stage_wm1")[rb], [P, PACK], F32) for rb in range(2)]
-        for rb in range(2):
-            nc.sync.dma_start(gains[rb][:], gain[KP * rb : KP * (rb + 1)].rearrange("(p t) -> p t", t=PACK))
-        wm_raw = [load_rows("tab_w%d" % rb, wmerit[KP * rb : KP * (rb + 1), :]) for rb in range(2)]
+            cols = slice(T // 2 * a, T // 2 * (a + 1))
+            nc.sync.dma_start(tab_w[1][:, cols], second_words[:, cols])
+            deal_scale_rows(v_sc[a], 0, sire_rows, a)
+        tab2_w = [load_words("tab2_w0", tab2_words, 0, T2)]
+        nc.sync.dma_start(pick_list[:], pos1)
+
+        def load_wcalf(a, rb):
+            return load_rows("raw%d%d" % (a, rb), wcalf[KP * a : KP * (a + 1), KP * rb : KP * (rb + 1)])
 
         def gather_words(name, window, offsets, count):
             gathered = held(name, [P, count], U32)
@@ -117,6 +116,20 @@ def tile_list_sire_calf_merit_kernel(
                 ws_sc_raw[:].rearrange("p (a b m t) -> p b a t m", a=2, t=PACK, m=P)[:, rb],
             )
         v0 = gather_words("v0", tab_w[0], sire_list[:], S)
+        calf_rows = held("calf_rows", [P, C], U8)
+        nc.vector.tensor_copy(calf_rows[:], tab2_sc[:].indirect(calf_list[:]))
+        wc_raw = {}
+        for a in range(2):
+            wc_raw[a, 0] = load_wcalf(a, 0)
+            deal_scale_rows(v2_sc, 4 * a, calf_rows, a)
+        tab2_w.append(load_words("tab2_w1", tab2_words, 1, T2))
+        for a in range(2):
+            wc_raw[a, 1] = load_wcalf(a, 1)
+        gains = [held(("gain0", "stage_wm1")[rb], [P, PACK], F32) for rb in range(2)]
+        for rb in range(2):
+            nc.sync.dma_start(gains[rb][:], gain[KP * rb : KP * (rb + 1)].rearrange("(p t) -> p t", t=PACK))
+        wm_raw = [load_rows("tab_w%d" % rb, wmerit[KP * rb : KP * (rb + 1), :]) for rb in range(2)]
+
         part = BANK // LIST_ROWS
         v1 = [gather_words("v1_%d" % u, tab_w[1], sire_list[:, part * u : part * (u + 1)], BANK) for u in range(2)]
 
@@ -157,12 +170,14 @@ def tile_list_sire_calf_merit_kernel(
             copy(grouped.rearrange("p (t m j) -> p m j t", t=PACK, j=PACK), wc_raw[a, rb][:].rearrange("p j (m t) -> p m j t", t=PACK))
             return grouped
 
-        def cast_wcalf_gpsimd(a, rb):
+        def cast_wcalf_gpsimd(a, rb, share=P):
             grouped = staged("stage%d%d" % (a, rb))
             dst = grouped.rearrange("p (t m j) -> p m t j", t=PACK, j=PACK)
             src = wc_raw[a, rb][:].rearrange("p j (m t) -> p m t j", t=PACK)
-            for m in range(0, P, 32):
+            for m in range(0, share, 32):
                 nc.gpsimd.tensor_scalar(dst[:, m : m + 32], src[:, m : m + 32], 1.0, 0.0, MULT, ADD)
+            if share < P:
+                on_vector(dst[:, share:P].rearrange("p m t j -> p m j t"), src[:, share:P].rearrange("p m t j -> p m j t"))
             return grouped
 
         def cast_wmerit(rb):
@@ -176,13 +191,11 @@ def tile_list_sire_calf_merit_kernel(
             nc.vector.quantize_mx(out=codes[:].bitcast(FP8X4), scales=scales[:], in_=grouped)
             return codes[:], scales[:]
 
-        sire_sums([(0, 0), (1, 0), (0, 1), (1, 1)])
+        sire_sums([(0, 0), (0, 1), (1, 0), (1, 1)])
         for s in range(2, 2 * PACK):
             sire_sums([(s, 0), (s, 1)])
 
         v2 = [gather_words("v2_%d" % a, tab2_w[a], calf_list[:], C) for a in range(2)]
-        v2_sc = held("v2_sc", [P, C], U8)
-        nc.vector.tensor_copy(v2_sc[:], tab2_sc[:].indirect(calf_list[:]))
         wc = {}
         wc[0, 0] = quantise("wc00", cast_wcalf_gpsimd(0, 0), BANK)
         x = [held("x%d" % rb, [P, PACK, C], F32) for rb in range(2)]
@@ -234,8 +247,8 @@ def tile_list_sire_calf_merit_kernel(
             return z[:]
 
         b0 = open_calf(0)
-        wc[1, 0] = quantise("wc10", cast_wcalf(on_scalar, 1, 0), BANK)
-        pick(5, held("stage10", [P, C], F32)[:])
+        wc[1, 0] = quantise("wc10", cast_wcalf_gpsimd(1, 0, P // 2), BANK)
+        pick(5, held("tab2_w1", [P, C], F32)[:])
         wc01_bf16 = cast_wcalf_gpsimd(0, 1)
         wc11_bf16 = cast_wcalf(on_scalar, 1, 1)
         close_calf(0, b0)

@@ -111,7 +111,7 @@ def tile_list_sire_calf_merit_kernel(
         )
         ws_sc = [held("ws_sc%d" % rb, [P, H], U8) for rb in range(2)]
         for rb in range(2):
-            nc.vector.tensor_copy(
+            nc.gpsimd.tensor_copy(
                 ws_sc[rb][:].rearrange("p (a t m) -> p a t m", t=PACK, m=P),
                 ws_sc_raw[:].rearrange("p (a b m t) -> p b a t m", a=2, t=PACK, m=P)[:, rb],
             )

@@ -34,12 +34,13 @@ def tile_list_sire_calf_merit_kernel(
     nc = tc.nc
     with ExitStack() as ctx:
         keep = ctx.enter_context(tc.tile_pool(name="keep", bufs=1))
+        placed = ctx.enter_context(tc.tile_pool(name="placed", bufs=1))
         psum = ctx.enter_context(tc.psum_pool(name="psum", bufs=4))
 
         def held(name, shape, dtype):
             return keep.tile(shape, dtype, name=name, align_bytes=64)
 
-        def bank(width, ring=0):
+        def bank(width, ring):
             return psum.tile([P, width], F32, name="ring%d" % ring)
 
         sire_list = held("sire_list", [P, S // LIST_ROWS], U16)
@@ -54,19 +55,12 @@ def tile_list_sire_calf_merit_kernel(
         for scale_tile in (tab_sc, ws_sc_raw, tab2_sc, v_sc[0], v_sc[1], v2_sc):
             nc.gpsimd.memset(scale_tile[:].bitcast(I32), 0)
 
-        def load_words(name, words, a, width):
-            window = held(name, [P, width], I32)
-            nc.sync.dma_start(window[:], words[a].rearrange("p t i -> p (t i)").bitcast(I32))
-            return window
+        def words_of(table, a):
+            return table[a].rearrange("p t i -> p (t i)").bitcast(I32)
 
-        def load_rows(name, rows):
-            raw = held(name, [P, PACK, BANK], F32)
-            nc.sync.dma_start(raw[:], rows.rearrange("(p j) c -> p j c", j=PACK))
-            return raw
-
-        ws_raw = held("ws_raw", [P, 2, H // 2], I32)
-        nc.sync.dma_start(ws_raw[:], wsire_words.bitcast(I32).rearrange("a p c -> p a c"))
-        nc.sync.dma_start(sire_list[:], offs)
+        def load_half(window, table, a, part):
+            cols = slice(T // 2 * part, T // 2 * (part + 1))
+            nc.sync.dma_start(window[:, cols], words_of(table, a)[:, cols])
 
         def load_scale_rows(window, scales):
             nc.sync.dma_start(window[0:P:SPREAD, :].bitcast(I32), scales.bitcast(I32).rearrange("a q c -> (a q) c"))
@@ -76,69 +70,88 @@ def tile_list_sire_calf_merit_kernel(
                 start = 64 * a + SPREAD * r
                 nc.sync.dma_start(plane[first + r : P : 32, :].bitcast(I32), gathered[start : 64 * (a + 1) : 16, :].bitcast(I32))
 
+        def gather(name, window, offsets, count, dtype):
+            gathered = held(name, [P, count], dtype)
+            nc.vector.tensor_copy(gathered[:], window.indirect(offsets))
+            return gathered
+
+        tab_w = [held("tab_w%d" % a, [P, T], I32) for a in range(2)]
+        load_half(tab_w[0], tab_words, 0, 0)
+        nc.sync.dma_start(sire_list[:], offs)
         load_scale_rows(tab_sc, tab_scales)
+        load_half(tab_w[0], tab_words, 0, 1)
+        ws_words = wsire_words.bitcast(I32).rearrange("a p (b c) -> b p a c", b=2)
+        ws_raw = [held("ws_raw%d" % rb, [P, 2, KP // RUN], I32) for rb in range(2)]
+        nc.sync.dma_start(ws_raw[0][:], ws_words[0])
         for q in range(4):
             nc.sync.dma_start(
                 ws_sc_raw[32 * q : 32 * q + 4, :].bitcast(I32).rearrange("r (a c) -> r a c", a=2),
                 wsire_scales[:, 4 * q : 4 * q + 4, :].bitcast(I32).rearrange("a r c -> r a c"),
             )
-        tab_w = [load_words("tab_w0", tab_words, 0, T)]
+        sire_rows = gather("sire_rows", tab_sc[:], sire_list[:], S, U8)
+        load_half(tab_w[1], tab_words, 1, 0)
         nc.sync.dma_start(calf_list[:], offs2)
         load_scale_rows(tab2_sc, tab2_scales)
-        sire_rows = held("sire_rows", [P, S], U8)
-        nc.vector.tensor_copy(sire_rows[:], tab_sc[:].indirect(sire_list[:]))
-        tab_w.append(held("tab_w1", [P, T], I32))
-        second_words = tab_words[1].rearrange("p t i -> p (t i)").bitcast(I32)
-        for a in range(2):
-            cols = slice(T // 2 * a, T // 2 * (a + 1))
-            nc.sync.dma_start(tab_w[1][:, cols], second_words[:, cols])
-            deal_scale_rows(v_sc[a], 0, sire_rows, a)
-        tab2_w = [load_words("tab2_w0", tab2_words, 0, T2)]
+        deal_scale_rows(v_sc[0], 0, sire_rows, 0)
+        load_half(tab_w[1], tab_words, 1, 1)
+        deal_scale_rows(v_sc[1], 0, sire_rows, 1)
+        tab2_w = [held("tab2_w%d" % a, [P, T2], I32) for a in range(2)]
+        nc.sync.dma_start(tab2_w[0][:], words_of(tab2_words, 0))
         nc.sync.dma_start(pick_list[:], pos1)
+        nc.sync.dma_start(ws_raw[1][:], ws_words[1])
 
-        def load_wcalf(a, rb):
-            return load_rows("raw%d%d" % (a, rb), wcalf[KP * a : KP * (a + 1), KP * rb : KP * (rb + 1)])
-
-        def gather_words(name, window, offsets, count):
-            gathered = held(name, [P, count], U32)
-            nc.vector.tensor_copy(gathered[:], window[:].bitcast(U32).indirect(offsets))
-            return gathered
-
-        ws = held("ws", [P, 2 * H], U16)
-        nc.vector.tensor_copy(
-            ws[:].rearrange("p (e t m) -> p e t m", t=PACK, m=P),
-            ws_raw[:].rearrange("p a c -> p (a c)").bitcast(U16).rearrange("p (e m t) -> p e t m", t=PACK, m=P),
-        )
+        v0 = gather("v0", tab_w[0][:].bitcast(U32), sire_list[:], S, U32)
+        ws = [held("ws%d" % rb, [P, KP], I32) for rb in range(2)]
+        for rb, engine in enumerate((nc.vector, nc.gpsimd)):
+            engine.tensor_copy(
+                ws[rb][:].rearrange("p (a t u) -> p a t u", t=PACK, u=P // RUN),
+                ws_raw[rb][:].rearrange("p a (u t) -> p a t u", t=PACK),
+            )
         ws_sc = [held("ws_sc%d" % rb, [P, H], U8) for rb in range(2)]
         for rb in range(2):
             nc.gpsimd.tensor_copy(
-                ws_sc[rb][:].rearrange("p (a t m) -> p a t m", t=PACK, m=P),
-                ws_sc_raw[:].rearrange("p (a b m t) -> p b a t m", a=2, t=PACK, m=P)[:, rb],
+                ws_sc[rb][:].rearrange("p (a t u i) -> p a t u i", t=PACK, u=P // RUN, i=RUN),
+                ws_sc_raw[:].rearrange("p (a b u t i) -> p b a t u i", a=2, t=PACK, u=P // RUN, i=RUN)[:, rb],
             )
-        v0 = gather_words("v0", tab_w[0], sire_list[:], S)
-        calf_rows = held("calf_rows", [P, C], U8)
-        nc.vector.tensor_copy(calf_rows[:], tab2_sc[:].indirect(calf_list[:]))
+        calf_rows = gather("calf_rows", tab2_sc[:], calf_list[:], C, U8)
+
+        def load_wcalf(a, rb):
+            if rb == 1:
+                raw = placed.tile([P, PACK, KP], F32, name="raw%d1" % a, offset=8192 * (1 - a), align_bytes=64)
+            else:
+                raw = held("raw%d%d" % (a, rb), [P, PACK, KP], F32)
+            rows = wcalf[KP * a : KP * (a + 1), KP * rb : KP * (rb + 1)]
+            nc.sync.dma_start(raw[:], rows.rearrange("(p j) c -> p j c", j=PACK))
+            return raw
+
         wc_raw = {}
         for a in range(2):
             wc_raw[a, 0] = load_wcalf(a, 0)
-            deal_scale_rows(v2_sc, 4 * a, calf_rows, a)
-        tab2_w.append(load_words("tab2_w1", tab2_words, 1, T2))
+            deal_scale_rows(v2_sc, 4 * (a + 1), calf_rows, a)
+        nc.sync.dma_start(tab2_w[1][:], words_of(tab2_words, 1))
+        gains = [held(("stage11", "stage_wm1")[rb], [P, 2 * PACK], F32) for rb in range(2)]
+        for rb in range(2):
+            for i in range(RUN):
+                eights = gain[KP * rb : KP * (rb + 1)].rearrange("(u e) -> u e", e=2 * PACK)
+                nc.sync.dma_start(gains[rb][i:P:RUN, 0:7], eights[:, i : i + 7])
         for a in range(2):
             wc_raw[a, 1] = load_wcalf(a, 1)
-        gains = [held(("gain0", "stage_wm1")[rb], [P, PACK], F32) for rb in range(2)]
+        wm_raw = [held("tab_w%d" % rb, [P, PACK, N], F32) for rb in range(2)]
         for rb in range(2):
-            nc.sync.dma_start(gains[rb][:], gain[KP * rb : KP * (rb + 1)].rearrange("(p t) -> p t", t=PACK))
-        wm_raw = [load_rows("tab_w%d" % rb, wmerit[KP * rb : KP * (rb + 1), :]) for rb in range(2)]
+            rows = wmerit[KP * rb : KP * (rb + 1), :].rearrange("(u j i) c -> j u i c", j=PACK, i=RUN)
+            for j in range(PACK):
+                nc.sync.dma_start(wm_raw[rb][:, j, :], rows[j])
 
         part = BANK // LIST_ROWS
-        v1 = [gather_words("v1_%d" % u, tab_w[1], sire_list[:, part * u : part * (u + 1)], BANK) for u in range(2)]
+        v1 = [gather("v1_%d" % u, tab_w[1][:].bitcast(U32), sire_list[:, part * u : part * (u + 1)], BANK, U32) for u in range(2)]
 
         def sire_pass(acc, s, u, a):
             rb, t = divmod(s, PACK)
             moving = v0[:, BANK * u : BANK * (u + 1)] if a == 0 else v1[u][:]
+            first = (PACK * a + t) * (P // RUN)
             nc.tensor.matmul_mx(
                 out=acc[:],
-                lhsT=ws[:, H * a + P * s : H * a + P * (s + 1)].bitcast(U8).bitcast(FP4X4),
+                lhsT=ws[rb][:, first : first + P // RUN].bitcast(U8).bitcast(FP4X4),
                 lhsT_scale=ws_sc[rb][:, KP * a + P * t : KP * a + P * (t + 1)],
                 rhs=moving.bitcast(FP8X4),
                 rhs_scale=v_sc[a][:, BANK * u : BANK * (u + 1)],
@@ -149,44 +162,41 @@ def tile_list_sire_calf_merit_kernel(
         h = [held("h%d" % s, [P, S], F32) for s in range(2 * PACK)]
 
         def sire_sums(sums):
-            banks = [bank(BANK) for s, u in sums]
+            banks = [bank(BANK, 0) for s, u in sums]
             for acc, (s, u) in zip(banks, sums):
                 sire_pass(acc, s, u, 0)
             for acc, (s, u) in zip(banks, sums):
                 sire_pass(acc, s, u, 1)
                 nc.scalar.activation(h[s][:, BANK * u : BANK * (u + 1)], acc[:], COPY)
 
-        def on_vector(dst, src):
-            nc.vector.tensor_copy(dst, src)
+        def wcalf_views(a, rb, order):
+            grouped = held("stage%d%d" % (a, rb), [P, PACK * KP], BF16)[:]
+            dst = grouped.rearrange("p (t u i j) -> p " + order, t=PACK, i=RUN, j=PACK)
+            src = wc_raw[a, rb][:].rearrange("p j (u t i) -> p " + order, t=PACK, i=RUN)
+            return grouped, dst, src
 
-        def on_scalar(dst, src):
-            nc.scalar.activation(dst, src, COPY)
-
-        def staged(name):
-            return held(name, [P, PACK * BANK], BF16)[:]
-
-        def cast_wcalf(copy, a, rb):
-            grouped = staged("stage%d%d" % (a, rb))
-            copy(grouped.rearrange("p (t m j) -> p m j t", t=PACK, j=PACK), wc_raw[a, rb][:].rearrange("p j (m t) -> p m j t", t=PACK))
+        def cast_on_gpsimd(a, rb, slices=PACK):
+            grouped, dst, src = wcalf_views(a, rb, "t u i j")
+            for t in range(slices):
+                nc.gpsimd.tensor_scalar(dst[:, t], src[:, t], 1.0, 0.0, MULT, ADD)
+            if slices < PACK:
+                order = "p t u i j -> p u t j i"
+                nc.vector.tensor_copy(dst[:, slices:].rearrange(order), src[:, slices:].rearrange(order))
             return grouped
 
-        def cast_wcalf_gpsimd(a, rb, share=P):
-            grouped = staged("stage%d%d" % (a, rb))
-            dst = grouped.rearrange("p (t m j) -> p m t j", t=PACK, j=PACK)
-            src = wc_raw[a, rb][:].rearrange("p j (m t) -> p m t j", t=PACK)
-            for m in range(0, share, 32):
-                nc.gpsimd.tensor_scalar(dst[:, m : m + 32], src[:, m : m + 32], 1.0, 0.0, MULT, ADD)
-            if share < P:
-                on_vector(dst[:, share:P].rearrange("p m t j -> p m j t"), src[:, share:P].rearrange("p m t j -> p m j t"))
+        def cast_on_scalar(a, rb):
+            grouped, dst, src = wcalf_views(a, rb, "u t j i")
+            nc.scalar.copy(dst, src)
             return grouped
 
-        def cast_wmerit(rb):
-            grouped = staged("stage_wm%d" % rb)
-            on_scalar(grouped.rearrange("p (c i j) -> p c j i", i=RUN, j=PACK), wm_raw[rb][:].rearrange("p j (c i) -> p c j i", i=RUN))
+        def cast_wmerit(rb, grouped):
+            nc.scalar.activation(
+                grouped.rearrange("p (c i j) -> p c j i", i=RUN, j=PACK),
+                wm_raw[rb][:].rearrange("p j (c i) -> p c j i", i=RUN), COPY)
             return grouped
 
-        def quantise(name, grouped, width):
-            codes = held(name + "_codes", [P, width], U32)
+        def quantise(name, grouped, width, under=None):
+            codes = held(under or name + "_codes", [P, width], U32)
             scales = held(name + "_scales", [P, width], U8)
             nc.vector.quantize_mx(out=codes[:].bitcast(FP8X4), scales=scales[:], in_=grouped)
             return codes[:], scales[:]
@@ -195,9 +205,9 @@ def tile_list_sire_calf_merit_kernel(
         for s in range(2, 2 * PACK):
             sire_sums([(s, 0), (s, 1)])
 
-        v2 = [gather_words("v2_%d" % a, tab2_w[a], calf_list[:], C) for a in range(2)]
+        v2 = [gather("v2_%d" % a, tab2_w[a][:].bitcast(U32), calf_list[:], C, U32) for a in range(2)]
         wc = {}
-        wc[0, 0] = quantise("wc00", cast_wcalf_gpsimd(0, 0), BANK)
+        wc[0, 0] = quantise("wc00", cast_on_gpsimd(0, 0), KP)
         x = [held("x%d" % rb, [P, PACK, C], F32) for rb in range(2)]
         picked = {}
 
@@ -205,8 +215,9 @@ def tile_list_sire_calf_merit_kernel(
             nc.vector.tensor_copy(dst, h[s][:].indirect(pick_list[:]))
             picked[s] = dst
 
-        for s in range(5):
-            pick(s, x[s // PACK][:, s % PACK, :])
+        pick(0, held("first_pick", [P, C], F32)[:])
+        for s in range(1, PACK):
+            pick(s, x[0][:, s, :])
 
         def calf_pass(acc, rb, t, a):
             codes, scales = wc[a, rb]
@@ -215,7 +226,7 @@ def tile_list_sire_calf_merit_kernel(
                 lhsT=codes[:, P * t : P * (t + 1)].bitcast(FP8X4),
                 lhsT_scale=scales[:, P * t : P * (t + 1)],
                 rhs=v2[a][:].bitcast(FP8X4),
-                rhs_scale=v2_sc[4 * a : P, :],
+                rhs_scale=v2_sc[4 * (a + 1) : P, :],
                 start=(a == 0),
                 stop=(a == 1),
             )
@@ -234,44 +245,41 @@ def tile_list_sire_calf_merit_kernel(
         def factors(name, rb):
             f = held(name, [P, PACK, C], F32)
             for t in range(PACK):
-                nc.scalar.activation(f[:, t, :], x[rb][:, t, :], COPY, bias=1.0, scale=gains[rb][:, t : t + 1])
+                nc.scalar.activation(f[:, t, :], x[rb][:, t, :], COPY, bias=1.0, scale=gains[rb][:, RUN * t : RUN * t + 1])
             return f
 
-        def make_z(name, rb, f, calves):
-            z = held(name, [P, PACK * (calves.stop - calves.start)], BF16)
+        def multiply(z, rb, f, calves):
             order = "p t (c i) -> p c t i"
             nc.vector.tensor_tensor(
-                z[:].rearrange("p (c i t) -> p c t i", i=RUN, t=PACK),
+                z.rearrange("p (c i t) -> p c t i", i=RUN, t=PACK),
                 x[rb][:, :, calves].rearrange(order, i=RUN), f[:, :, calves].rearrange(order, i=RUN), MULT,
             )
-            return z[:]
 
         b0 = open_calf(0)
-        wc[1, 0] = quantise("wc10", cast_wcalf_gpsimd(1, 0, P // 2), BANK)
-        pick(5, held("tab2_w1", [P, C], F32)[:])
-        wc01_bf16 = cast_wcalf_gpsimd(0, 1)
-        wc11_bf16 = cast_wcalf(on_scalar, 1, 1)
+        wc[1, 0] = quantise("wc10", cast_on_gpsimd(1, 0, PACK // 2), KP)
+        pick(4, held("raw10", [P, C], F32)[:])
+        wc01_bf16 = cast_on_gpsimd(0, 1)
         close_calf(0, b0)
-        wc[0, 1] = quantise("wc01", wc01_bf16, BANK)
+        f0 = factors("raw00", 0)
+        wc11_bf16 = cast_on_scalar(1, 1)
+        pick(5, held("first_pick", [P, C], F32)[:])
+        wc[0, 1] = quantise("wc01", wc01_bf16, KP)
         b1 = open_calf(1)
-        wc[1, 1] = quantise("wc11", wc11_bf16, BANK)
-        late = held("stage11", [P, 2, C], F32)
-        pick(6, late[:, 0, :])
-        pick(7, late[:, 1, :])
-        f0 = factors("raw11", 0)
-        z0 = held("z0", [P, PACK * C], BF16)[:]
-        order = "p t (c i) -> p c t i"
+        pick(6, placed.tile([P, C], F32, name="pick6", offset=8192 + 4096, align_bytes=64)[:])
+        wc[1, 1] = quantise("wc11", wc11_bf16, KP)
+        pick(7, placed.tile([P, C], F32, name="last_pick", offset=4096, align_bytes=64)[:])
+        z0 = placed.tile([P, PACK * C], BF16, name="z0", offset=8192, align_bytes=64)[:]
         for c in range(0, C, P):
             nc.gpsimd.tensor_tensor(
-                z0[:, PACK * c : PACK * (c + P)].rearrange("p (c i t) -> p c t i", i=RUN, t=PACK),
-                x[0][:, :, c : c + P].rearrange(order, i=RUN), f0[:, :, c : c + P].rearrange(order, i=RUN), MULT,
+                z0[:, PACK * c : PACK * (c + P)].rearrange("p (c t) -> p c t", t=PACK),
+                x[0][:, :, c : c + P].rearrange("p t c -> p c t"), f0[:, :, c : c + P].rearrange("p t c -> p c t"), MULT,
             )
-        wm0_bf16 = cast_wmerit(0)
+        wm0_bf16 = cast_wmerit(0, placed.tile([P, PACK * N], BF16, name="stage_wm0", offset=0, align_bytes=64)[:])
         close_calf(1, b1)
         f1 = factors("tab_w0", 1)
-        wm1_bf16 = cast_wmerit(1)
+        wm1_bf16 = cast_wmerit(1, held("stage_wm1", [P, PACK * N], BF16)[:])
         wm = [quantise("wm0", wm0_bf16, N)]
-        z0_codes, z0_scales = quantise("zq0", z0, C)
+        z0_codes, z0_scales = quantise("zq0", z0, C, "first_pick")
 
         def merit_pass(acc, n, rb, z_codes, z_scales):
             nc.tensor.matmul_mx(
@@ -290,7 +298,9 @@ def tile_list_sire_calf_merit_kernel(
             for n in range(N // P):
                 merits[u, n] = bank(HALF, 1 - u)
                 merit_pass(merits[u, n], n, 0, z0_codes[:, halves[u]], z0_scales[:, halves[u]])
-        z1 = [make_z("z1_%d" % u, 1, f1, halves[u]) for u in range(2)]
+        z1 = [held("z1_%d" % u, [P, PACK * HALF], BF16)[:] for u in range(2)]
+        for u in range(2):
+            multiply(z1[u], 1, f1, halves[u])
         wm.append(quantise("wm1", wm1_bf16, N))
         for u in range(2):
             z1_codes, z1_scales = quantise("zq1_%d" % u, z1[u], HALF)
@@ -299,6 +309,8 @@ def tile_list_sire_calf_merit_kernel(
         for u in range(2):
             for n in range(N // P):
                 res = held("res%d%d" % (u, n), [P, HALF], F32)
-                copy_out = on_vector if (n % 2 == 0 and u + n > 0) else on_scalar
-                copy_out(res[:], merits[u, n][:])
+                if n % 2 == 0 and u + n > 0:
+                    nc.vector.tensor_copy(res[:], merits[u, n][:])
+                else:
+                    nc.scalar.activation(res[:], merits[u, n][:], COPY)
                 nc.sync.dma_start(out[P * n : P * (n + 1), halves[u]], res[:])

@@ -79,47 +79,45 @@ def tile_list_sire_calf_merit_kernel(
         load_half(tab_w[0], tab_words, 0, 0)
         nc.sync.dma_start(sire_list[:], offs)
         load_scale_rows(tab_sc, tab_scales)
-        load_half(tab_w[0], tab_words, 0, 1)
-        ws_words = wsire_words.bitcast(I32).rearrange("a p (b c) -> b p a c", b=2)
-        ws_raw = [held("ws_raw%d" % rb, [P, 2, KP // RUN], I32) for rb in range(2)]
-        nc.sync.dma_start(ws_raw[0][:], ws_words[0])
         for q in range(4):
             nc.sync.dma_start(
                 ws_sc_raw[32 * q : 32 * q + 4, :].bitcast(I32).rearrange("r (a c) -> r a c", a=2),
                 wsire_scales[:, 4 * q : 4 * q + 4, :].bitcast(I32).rearrange("a r c -> r a c"),
             )
+        load_half(tab_w[0], tab_words, 0, 1)
         sire_rows = gather("sire_rows", tab_sc[:], sire_list[:], S, U8)
-        load_half(tab_w[1], tab_words, 1, 0)
         nc.sync.dma_start(calf_list[:], offs2)
+        ws_raw = held("ws_raw", [P, 2, H // 2], I32)
+        nc.sync.dma_start(ws_raw[:], wsire_words.bitcast(I32).rearrange("a p c -> p a c"))
         load_scale_rows(tab2_sc, tab2_scales)
+        load_half(tab_w[1], tab_words, 1, 0)
         deal_scale_rows(v_sc[0], 0, sire_rows, 0)
         load_half(tab_w[1], tab_words, 1, 1)
         deal_scale_rows(v_sc[1], 0, sire_rows, 1)
         tab2_w = [held("tab2_w%d" % a, [P, T2], I32) for a in range(2)]
         nc.sync.dma_start(tab2_w[0][:], words_of(tab2_words, 0))
         nc.sync.dma_start(pick_list[:], pos1)
-        nc.sync.dma_start(ws_raw[1][:], ws_words[1])
 
         v0 = gather("v0", tab_w[0][:].bitcast(U32), sire_list[:], S, U32)
-        ws = [held("ws%d" % rb, [P, KP], I32) for rb in range(2)]
-        for rb, engine in enumerate((nc.vector, nc.gpsimd)):
-            engine.tensor_copy(
-                ws[rb][:].rearrange("p (a t u) -> p a t u", t=PACK, u=P // RUN),
-                ws_raw[rb][:].rearrange("p a (u t) -> p a t u", t=PACK),
-            )
+        ws = held("ws", [P, 2 * H], U16)
+        nc.vector.tensor_copy(
+            ws[:].rearrange("p (e t m) -> p e t m", t=PACK, m=P),
+            ws_raw[:].rearrange("p a c -> p (a c)").bitcast(U16).rearrange("p (e m t) -> p e t m", t=PACK, m=P),
+        )
         ws_sc = [held("ws_sc%d" % rb, [P, H], U8) for rb in range(2)]
         for rb in range(2):
             nc.gpsimd.tensor_copy(
-                ws_sc[rb][:].rearrange("p (a t u i) -> p a t u i", t=PACK, u=P // RUN, i=RUN),
-                ws_sc_raw[:].rearrange("p (a b u t i) -> p b a t u i", a=2, t=PACK, u=P // RUN, i=RUN)[:, rb],
+                ws_sc[rb][:].rearrange("p (a t m) -> p a t m", t=PACK, m=P),
+                ws_sc_raw[:].rearrange("p (a b m t) -> p b a t m", a=2, t=PACK, m=P)[:, rb],
             )
+
         calf_rows = gather("calf_rows", tab2_sc[:], calf_list[:], C, U8)
 
         def load_wcalf(a, rb):
-            if rb == 1:
-                raw = placed.tile([P, PACK, KP], F32, name="raw%d1" % a, offset=8192 * (1 - a), align_bytes=64)
+            if (a, rb) == (0, 0):
+                raw = held("raw00", [P, PACK, KP], F32)
             else:
-                raw = held("raw%d%d" % (a, rb), [P, PACK, KP], F32)
+                raw = placed.tile([P, PACK, KP], F32, name="raw%d%d" % (a, rb), offset={(1, 1): 0, (0, 1): 8192, (1, 0): 16384}[a, rb], align_bytes=64)
             rows = wcalf[KP * a : KP * (a + 1), KP * rb : KP * (rb + 1)]
             nc.sync.dma_start(raw[:], rows.rearrange("(p j) c -> p j c", j=PACK))
             return raw
@@ -129,18 +127,14 @@ def tile_list_sire_calf_merit_kernel(
             wc_raw[a, 0] = load_wcalf(a, 0)
             deal_scale_rows(v2_sc, 4 * (a + 1), calf_rows, a)
         nc.sync.dma_start(tab2_w[1][:], words_of(tab2_words, 1))
-        gains = [held(("stage11", "stage_wm1")[rb], [P, 2 * PACK], F32) for rb in range(2)]
+        gains = [held(("stage11", "stage_wm1")[rb], [P, PACK], F32) for rb in range(2)]
         for rb in range(2):
-            for i in range(RUN):
-                eights = gain[KP * rb : KP * (rb + 1)].rearrange("(u e) -> u e", e=2 * PACK)
-                nc.sync.dma_start(gains[rb][i:P:RUN, 0:7], eights[:, i : i + 7])
+            nc.sync.dma_start(gains[rb][:], gain[KP * rb : KP * (rb + 1)].rearrange("(p t) -> p t", t=PACK))
         for a in range(2):
             wc_raw[a, 1] = load_wcalf(a, 1)
         wm_raw = [held("tab_w%d" % rb, [P, PACK, N], F32) for rb in range(2)]
         for rb in range(2):
-            rows = wmerit[KP * rb : KP * (rb + 1), :].rearrange("(u j i) c -> j u i c", j=PACK, i=RUN)
-            for j in range(PACK):
-                nc.sync.dma_start(wm_raw[rb][:, j, :], rows[j])
+            nc.sync.dma_start(wm_raw[rb][:], wmerit[KP * rb : KP * (rb + 1), :].rearrange("(p j) c -> p j c", j=PACK))
 
         part = BANK // LIST_ROWS
         v1 = [gather("v1_%d" % u, tab_w[1][:].bitcast(U32), sire_list[:, part * u : part * (u + 1)], BANK, U32) for u in range(2)]
@@ -148,10 +142,9 @@ def tile_list_sire_calf_merit_kernel(
         def sire_pass(acc, s, u, a):
             rb, t = divmod(s, PACK)
             moving = v0[:, BANK * u : BANK * (u + 1)] if a == 0 else v1[u][:]
-            first = (PACK * a + t) * (P // RUN)
             nc.tensor.matmul_mx(
                 out=acc[:],
-                lhsT=ws[rb][:, first : first + P // RUN].bitcast(U8).bitcast(FP4X4),
+                lhsT=ws[:, H * a + P * s : H * a + P * (s + 1)].bitcast(U8).bitcast(FP4X4),
                 lhsT_scale=ws_sc[rb][:, KP * a + P * t : KP * a + P * (t + 1)],
                 rhs=moving.bitcast(FP8X4),
                 rhs_scale=v_sc[a][:, BANK * u : BANK * (u + 1)],
@@ -159,7 +152,10 @@ def tile_list_sire_calf_merit_kernel(
                 stop=(a == 1),
             )
 
-        h = [held("h%d" % s, [P, S], F32) for s in range(2 * PACK)]
+        h = [
+            placed.tile([P, S], F32, name="h%d" % s, offset=16384 + 4096 * (s - PACK), align_bytes=64) if s in (4, 5) else held("h%d" % s, [P, S], F32)
+            for s in range(2 * PACK)
+        ]
 
         def sire_sums(sums):
             banks = [bank(BANK, 0) for s, u in sums]
@@ -169,25 +165,24 @@ def tile_list_sire_calf_merit_kernel(
                 sire_pass(acc, s, u, 1)
                 nc.scalar.activation(h[s][:, BANK * u : BANK * (u + 1)], acc[:], COPY)
 
-        def wcalf_views(a, rb, order):
-            grouped = held("stage%d%d" % (a, rb), [P, PACK * KP], BF16)[:]
-            dst = grouped.rearrange("p (t u i j) -> p " + order, t=PACK, i=RUN, j=PACK)
-            src = wc_raw[a, rb][:].rearrange("p j (u t i) -> p " + order, t=PACK, i=RUN)
-            return grouped, dst, src
+        def wcalf_views(grouped, a, rb, order):
+            dst = grouped.rearrange("p (t m j) -> p " + order, t=PACK, j=PACK)
+            src = wc_raw[a, rb][:].rearrange("p j (m t) -> p " + order, t=PACK)
+            return dst, src
 
-        def cast_on_gpsimd(a, rb, slices=PACK):
-            grouped, dst, src = wcalf_views(a, rb, "t u i j")
-            for t in range(slices):
-                nc.gpsimd.tensor_scalar(dst[:, t], src[:, t], 1.0, 0.0, MULT, ADD)
-            if slices < PACK:
-                order = "p t u i j -> p u t j i"
-                nc.vector.tensor_copy(dst[:, slices:].rearrange(order), src[:, slices:].rearrange(order))
-            return grouped
+        def cast_on_gpsimd(grouped, a, rb):
+            dst, src = wcalf_views(grouped, a, rb, "m t j")
+            for m in range(0, P, 32):
+                nc.gpsimd.tensor_scalar(dst[:, m : m + 32], src[:, m : m + 32], 1.0, 0.0, MULT, ADD)
 
-        def cast_on_scalar(a, rb):
-            grouped, dst, src = wcalf_views(a, rb, "u t j i")
-            nc.scalar.copy(dst, src)
-            return grouped
+        def cast_on_scalar(grouped, a, rb):
+            dst, src = wcalf_views(grouped, a, rb, "m j t")
+            nc.scalar.activation(dst, src, COPY)
+
+        def cast_shared(grouped, a, rb):
+            dst, src = wcalf_views(grouped, a, rb, "m j t")
+            nc.scalar.activation(dst[:, :, :, :2], src[:, :, :, :2], COPY)
+            nc.vector.tensor_copy(dst[:, :, :, 2:], src[:, :, :, 2:])
 
         def cast_wmerit(rb, grouped):
             nc.scalar.activation(
@@ -201,13 +196,17 @@ def tile_list_sire_calf_merit_kernel(
             nc.vector.quantize_mx(out=codes[:].bitcast(FP8X4), scales=scales[:], in_=grouped)
             return codes[:], scales[:]
 
+        wc00_bf16 = held("stage00", [P, PACK * KP], BF16)[:]
+        cast_on_gpsimd(wc00_bf16, 0, 0)
+        wc10_bf16 = held("stage10", [P, PACK * KP], BF16)[:]
+        cast_on_scalar(wc10_bf16, 1, 0)
         sire_sums([(0, 0), (0, 1), (1, 0), (1, 1)])
         for s in range(2, 2 * PACK):
             sire_sums([(s, 0), (s, 1)])
 
         v2 = [gather("v2_%d" % a, tab2_w[a][:].bitcast(U32), calf_list[:], C, U32) for a in range(2)]
         wc = {}
-        wc[0, 0] = quantise("wc00", cast_on_gpsimd(0, 0), KP)
+        wc[0, 0] = quantise("wc00", wc00_bf16, KP)
         x = [held("x%d" % rb, [P, PACK, C], F32) for rb in range(2)]
         picked = {}
 
@@ -215,7 +214,7 @@ def tile_list_sire_calf_merit_kernel(
             nc.vector.tensor_copy(dst, h[s][:].indirect(pick_list[:]))
             picked[s] = dst
 
-        pick(0, held("first_pick", [P, C], F32)[:])
+        pick(0, held("tab2_w0", [P, C], F32)[:])
         for s in range(1, PACK):
             pick(s, x[0][:, s, :])
 
@@ -245,24 +244,26 @@ def tile_list_sire_calf_merit_kernel(
         def factors(name, rb):
             f = held(name, [P, PACK, C], F32)
             for t in range(PACK):
-                nc.scalar.activation(f[:, t, :], x[rb][:, t, :], COPY, bias=1.0, scale=gains[rb][:, RUN * t : RUN * t + 1])
+                nc.scalar.activation(f[:, t, :], x[rb][:, t, :], COPY, bias=1.0, scale=gains[rb][:, t : t + 1])
             return f
 
-        def multiply(z, rb, f, calves):
+        def multiply(engine, z, rb, f, calves):
             order = "p t (c i) -> p c t i"
-            nc.vector.tensor_tensor(
+            engine.tensor_tensor(
                 z.rearrange("p (c i t) -> p c t i", i=RUN, t=PACK),
                 x[rb][:, :, calves].rearrange(order, i=RUN), f[:, :, calves].rearrange(order, i=RUN), MULT,
             )
 
         b0 = open_calf(0)
-        wc[1, 0] = quantise("wc10", cast_on_gpsimd(1, 0, PACK // 2), KP)
-        pick(4, held("raw10", [P, C], F32)[:])
-        wc01_bf16 = cast_on_gpsimd(0, 1)
+        wc[1, 0] = quantise("wc10", wc10_bf16, KP)
+        pick(4, held("tab2_w1", [P, C], F32)[:])
+        wc01_bf16 = held("stage01", [P, PACK * KP], BF16)[:]
+        cast_on_gpsimd(wc01_bf16, 0, 1)
         close_calf(0, b0)
         f0 = factors("raw00", 0)
-        wc11_bf16 = cast_on_scalar(1, 1)
-        pick(5, held("first_pick", [P, C], F32)[:])
+        wc11_bf16 = held("stage11", [P, PACK * KP], BF16)[:]
+        cast_shared(wc11_bf16, 1, 1)
+        pick(5, held("tab2_w0", [P, C], F32)[:])
         wc[0, 1] = quantise("wc01", wc01_bf16, KP)
         b1 = open_calf(1)
         pick(6, placed.tile([P, C], F32, name="pick6", offset=8192 + 4096, align_bytes=64)[:])
@@ -270,16 +271,13 @@ def tile_list_sire_calf_merit_kernel(
         pick(7, placed.tile([P, C], F32, name="last_pick", offset=4096, align_bytes=64)[:])
         z0 = placed.tile([P, PACK * C], BF16, name="z0", offset=8192, align_bytes=64)[:]
         for c in range(0, C, P):
-            nc.gpsimd.tensor_tensor(
-                z0[:, PACK * c : PACK * (c + P)].rearrange("p (c t) -> p c t", t=PACK),
-                x[0][:, :, c : c + P].rearrange("p t c -> p c t"), f0[:, :, c : c + P].rearrange("p t c -> p c t"), MULT,
-            )
+            multiply(nc.gpsimd, z0[:, PACK * c : PACK * (c + P)], 0, f0, slice(c, c + P))
         wm0_bf16 = cast_wmerit(0, placed.tile([P, PACK * N], BF16, name="stage_wm0", offset=0, align_bytes=64)[:])
         close_calf(1, b1)
         f1 = factors("tab_w0", 1)
         wm1_bf16 = cast_wmerit(1, held("stage_wm1", [P, PACK * N], BF16)[:])
         wm = [quantise("wm0", wm0_bf16, N)]
-        z0_codes, z0_scales = quantise("zq0", z0, C, "first_pick")
+        z0_codes, z0_scales = quantise("zq0", z0, C, "tab2_w0")
 
         def merit_pass(acc, n, rb, z_codes, z_scales):
             nc.tensor.matmul_mx(
@@ -300,7 +298,7 @@ def tile_list_sire_calf_merit_kernel(
                 merit_pass(merits[u, n], n, 0, z0_codes[:, halves[u]], z0_scales[:, halves[u]])
         z1 = [held("z1_%d" % u, [P, PACK * HALF], BF16)[:] for u in range(2)]
         for u in range(2):
-            multiply(z1[u], 1, f1, halves[u])
+            multiply(nc.vector, z1[u], 1, f1, halves[u])
         wm.append(quantise("wm1", wm1_bf16, N))
         for u in range(2):
             z1_codes, z1_scales = quantise("zq1_%d" % u, z1[u], HALF)

@@ -153,12 +153,12 @@ def tile_list_sire_calf_merit_kernel(
             )
 
         h = [
-            placed.tile([P, S], F32, name="h%d" % s, offset=16384 + 4096 * (s - PACK), align_bytes=64) if s in (4, 5) else held("h%d" % s, [P, S], F32)
+            placed.tile([P, S], F32, name="h%d" % s, offset={4: 16384, 5: 20480, 7: 4096}[s], align_bytes=64) if s in (4, 5, 7) else held("h%d" % s, [P, S], F32)
             for s in range(2 * PACK)
         ]
 
-        def sire_sums(sums):
-            banks = [bank(BANK, 0) for s, u in sums]
+        def sire_sums(sums, ring):
+            banks = [bank(BANK, ring) for s, u in sums]
             for acc, (s, u) in zip(banks, sums):
                 sire_pass(acc, s, u, 0)
             for acc, (s, u) in zip(banks, sums):
@@ -184,10 +184,10 @@ def tile_list_sire_calf_merit_kernel(
             nc.scalar.activation(dst[:, :, :, :2], src[:, :, :, :2], COPY)
             nc.vector.tensor_copy(dst[:, :, :, 2:], src[:, :, :, 2:])
 
-        def cast_wmerit(rb, grouped):
+        def cast_wmerit(rb, grouped, cols):
             nc.scalar.activation(
                 grouped.rearrange("p (c i j) -> p c j i", i=RUN, j=PACK),
-                wm_raw[rb][:].rearrange("p j (c i) -> p c j i", i=RUN), COPY)
+                wm_raw[rb][:, :, cols].rearrange("p j (c i) -> p c j i", i=RUN), COPY)
             return grouped
 
         def quantise(name, grouped, width, under=None):
@@ -200,9 +200,9 @@ def tile_list_sire_calf_merit_kernel(
         cast_on_gpsimd(wc00_bf16, 0, 0)
         wc10_bf16 = held("stage10", [P, PACK * KP], BF16)[:]
         cast_on_scalar(wc10_bf16, 1, 0)
-        sire_sums([(0, 0), (0, 1), (1, 0), (1, 1)])
-        for s in range(2, 2 * PACK):
-            sire_sums([(s, 0), (s, 1)])
+        sire_sums([(0, 0), (0, 1), (1, 0), (1, 1)], 0)
+        for s in range(2, 2 * PACK - 1):
+            sire_sums([(s, 0), (s, 1)], 0)
 
         v2 = [gather("v2_%d" % a, tab2_w[a][:].bitcast(U32), calf_list[:], C, U32) for a in range(2)]
         wc = {}
@@ -263,31 +263,33 @@ def tile_list_sire_calf_merit_kernel(
         f0 = factors("raw00", 0)
         wc11_bf16 = held("stage11", [P, PACK * KP], BF16)[:]
         cast_shared(wc11_bf16, 1, 1)
+        sire_sums([(2 * PACK - 1, 0), (2 * PACK - 1, 1)], 1)
         pick(5, held("tab2_w0", [P, C], F32)[:])
         wc[0, 1] = quantise("wc01", wc01_bf16, KP)
         b1 = open_calf(1)
         pick(6, placed.tile([P, C], F32, name="pick6", offset=8192 + 4096, align_bytes=64)[:])
         wc[1, 1] = quantise("wc11", wc11_bf16, KP)
-        pick(7, placed.tile([P, C], F32, name="last_pick", offset=4096, align_bytes=64)[:])
+        pick(7, held("last_pick", [P, C], F32)[:])
         z0 = placed.tile([P, PACK * C], BF16, name="z0", offset=8192, align_bytes=64)[:]
         for c in range(0, C, P):
             multiply(nc.gpsimd, z0[:, PACK * c : PACK * (c + P)], 0, f0, slice(c, c + P))
-        wm0_bf16 = cast_wmerit(0, placed.tile([P, PACK * N], BF16, name="stage_wm0", offset=0, align_bytes=64)[:])
+        wm0_bf16 = cast_wmerit(0, placed.tile([P, PACK * N], BF16, name="stage_wm0", offset=0, align_bytes=64)[:], slice(0, N))
         close_calf(1, b1)
         f1 = factors("tab_w0", 1)
-        wm1_bf16 = cast_wmerit(1, held("stage_wm1", [P, PACK * N], BF16)[:])
-        wm = [quantise("wm0", wm0_bf16, N)]
+        stage_wm1 = held("stage_wm1", [P, 2, PACK * HALF], BF16)
+        wm1_bf16 = [cast_wmerit(1, stage_wm1[:, e, :], slice(HALF * e, HALF * (e + 1))) for e in range(2)]
+        wm0 = quantise("wm0", wm0_bf16, N)
         z0_codes, z0_scales = quantise("zq0", z0, C, "tab2_w0")
 
-        def merit_pass(acc, n, rb, z_codes, z_scales):
+        def merit_pass(acc, weights, n, z_codes, z_scales, start, stop):
             nc.tensor.matmul_mx(
-                out=acc[:],
-                lhsT=wm[rb][0][:, P * n : P * (n + 1)].bitcast(FP8X4),
-                lhsT_scale=wm[rb][1][:, P * n : P * (n + 1)],
+                out=acc,
+                lhsT=weights[0][:, P * n : P * (n + 1)].bitcast(FP8X4),
+                lhsT_scale=weights[1][:, P * n : P * (n + 1)],
                 rhs=z_codes.bitcast(FP8X4),
                 rhs_scale=z_scales,
-                start=(rb == 0),
-                stop=(rb == 1),
+                start=start,
+                stop=stop,
             )
 
         halves = [slice(HALF * u, HALF * (u + 1)) for u in range(2)]
@@ -295,20 +297,33 @@ def tile_list_sire_calf_merit_kernel(
         for u in range(2):
             for n in range(N // P):
                 merits[u, n] = bank(HALF, 1 - u)
-                merit_pass(merits[u, n], n, 0, z0_codes[:, halves[u]], z0_scales[:, halves[u]])
-        z1 = [held("z1_%d" % u, [P, PACK * HALF], BF16)[:] for u in range(2)]
-        for u in range(2):
-            multiply(nc.vector, z1[u], 1, f1, halves[u])
-        wm.append(quantise("wm1", wm1_bf16, N))
-        for u in range(2):
-            z1_codes, z1_scales = quantise("zq1_%d" % u, z1[u], HALF)
+                merit_pass(merits[u, n][:], wm0, n, z0_codes[:, halves[u]], z0_scales[:, halves[u]], True, False)
+
+        def store(u, n, engine):
+            res = held("res%d%d" % (u, n), [P, HALF], F32)
+            if engine == "vector":
+                nc.vector.tensor_copy(res[:], merits[u, n][:])
+            else:
+                nc.scalar.activation(res[:], merits[u, n][:], COPY)
+            nc.sync.dma_start(out[P * n : P * (n + 1), halves[u]], res[:])
+
+        def make_z1(name, calves):
+            z = held(name, [P, PACK * (calves.stop - calves.start)], BF16)[:]
+            multiply(nc.vector, z, 1, f1, calves)
+            return z
+
+        z1_first = make_z1("z1_first", halves[0])
+        wm1 = [quantise("wm1_0", wm1_bf16[0], HALF)]
+        z_codes, z_scales = quantise("zq1_first", z1_first, HALF)
+        wm1.append(quantise("wm1_1", wm1_bf16[1], HALF))
+        for n in range(N // P):
+            merit_pass(merits[0, n][:], wm1[n // 2], n % 2, z_codes, z_scales, False, True)
+        z1_last = [make_z1("z1_last%d" % q, slice(HALF + P * q, HALF + P * (q + 1))) for q in range(2)]
+        for n in range(N // P):
+            store(0, n, "scalar")
+        for q in range(2):
+            z_codes, z_scales = quantise("zq1_last%d" % q, z1_last[q], P)
             for n in range(N // P):
-                merit_pass(merits[u, n], n, 1, z1_codes, z1_scales)
-        for u in range(2):
-            for n in range(N // P):
-                res = held("res%d%d" % (u, n), [P, HALF], F32)
-                if n % 2 == 0 and u + n > 0:
-                    nc.vector.tensor_copy(res[:], merits[u, n][:])
-                else:
-                    nc.scalar.activation(res[:], merits[u, n][:], COPY)
-                nc.sync.dma_start(out[P * n : P * (n + 1), halves[u]], res[:])
+                merit_pass(merits[1, n][:, P * q : P * (q + 1)], wm1[n // 2], n % 2, z_codes, z_scales, False, q == 1)
+        for n in range(N // P):
+            store(1, n, ("scalar", "vector")[n % 2])

@@ -51,15 +51,14 @@ def tile_list_sire_calf_merit_kernel(
         ws_sc_raw = held("ws_sc_raw", [P, 2 * H], U8)
         tab2_sc = held("tab2_sc", [P, T2], U8)
         v_sc = [held("v_sc%d" % a, [P, S], U8) for a in range(2)]
-        v2_sc = held("v2_sc", [P, C], U8)
-        for scale_tile in (tab_sc, ws_sc_raw, tab2_sc, v_sc[0], v_sc[1], v2_sc):
+        v2_sc = [held("v2_sc%d" % a, [P, C], U8) for a in range(2)]
+        for scale_tile in (tab_sc, ws_sc_raw, tab2_sc, v_sc[0], v_sc[1], v2_sc[0], v2_sc[1]):
             nc.gpsimd.memset(scale_tile[:].bitcast(I32), 0)
 
         def words_of(table, a):
             return table[a].rearrange("p t i -> p (t i)").bitcast(I32)
 
-        def load_half(window, table, a, part):
-            cols = slice(T // 2 * part, T // 2 * (part + 1))
+        def load_part(window, table, a, cols):
             nc.sync.dma_start(window[:, cols], words_of(table, a)[:, cols])
 
         def load_scale_rows(window, scales):
@@ -76,7 +75,7 @@ def tile_list_sire_calf_merit_kernel(
             return gathered
 
         tab_w = [held("tab_w%d" % a, [P, T], I32) for a in range(2)]
-        load_half(tab_w[0], tab_words, 0, 0)
+        load_part(tab_w[0], tab_words, 0, slice(0, T // 2))
         nc.sync.dma_start(sire_list[:], offs)
         load_scale_rows(tab_sc, tab_scales)
         for q in range(4):
@@ -84,15 +83,15 @@ def tile_list_sire_calf_merit_kernel(
                 ws_sc_raw[32 * q : 32 * q + 4, :].bitcast(I32).rearrange("r (a c) -> r a c", a=2),
                 wsire_scales[:, 4 * q : 4 * q + 4, :].bitcast(I32).rearrange("a r c -> r a c"),
             )
-        load_half(tab_w[0], tab_words, 0, 1)
+        load_part(tab_w[0], tab_words, 0, slice(T // 2, T))
         sire_rows = gather("sire_rows", tab_sc[:], sire_list[:], S, U8)
         nc.sync.dma_start(calf_list[:], offs2)
         ws_raw = held("ws_raw", [P, 2, H // 2], I32)
         nc.sync.dma_start(ws_raw[:], wsire_words.bitcast(I32).rearrange("a p c -> p a c"))
         load_scale_rows(tab2_sc, tab2_scales)
-        load_half(tab_w[1], tab_words, 1, 0)
+        load_part(tab_w[1], tab_words, 1, slice(0, 3 * T // 8))
         deal_scale_rows(v_sc[0], 0, sire_rows, 0)
-        load_half(tab_w[1], tab_words, 1, 1)
+        load_part(tab_w[1], tab_words, 1, slice(3 * T // 8, T))
         deal_scale_rows(v_sc[1], 0, sire_rows, 1)
         tab2_w = [held("tab2_w%d" % a, [P, T2], I32) for a in range(2)]
         nc.sync.dma_start(tab2_w[0][:], words_of(tab2_words, 0))
@@ -117,21 +116,27 @@ def tile_list_sire_calf_merit_kernel(
             if (a, rb) == (0, 0):
                 raw = held("raw00", [P, PACK, KP], F32)
             else:
-                raw = placed.tile([P, PACK, KP], F32, name="raw%d%d" % (a, rb), offset={(1, 1): 0, (0, 1): 8192, (1, 0): 16384}[a, rb], align_bytes=64)
+                rows_held = PACK + 1 if (a, rb) == (1, 1) else PACK
+                raw = placed.tile([P, rows_held, KP], F32, name="raw%d%d" % (a, rb), offset={(1, 1): 0, (0, 1): 10240, (1, 0): 18432}[a, rb], align_bytes=64)
             rows = wcalf[KP * a : KP * (a + 1), KP * rb : KP * (rb + 1)]
-            nc.sync.dma_start(raw[:], rows.rearrange("(p j) c -> p j c", j=PACK))
-            return raw
+            nc.sync.dma_start(raw[:, 0:PACK, :], rows.rearrange("(p j) c -> p j c", j=PACK))
+            return raw[:, 0:PACK, :]
 
         wc_raw = {}
-        for a in range(2):
-            wc_raw[a, 0] = load_wcalf(a, 0)
-            deal_scale_rows(v2_sc, 4 * (a + 1), calf_rows, a)
-        nc.sync.dma_start(tab2_w[1][:], words_of(tab2_words, 1))
         gains = [held(("stage11", "stage_wm1")[rb], [P, PACK], F32) for rb in range(2)]
-        for rb in range(2):
+
+        def load_gains(rb):
             nc.sync.dma_start(gains[rb][:], gain[KP * rb : KP * (rb + 1)].rearrange("(p t) -> p t", t=PACK))
-        for a in range(2):
-            wc_raw[a, 1] = load_wcalf(a, 1)
+
+        wc_raw[0, 0] = load_wcalf(0, 0)
+        deal_scale_rows(v2_sc[0], 4, calf_rows, 0)
+        wc_raw[1, 0] = load_wcalf(1, 0)
+        load_gains(0)
+        nc.sync.dma_start(tab2_w[1][:], words_of(tab2_words, 1))
+        deal_scale_rows(v2_sc[1], 8, calf_rows, 1)
+        wc_raw[0, 1] = load_wcalf(0, 1)
+        load_gains(1)
+        wc_raw[1, 1] = load_wcalf(1, 1)
         wm_raw = [held("tab_w%d" % rb, [P, PACK, N], F32) for rb in range(2)]
         for rb in range(2):
             nc.sync.dma_start(wm_raw[rb][:], wmerit[KP * rb : KP * (rb + 1), :].rearrange("(p j) c -> p j c", j=PACK))
@@ -153,7 +158,7 @@ def tile_list_sire_calf_merit_kernel(
             )
 
         h = [
-            placed.tile([P, S], F32, name="h%d" % s, offset={4: 16384, 5: 20480, 7: 4096}[s], align_bytes=64) if s in (4, 5, 7) else held("h%d" % s, [P, S], F32)
+            placed.tile([P, S], F32, name="h%d" % s, offset={4: 18432, 5: 22528, 7: 4096}[s], align_bytes=64) if s in (4, 5, 7) else held("h%d" % s, [P, S], F32)
             for s in range(2 * PACK)
         ]
 
@@ -167,7 +172,7 @@ def tile_list_sire_calf_merit_kernel(
 
         def wcalf_views(grouped, a, rb, order):
             dst = grouped.rearrange("p (t m j) -> p " + order, t=PACK, j=PACK)
-            src = wc_raw[a, rb][:].rearrange("p j (m t) -> p " + order, t=PACK)
+            src = wc_raw[a, rb].rearrange("p j (m t) -> p " + order, t=PACK)
             return dst, src
 
         def cast_on_gpsimd(grouped, a, rb):
@@ -225,7 +230,7 @@ def tile_list_sire_calf_merit_kernel(
                 lhsT=codes[:, P * t : P * (t + 1)].bitcast(FP8X4),
                 lhsT_scale=scales[:, P * t : P * (t + 1)],
                 rhs=v2[a][:].bitcast(FP8X4),
-                rhs_scale=v2_sc[4 * (a + 1) : P, :],
+                rhs_scale=v2_sc[a][4 * (a + 1) : P, :],
                 start=(a == 0),
                 stop=(a == 1),
             )
@@ -267,10 +272,10 @@ def tile_list_sire_calf_merit_kernel(
         pick(5, held("tab2_w0", [P, C], F32)[:])
         wc[0, 1] = quantise("wc01", wc01_bf16, KP)
         b1 = open_calf(1)
-        pick(6, placed.tile([P, C], F32, name="pick6", offset=8192 + 4096, align_bytes=64)[:])
+        pick(6, placed.tile([P, C], F32, name="pick6", offset=8192, align_bytes=64)[:])
         wc[1, 1] = quantise("wc11", wc11_bf16, KP)
         pick(7, held("last_pick", [P, C], F32)[:])
-        z0 = placed.tile([P, PACK * C], BF16, name="z0", offset=8192, align_bytes=64)[:]
+        z0 = placed.tile([P, PACK * C], BF16, name="z0", offset=10240, align_bytes=64)[:]
         for c in range(0, C, P):
             multiply(nc.gpsimd, z0[:, PACK * c : PACK * (c + P)], 0, f0, slice(c, c + P))
         wm0_bf16 = cast_wmerit(0, placed.tile([P, PACK * N], BF16, name="stage_wm0", offset=0, align_bytes=64)[:], slice(0, N))

@@ -64,8 +64,8 @@ def tile_list_sire_calf_merit_kernel(
         def load_scale_rows(window, scales):
             nc.sync.dma_start(window[0:P:SPREAD, :].bitcast(I32), scales.bitcast(I32).rearrange("a q c -> (a q) c"))
 
-        def deal_scale_rows(plane, first, gathered, a):
-            for r in range(4):
+        def deal_scale_rows(plane, first, gathered, a, rows=range(4)):
+            for r in rows:
                 start = 64 * a + SPREAD * r
                 nc.sync.dma_start(plane[first + r : P : 32, :].bitcast(I32), gathered[start : 64 * (a + 1) : 16, :].bitcast(I32))
 
@@ -113,30 +113,36 @@ def tile_list_sire_calf_merit_kernel(
         calf_rows = gather("calf_rows", tab2_sc[:], calf_list[:], C, U8)
 
         def load_wcalf(a, rb):
-            if (a, rb) == (0, 0):
-                raw = held("raw00", [P, PACK, KP], F32)
-            else:
-                rows_held = PACK + 1 if (a, rb) == (1, 1) else PACK
-                raw = placed.tile([P, rows_held, KP], F32, name="raw%d%d" % (a, rb), offset={(1, 1): 0, (0, 1): 10240, (1, 0): 18432}[a, rb], align_bytes=64)
+            raw = placed.tile([P, PACK, KP], F32, name="raw10", offset=24576, align_bytes=64)
             rows = wcalf[KP * a : KP * (a + 1), KP * rb : KP * (rb + 1)]
-            nc.sync.dma_start(raw[:, 0:PACK, :], rows.rearrange("(p j) c -> p j c", j=PACK))
-            return raw[:, 0:PACK, :]
+            nc.sync.dma_start(raw[:], rows.rearrange("(p j) c -> p j c", j=PACK))
+            return raw[:]
+
+        def load_wcalf_half(raw, a, rb, e):
+            rows = wcalf[KP * a : KP * (a + 1), KP * rb + HALF * e : KP * rb + HALF * (e + 1)]
+            nc.sync.dma_start(raw, rows.rearrange("(p j) c -> p j c", j=PACK))
+            wc_raw[a, rb, e] = raw
 
         wc_raw = {}
-        gains = [held(("stage11", "stage_wm1")[rb], [P, PACK], F32) for rb in range(2)]
+        gains = [placed.tile([P, 32], F32, name="gain0", offset=16384 + 4096 - 64, align_bytes=64)[:, 0:PACK], held("stage_wm1", [P, PACK], F32)[:]]
 
         def load_gains(rb):
-            nc.sync.dma_start(gains[rb][:], gain[KP * rb : KP * (rb + 1)].rearrange("(p t) -> p t", t=PACK))
+            nc.sync.dma_start(gains[rb], gain[KP * rb : KP * (rb + 1)].rearrange("(p t) -> p t", t=PACK))
 
-        wc_raw[0, 0] = load_wcalf(0, 0)
-        deal_scale_rows(v2_sc[0], 4, calf_rows, 0)
+        for e in range(2):
+            load_wcalf_half(held("raw00_%d" % e, [P, PACK, HALF], F32)[:], 0, 0, e)
+        deal_scale_rows(v2_sc[0], 4, calf_rows, 0, range(0, 2))
         wc_raw[1, 0] = load_wcalf(1, 0)
+        deal_scale_rows(v2_sc[0], 4, calf_rows, 0, range(2, 4))
         load_gains(0)
         nc.sync.dma_start(tab2_w[1][:], words_of(tab2_words, 1))
-        deal_scale_rows(v2_sc[1], 8, calf_rows, 1)
-        wc_raw[0, 1] = load_wcalf(0, 1)
+        deal_scale_rows(v2_sc[1], 8, calf_rows, 1, range(0, 2))
+        load_wcalf_half(held("raw01_0", [P, PACK, HALF], F32)[:], 0, 1, 0)
+        deal_scale_rows(v2_sc[1], 8, calf_rows, 1, range(2, 4))
+        load_wcalf_half(placed.tile([P, PACK, HALF], F32, name="raw11_0", offset=4096, align_bytes=64)[:], 1, 1, 0)
+        load_wcalf_half(held("raw01_1", [P, PACK, HALF], F32)[:], 0, 1, 1)
         load_gains(1)
-        wc_raw[1, 1] = load_wcalf(1, 1)
+        load_wcalf_half(placed.tile([P, PACK + 2, HALF], F32, name="raw11_1", offset=8192, align_bytes=64)[:, 0:PACK, :], 1, 1, 1)
         wm_raw = [held("tab_w%d" % rb, [P, PACK, N], F32) for rb in range(2)]
         for rb in range(2):
             nc.sync.dma_start(wm_raw[rb][:], wmerit[KP * rb : KP * (rb + 1), :].rearrange("(p j) c -> p j c", j=PACK))
@@ -158,7 +164,7 @@ def tile_list_sire_calf_merit_kernel(
             )
 
         h = [
-            placed.tile([P, S], F32, name="h%d" % s, offset={4: 18432, 5: 22528, 7: 4096}[s], align_bytes=64) if s in (4, 5, 7) else held("h%d" % s, [P, S], F32)
+            placed.tile([P, S], F32, name="h%d" % s, offset={4: 24576, 5: 28672, 7: 16384}[s], align_bytes=64) if s in (4, 5, 7) else held("h%d" % s, [P, S], F32)
             for s in range(2 * PACK)
         ]
 
@@ -170,24 +176,27 @@ def tile_list_sire_calf_merit_kernel(
                 sire_pass(acc, s, u, 1)
                 nc.scalar.activation(h[s][:, BANK * u : BANK * (u + 1)], acc[:], COPY)
 
-        def wcalf_views(grouped, a, rb, order):
+        def wcalf_views(grouped, raw, order):
             dst = grouped.rearrange("p (t m j) -> p " + order, t=PACK, j=PACK)
-            src = wc_raw[a, rb].rearrange("p j (m t) -> p " + order, t=PACK)
+            src = raw.rearrange("p j (m t) -> p " + order, t=PACK)
             return dst, src
 
         def cast_on_gpsimd(grouped, a, rb):
-            dst, src = wcalf_views(grouped, a, rb, "m t j")
-            for m in range(0, P, 32):
-                nc.gpsimd.tensor_scalar(dst[:, m : m + 32], src[:, m : m + 32], 1.0, 0.0, MULT, ADD)
+            for e in range(2):
+                dst, src = wcalf_views(grouped, wc_raw[a, rb, e], "m t j")
+                for m in range(0, P // 2, 32):
+                    nc.gpsimd.tensor_scalar(dst[:, P // 2 * e + m : P // 2 * e + m + 32], src[:, m : m + 32], 1.0, 0.0, MULT, ADD)
 
         def cast_on_scalar(grouped, a, rb):
-            dst, src = wcalf_views(grouped, a, rb, "m j t")
+            dst, src = wcalf_views(grouped, wc_raw[a, rb], "m j t")
             nc.scalar.activation(dst, src, COPY)
 
-        def cast_shared(grouped, a, rb):
-            dst, src = wcalf_views(grouped, a, rb, "m j t")
-            nc.scalar.activation(dst[:, :, :, :2], src[:, :, :, :2], COPY)
-            nc.vector.tensor_copy(dst[:, :, :, 2:], src[:, :, :, 2:])
+        def cast_half(engine, grouped, e):
+            dst, src = wcalf_views(grouped, wc_raw[1, 1, e], "m j t")
+            if engine == "scalar":
+                nc.scalar.activation(dst[:, P // 2 * e : P // 2 * (e + 1)], src, COPY)
+            else:
+                nc.vector.tensor_copy(dst[:, P // 2 * e : P // 2 * (e + 1)], src)
 
         def cast_wmerit(rb, grouped, cols):
             nc.scalar.activation(
@@ -196,7 +205,7 @@ def tile_list_sire_calf_merit_kernel(
             return grouped
 
         def quantise(name, grouped, width, under=None):
-            codes = held(under or name + "_codes", [P, width], U32)
+            codes = under if under is not None else held(name + "_codes", [P, width], U32)
             scales = held(name + "_scales", [P, width], U8)
             nc.vector.quantize_mx(out=codes[:].bitcast(FP8X4), scales=scales[:], in_=grouped)
             return codes[:], scales[:]
@@ -246,8 +255,7 @@ def tile_list_sire_calf_merit_kernel(
                 calf_pass(sums[t], rb, t, 1)
                 nc.vector.tensor_tensor(x[rb][:, t, :], picked[PACK * rb + t], sums[t][:], ADD)
 
-        def factors(name, rb):
-            f = held(name, [P, PACK, C], F32)
+        def factors(f, rb):
             for t in range(PACK):
                 nc.scalar.activation(f[:, t, :], x[rb][:, t, :], COPY, bias=1.0, scale=gains[rb][:, t : t + 1])
             return f
@@ -264,27 +272,30 @@ def tile_list_sire_calf_merit_kernel(
         pick(4, held("tab2_w1", [P, C], F32)[:])
         wc01_bf16 = held("stage01", [P, PACK * KP], BF16)[:]
         cast_on_gpsimd(wc01_bf16, 0, 1)
-        close_calf(0, b0)
-        f0 = factors("raw00", 0)
         wc11_bf16 = held("stage11", [P, PACK * KP], BF16)[:]
-        cast_shared(wc11_bf16, 1, 1)
+        cast_half("scalar", wc11_bf16, 0)
+        close_calf(0, b0)
+        f0 = factors(placed.tile([P, PACK, C], F32, name="f0", offset=0, align_bytes=64), 0)
         sire_sums([(2 * PACK - 1, 0), (2 * PACK - 1, 1)], 1)
-        pick(5, held("tab2_w0", [P, C], F32)[:])
+        cast_half("vector", wc11_bf16, 1)
         wc[0, 1] = quantise("wc01", wc01_bf16, KP)
         b1 = open_calf(1)
-        pick(6, placed.tile([P, C], F32, name="pick6", offset=8192, align_bytes=64)[:])
         wc[1, 1] = quantise("wc11", wc11_bf16, KP)
-        pick(7, held("last_pick", [P, C], F32)[:])
-        z0 = placed.tile([P, PACK * C], BF16, name="z0", offset=10240, align_bytes=64)[:]
-        for c in range(0, C, P):
+        for s in range(5, 2 * PACK):
+            pick(s, placed.tile([P, C], F32, name="pick%d" % s, offset=8192 + 2048 * (s - 5), align_bytes=64)[:])
+        z0 = held("stage11", [P, PACK * 3 * P], BF16)[:]
+        for c in range(0, 3 * P, P):
             multiply(nc.gpsimd, z0[:, PACK * c : PACK * (c + P)], 0, f0, slice(c, c + P))
-        wm0_bf16 = cast_wmerit(0, placed.tile([P, PACK * N], BF16, name="stage_wm0", offset=0, align_bytes=64)[:], slice(0, N))
+        wm0_bf16 = cast_wmerit(0, placed.tile([P, PACK * N], BF16, name="stage_wm0", offset=16384 + 4096, align_bytes=64)[:], slice(0, N))
         close_calf(1, b1)
-        f1 = factors("tab_w0", 1)
+        f1 = factors(held("tab_w0", [P, PACK, C], F32), 1)
         stage_wm1 = held("stage_wm1", [P, 2, PACK * HALF], BF16)
         wm1_bf16 = [cast_wmerit(1, stage_wm1[:, e, :], slice(HALF * e, HALF * (e + 1))) for e in range(2)]
+        z0_last = placed.tile([P, PACK * P], BF16, name="z0_last", offset=8192 + 2048, align_bytes=64)[:]
+        multiply(nc.vector, z0_last, 0, f0, slice(3 * P, C))
         wm0 = quantise("wm0", wm0_bf16, N)
-        z0_codes, z0_scales = quantise("zq0", z0, C, "tab2_w0")
+        z0_first = quantise("zq0_first", z0[:, 0 : PACK * HALF], HALF, held("tab2_w1", [P, HALF], U32))
+        z0_quarters = [quantise("zq0_third", z0[:, PACK * HALF : PACK * 3 * P], P, placed.tile([P, P], U32, name="zq0_third_codes", offset=8192 + 4096, align_bytes=64)), quantise("zq0_last", z0_last, P)]
 
         def merit_pass(acc, weights, n, z_codes, z_scales, start, stop):
             nc.tensor.matmul_mx(
@@ -299,10 +310,14 @@ def tile_list_sire_calf_merit_kernel(
 
         halves = [slice(HALF * u, HALF * (u + 1)) for u in range(2)]
         merits = {}
-        for u in range(2):
+        for n in range(N // P):
+            merits[0, n] = bank(HALF, 1)
+            merit_pass(merits[0, n][:], wm0, n, z0_first[0], z0_first[1], True, False)
+        for n in range(N // P):
+            merits[1, n] = bank(HALF, 0)
+        for q in range(2):
             for n in range(N // P):
-                merits[u, n] = bank(HALF, 1 - u)
-                merit_pass(merits[u, n][:], wm0, n, z0_codes[:, halves[u]], z0_scales[:, halves[u]], True, False)
+                merit_pass(merits[1, n][:, P * q : P * (q + 1)], wm0, n, z0_quarters[q][0], z0_quarters[q][1], q == 0, False)
 
         def store(u, n, engine):
             res = held("res%d%d" % (u, n), [P, HALF], F32)

@@ -35,13 +35,13 @@ def tile_list_sire_calf_merit_kernel(
     with ExitStack() as ctx:
         keep = ctx.enter_context(tc.tile_pool(name="keep", bufs=1))
         placed = ctx.enter_context(tc.tile_pool(name="placed", bufs=1))
-        psum = ctx.enter_context(tc.psum_pool(name="psum", bufs=4))
+        psum = ctx.enter_context(tc.psum_pool(name="psum", bufs=1))
 
         def held(name, shape, dtype):
             return keep.tile(shape, dtype, name=name, align_bytes=64)
 
-        def bank(width, ring):
-            return psum.tile([P, width], F32, name="ring%d" % ring)
+        def bank(width, number):
+            return psum.tile([P, width], F32, name="bank%d" % number)
 
         sire_list = held("sire_list", [P, S // LIST_ROWS], U16)
         calf_list = held("calf_list", [P, C // LIST_ROWS], U16)
@@ -113,7 +113,7 @@ def tile_list_sire_calf_merit_kernel(
         calf_rows = gather("calf_rows", tab2_sc[:], calf_list[:], C, U8)
 
         def load_wcalf(a, rb):
-            raw = placed.tile([P, PACK, KP], F32, name="raw10", offset=24576, align_bytes=64)
+            raw = placed.tile([P, PACK, KP], F32, name="raw10", offset=8192, align_bytes=64)
             rows = wcalf[KP * a : KP * (a + 1), KP * rb : KP * (rb + 1)]
             nc.sync.dma_start(raw[:], rows.rearrange("(p j) c -> p j c", j=PACK))
             return raw[:]
@@ -124,7 +124,7 @@ def tile_list_sire_calf_merit_kernel(
             wc_raw[a, rb, e] = raw
 
         wc_raw = {}
-        gains = [placed.tile([P, 32], F32, name="gain0", offset=16384 + 4096 - 64, align_bytes=64)[:, 0:PACK], held("stage_wm1", [P, PACK], F32)[:]]
+        gains = [held(("stage_wm0", "stage_wm1")[rb], [P, PACK], F32)[:] for rb in range(2)]
 
         def load_gains(rb):
             nc.sync.dma_start(gains[rb], gain[KP * rb : KP * (rb + 1)].rearrange("(p t) -> p t", t=PACK))
@@ -139,10 +139,10 @@ def tile_list_sire_calf_merit_kernel(
         deal_scale_rows(v2_sc[1], 8, calf_rows, 1, range(0, 2))
         load_wcalf_half(held("raw01_0", [P, PACK, HALF], F32)[:], 0, 1, 0)
         deal_scale_rows(v2_sc[1], 8, calf_rows, 1, range(2, 4))
-        load_wcalf_half(placed.tile([P, PACK, HALF], F32, name="raw11_0", offset=4096, align_bytes=64)[:], 1, 1, 0)
+        load_wcalf_half(placed.tile([P, PACK, HALF], F32, name="raw11_0", offset=16384, align_bytes=64)[:], 1, 1, 0)
         load_wcalf_half(held("raw01_1", [P, PACK, HALF], F32)[:], 0, 1, 1)
         load_gains(1)
-        load_wcalf_half(placed.tile([P, PACK + 2, HALF], F32, name="raw11_1", offset=8192, align_bytes=64)[:, 0:PACK, :], 1, 1, 1)
+        load_wcalf_half(placed.tile([P, PACK, HALF], F32, name="raw11_1", offset=1536, align_bytes=64)[:], 1, 1, 1)
         wm_raw = [held("tab_w%d" % rb, [P, PACK, N], F32) for rb in range(2)]
         for rb in range(2):
             nc.sync.dma_start(wm_raw[rb][:], wmerit[KP * rb : KP * (rb + 1), :].rearrange("(p j) c -> p j c", j=PACK))
@@ -164,12 +164,12 @@ def tile_list_sire_calf_merit_kernel(
             )
 
         h = [
-            placed.tile([P, S], F32, name="h%d" % s, offset={4: 24576, 5: 28672, 7: 16384}[s], align_bytes=64) if s in (4, 5, 7) else held("h%d" % s, [P, S], F32)
+            placed.tile([P, S], F32, name="h%d" % s, offset=8192 + 4096 * (s - 4), align_bytes=64) if s in (4, 5) else held("h%d" % s, [P, S], F32)
             for s in range(2 * PACK)
         ]
 
-        def sire_sums(sums, ring):
-            banks = [bank(BANK, ring) for s, u in sums]
+        def sire_sums(sums, first):
+            banks = [bank(BANK, first + i) for i in range(len(sums))]
             for acc, (s, u) in zip(banks, sums):
                 sire_pass(acc, s, u, 0)
             for acc, (s, u) in zip(banks, sums):
@@ -196,7 +196,9 @@ def tile_list_sire_calf_merit_kernel(
             if engine == "scalar":
                 nc.scalar.activation(dst[:, P // 2 * e : P // 2 * (e + 1)], src, COPY)
             else:
-                nc.vector.tensor_copy(dst[:, P // 2 * e : P // 2 * (e + 1)], src)
+                dst = grouped.rearrange("p (u t m j) -> p u m j t", u=2, t=2, j=PACK)
+                src = wc_raw[1, 1, e].rearrange("p j (m u t) -> p u m j t", u=2, t=2)
+                nc.vector.tensor_copy(dst[:, :, P // 2 * e : P // 2 * (e + 1)], src)
 
         def cast_wmerit(rb, grouped, cols):
             nc.scalar.activation(
@@ -216,7 +218,7 @@ def tile_list_sire_calf_merit_kernel(
         cast_on_scalar(wc10_bf16, 1, 0)
         sire_sums([(0, 0), (0, 1), (1, 0), (1, 1)], 0)
         for s in range(2, 2 * PACK - 1):
-            sire_sums([(s, 0), (s, 1)], 0)
+            sire_sums([(s, 0), (s, 1)], 2 * (s % 2))
 
         v2 = [gather("v2_%d" % a, tab2_w[a][:].bitcast(U32), calf_list[:], C, U32) for a in range(2)]
         wc = {}
@@ -244,8 +246,8 @@ def tile_list_sire_calf_merit_kernel(
                 stop=(a == 1),
             )
 
-        def open_calf(rb):
-            sums = [bank(C, 1 - rb) for t in range(PACK)]
+        def open_calf(rb, numbers):
+            sums = [bank(C, number) for number in numbers]
             for t in range(PACK):
                 calf_pass(sums[t], rb, t, 0)
             return sums
@@ -267,7 +269,7 @@ def tile_list_sire_calf_merit_kernel(
                 x[rb][:, :, calves].rearrange(order, i=RUN), f[:, :, calves].rearrange(order, i=RUN), MULT,
             )
 
-        b0 = open_calf(0)
+        b0 = open_calf(0, (4, 5, 6, 7))
         wc[1, 0] = quantise("wc10", wc10_bf16, KP)
         pick(4, held("tab2_w1", [P, C], F32)[:])
         wc01_bf16 = held("stage01", [P, PACK * KP], BF16)[:]
@@ -275,27 +277,27 @@ def tile_list_sire_calf_merit_kernel(
         wc11_bf16 = held("stage11", [P, PACK * KP], BF16)[:]
         cast_half("scalar", wc11_bf16, 0)
         close_calf(0, b0)
-        f0 = factors(placed.tile([P, PACK, C], F32, name="f0", offset=0, align_bytes=64), 0)
-        sire_sums([(2 * PACK - 1, 0), (2 * PACK - 1, 1)], 1)
+        f0 = factors(placed.tile([P, PACK, C], F32, name="f0", offset=16384, align_bytes=64), 0)
+        sire_sums([(2 * PACK - 1, 0), (2 * PACK - 1, 1)], 6)
         cast_half("vector", wc11_bf16, 1)
         wc[0, 1] = quantise("wc01", wc01_bf16, KP)
-        b1 = open_calf(1)
+        b1 = open_calf(1, (0, 1, 2, 3))
+        z0_last = placed.tile([P, PACK * P], BF16, name="z0_last", offset=2048, align_bytes=64)[:]
+        multiply(nc.vector, z0_last, 0, f0, slice(3 * P, C))
         wc[1, 1] = quantise("wc11", wc11_bf16, KP)
         for s in range(5, 2 * PACK):
-            pick(s, placed.tile([P, C], F32, name="pick%d" % s, offset=8192 + 2048 * (s - 5), align_bytes=64)[:])
+            pick(s, placed.tile([P, C], F32, name="pick%d" % s, offset={5: 3072, 6: 5120, 7: 0}[s], align_bytes=64)[:])
         z0 = held("stage11", [P, PACK * 3 * P], BF16)[:]
         for c in range(0, 3 * P, P):
             multiply(nc.gpsimd, z0[:, PACK * c : PACK * (c + P)], 0, f0, slice(c, c + P))
-        wm0_bf16 = cast_wmerit(0, placed.tile([P, PACK * N], BF16, name="stage_wm0", offset=16384 + 4096, align_bytes=64)[:], slice(0, N))
+        wm0_bf16 = cast_wmerit(0, held("stage_wm0", [P, PACK * N], BF16)[:], slice(0, N))
         close_calf(1, b1)
         f1 = factors(held("tab_w0", [P, PACK, C], F32), 1)
         stage_wm1 = held("stage_wm1", [P, 2, PACK * HALF], BF16)
         wm1_bf16 = [cast_wmerit(1, stage_wm1[:, e, :], slice(HALF * e, HALF * (e + 1))) for e in range(2)]
-        z0_last = placed.tile([P, PACK * P], BF16, name="z0_last", offset=8192 + 2048, align_bytes=64)[:]
-        multiply(nc.vector, z0_last, 0, f0, slice(3 * P, C))
-        wm0 = quantise("wm0", wm0_bf16, N)
-        z0_first = quantise("zq0_first", z0[:, 0 : PACK * HALF], HALF, held("tab2_w1", [P, HALF], U32))
-        z0_quarters = [quantise("zq0_third", z0[:, PACK * HALF : PACK * 3 * P], P, placed.tile([P, P], U32, name="zq0_third_codes", offset=8192 + 4096, align_bytes=64)), quantise("zq0_last", z0_last, P)]
+        wm0 = quantise("wm0", wm0_bf16, N, placed.tile([P, N], U32, name="wm0_codes", offset=5120, align_bytes=64))
+        z0_first = quantise("zq0_first", z0[:, 0 : PACK * HALF], HALF, placed.tile([P, HALF], U32, name="zq0_first_codes", offset=0, align_bytes=64))
+        z0_quarters = [quantise("zq0_third", z0[:, PACK * HALF : PACK * 3 * P], P, placed.tile([P, P], U32, name="zq0_third_codes", offset=1024, align_bytes=64)), quantise("zq0_last", z0_last, P, placed.tile([P, P], U32, name="zq0_last_codes", offset=1536, align_bytes=64))]
 
         def merit_pass(acc, weights, n, z_codes, z_scales, start, stop):
             nc.tensor.matmul_mx(
@@ -311,10 +313,10 @@ def tile_list_sire_calf_merit_kernel(
         halves = [slice(HALF * u, HALF * (u + 1)) for u in range(2)]
         merits = {}
         for n in range(N // P):
-            merits[0, n] = bank(HALF, 1)
+            merits[0, n] = bank(HALF, PACK + n)
             merit_pass(merits[0, n][:], wm0, n, z0_first[0], z0_first[1], True, False)
         for n in range(N // P):
-            merits[1, n] = bank(HALF, 0)
+            merits[1, n] = bank(HALF, n)
         for q in range(2):
             for n in range(N // P):
                 merit_pass(merits[1, n][:, P * q : P * (q + 1)], wm0, n, z0_quarters[q][0], z0_quarters[q][1], q == 0, False)

@@ -196,9 +196,7 @@ def tile_list_sire_calf_merit_kernel(
             if engine == "scalar":
                 nc.scalar.activation(dst[:, P // 2 * e : P // 2 * (e + 1)], src, COPY)
             else:
-                dst = grouped.rearrange("p (u t m j) -> p u m j t", u=2, t=2, j=PACK)
-                src = wc_raw[1, 1, e].rearrange("p j (m u t) -> p u m j t", u=2, t=2)
-                nc.vector.tensor_copy(dst[:, :, P // 2 * e : P // 2 * (e + 1)], src)
+                nc.vector.tensor_copy(dst[:, P // 2 * e : P // 2 * (e + 1)], src)
 
         def cast_wmerit(rb, grouped, cols):
             nc.scalar.activation(
@@ -282,11 +280,9 @@ def tile_list_sire_calf_merit_kernel(
         cast_half("vector", wc11_bf16, 1)
         wc[0, 1] = quantise("wc01", wc01_bf16, KP)
         b1 = open_calf(1, (0, 1, 2, 3))
-        z0_last = placed.tile([P, PACK * P], BF16, name="z0_last", offset=2048, align_bytes=64)[:]
-        multiply(nc.vector, z0_last, 0, f0, slice(3 * P, C))
         wc[1, 1] = quantise("wc11", wc11_bf16, KP)
         for s in range(5, 2 * PACK):
-            pick(s, placed.tile([P, C], F32, name="pick%d" % s, offset={5: 3072, 6: 5120, 7: 0}[s], align_bytes=64)[:])
+            pick(s, placed.tile([P, C], F32, name="pick%d" % s, offset={5: 2048, 6: 4096, 7: 0}[s], align_bytes=64)[:])
         z0 = held("stage11", [P, PACK * 3 * P], BF16)[:]
         for c in range(0, 3 * P, P):
             multiply(nc.gpsimd, z0[:, PACK * c : PACK * (c + P)], 0, f0, slice(c, c + P))
@@ -295,9 +291,11 @@ def tile_list_sire_calf_merit_kernel(
         f1 = factors(held("tab_w0", [P, PACK, C], F32), 1)
         stage_wm1 = held("stage_wm1", [P, 2, PACK * HALF], BF16)
         wm1_bf16 = [cast_wmerit(1, stage_wm1[:, e, :], slice(HALF * e, HALF * (e + 1))) for e in range(2)]
-        wm0 = quantise("wm0", wm0_bf16, N, placed.tile([P, N], U32, name="wm0_codes", offset=5120, align_bytes=64))
-        z0_first = quantise("zq0_first", z0[:, 0 : PACK * HALF], HALF, placed.tile([P, HALF], U32, name="zq0_first_codes", offset=0, align_bytes=64))
-        z0_quarters = [quantise("zq0_third", z0[:, PACK * HALF : PACK * 3 * P], P, placed.tile([P, P], U32, name="zq0_third_codes", offset=1024, align_bytes=64)), quantise("zq0_last", z0_last, P, placed.tile([P, P], U32, name="zq0_last_codes", offset=1536, align_bytes=64))]
+        z0_last = placed.tile([P, PACK * P], BF16, name="z0_last", offset=4096, align_bytes=64)[:]
+        multiply(nc.vector, z0_last, 0, f0, slice(3 * P, C))
+        wm0 = quantise("wm0", wm0_bf16, N)
+        z0_first = quantise("zq0_first", z0[:, 0 : PACK * HALF], HALF, held("tab2_w1", [P, HALF], U32))
+        z0_quarters = [quantise("zq0_third", z0[:, PACK * HALF : PACK * 3 * P], P, placed.tile([P, P], U32, name="zq0_third_codes", offset=0, align_bytes=64)), quantise("zq0_last", z0_last, P)]
 
         def merit_pass(acc, weights, n, z_codes, z_scales, start, stop):
             nc.tensor.matmul_mx(

@@ -22,9 +22,11 @@ PACK = 4
 KP = P * PACK
 BANK = 512
 HALF = C // 2
+QUARTER = C // 4
 LIST_ROWS = 16
 SPREAD = 4
 RUN = 2
+PAIRS = P // RUN
 
 
 def tile_list_sire_calf_merit_kernel(
@@ -39,6 +41,9 @@ def tile_list_sire_calf_merit_kernel(
 
         def held(name, shape, dtype):
             return keep.tile(shape, dtype, name=name, align_bytes=64)
+
+        def at(offset, name, shape, dtype):
+            return placed.tile(shape, dtype, name=name, offset=offset, align_bytes=64)
 
         def bank(width, number):
             return psum.tile([P, width], F32, name="bank%d" % number)
@@ -64,18 +69,35 @@ def tile_list_sire_calf_merit_kernel(
         def load_scale_rows(window, scales):
             nc.sync.dma_start(window[0:P:SPREAD, :].bitcast(I32), scales.bitcast(I32).rearrange("a q c -> (a q) c"))
 
-        def deal_scale_rows(plane, first, gathered, a, rows=range(4)):
+        def deal_scale_rows(plane, first, gathered, a, rows):
             for r in rows:
                 start = 64 * a + SPREAD * r
                 nc.sync.dma_start(plane[first + r : P : 32, :].bitcast(I32), gathered[start : 64 * (a + 1) : 16, :].bitcast(I32))
 
-        def gather(name, window, offsets, count, dtype):
-            gathered = held(name, [P, count], dtype)
+        def gather(name, window, offsets, count, dtype, offset=None):
+            gathered = held(name, [P, count], dtype) if offset is None else at(offset, name, [P, count], dtype)
             nc.vector.tensor_copy(gathered[:], window.indirect(offsets))
             return gathered
 
+        ws = {}
+
+        def load_and_deal_wsire(rb, engine, groups):
+            raw = held("ws_raw%d" % rb, [P, 2, KP // RUN], I32)
+            pairs = wsire_words.bitcast(I32)[:, :, KP // RUN * rb : KP // RUN * (rb + 1)]
+            nc.sync.dma_start(raw[:], pairs.rearrange("a p c -> p a c"))
+            by_slice = raw[:].rearrange("p a (q t) -> p a t q", t=PACK)
+            for first, last in groups:
+                shape = [P, 2 * (last - first) * PAIRS]
+                dealt = at(24576, "ws4", shape, I32) if (rb, first) == (1, 0) else held("ws%d_%d" % (rb, first), shape, I32)
+                engine.tensor_copy(dealt[:].rearrange("p (a t q) -> p a t q", a=2, q=PAIRS), by_slice[:, :, first:last, :])
+                for t in range(first, last):
+                    for a in range(2):
+                        start = PAIRS * (a * (last - first) + t - first)
+                        ws[PACK * rb + t, a] = dealt[:, start : start + PAIRS]
+
+        lead = 3 * T // 8
         tab_w = [held("tab_w%d" % a, [P, T], I32) for a in range(2)]
-        load_part(tab_w[0], tab_words, 0, slice(0, T // 2))
+        load_part(tab_w[0], tab_words, 0, slice(0, lead))
         nc.sync.dma_start(sire_list[:], offs)
         load_scale_rows(tab_sc, tab_scales)
         for q in range(4):
@@ -83,69 +105,62 @@ def tile_list_sire_calf_merit_kernel(
                 ws_sc_raw[32 * q : 32 * q + 4, :].bitcast(I32).rearrange("r (a c) -> r a c", a=2),
                 wsire_scales[:, 4 * q : 4 * q + 4, :].bitcast(I32).rearrange("a r c -> r a c"),
             )
-        load_part(tab_w[0], tab_words, 0, slice(T // 2, T))
+        load_part(tab_w[0], tab_words, 0, slice(lead, T))
         sire_rows = gather("sire_rows", tab_sc[:], sire_list[:], S, U8)
+        ws_sc = held("ws_sc", [P, 2 * H], U8)
+        nc.vector.tensor_copy(
+            ws_sc[:].bitcast(U16).rearrange("p (b a t q) -> p b a t q", b=2, a=2, t=PACK),
+            ws_sc_raw[:].bitcast(U16).rearrange("p (a b q t) -> p b a t q", a=2, b=2, t=PACK),
+        )
+        v0 = gather("v0", tab_w[0][:].bitcast(U32), sire_list[:], S, U32)
         nc.sync.dma_start(calf_list[:], offs2)
-        ws_raw = held("ws_raw", [P, 2, H // 2], I32)
-        nc.sync.dma_start(ws_raw[:], wsire_words.bitcast(I32).rearrange("a p c -> p a c"))
+        load_and_deal_wsire(0, nc.vector, [(0, PACK)])
         load_scale_rows(tab2_sc, tab2_scales)
-        load_part(tab_w[1], tab_words, 1, slice(0, 3 * T // 8))
-        deal_scale_rows(v_sc[0], 0, sire_rows, 0)
-        load_part(tab_w[1], tab_words, 1, slice(3 * T // 8, T))
-        deal_scale_rows(v_sc[1], 0, sire_rows, 1)
+        calf_rows = gather("calf_rows", tab2_sc[:], calf_list[:], C, U8)
+        load_part(tab_w[1], tab_words, 1, slice(0, lead))
+        deal_scale_rows(v_sc[0], 0, sire_rows, 0, range(4))
+        load_part(tab_w[1], tab_words, 1, slice(lead, T))
+        deal_scale_rows(v_sc[1], 0, sire_rows, 1, range(4))
         tab2_w = [held("tab2_w%d" % a, [P, T2], I32) for a in range(2)]
         nc.sync.dma_start(tab2_w[0][:], words_of(tab2_words, 0))
+        load_and_deal_wsire(1, nc.gpsimd, [(0, 1), (1, PACK)])
         nc.sync.dma_start(pick_list[:], pos1)
 
-        v0 = gather("v0", tab_w[0][:].bitcast(U32), sire_list[:], S, U32)
-        ws = held("ws", [P, 2 * H], U16)
-        nc.vector.tensor_copy(
-            ws[:].rearrange("p (e t m) -> p e t m", t=PACK, m=P),
-            ws_raw[:].rearrange("p a c -> p (a c)").bitcast(U16).rearrange("p (e m t) -> p e t m", t=PACK, m=P),
-        )
-        ws_sc = [held("ws_sc%d" % rb, [P, H], U8) for rb in range(2)]
-        for rb in range(2):
-            nc.gpsimd.tensor_copy(
-                ws_sc[rb][:].rearrange("p (a t m) -> p a t m", t=PACK, m=P),
-                ws_sc_raw[:].rearrange("p (a b m t) -> p b a t m", a=2, t=PACK, m=P)[:, rb],
-            )
-
-        calf_rows = gather("calf_rows", tab2_sc[:], calf_list[:], C, U8)
-
-        def load_wcalf(a, rb):
-            raw = placed.tile([P, PACK, KP], F32, name="raw10", offset=8192, align_bytes=64)
-            rows = wcalf[KP * a : KP * (a + 1), KP * rb : KP * (rb + 1)]
-            nc.sync.dma_start(raw[:], rows.rearrange("(p j) c -> p j c", j=PACK))
-            return raw[:]
-
-        def load_wcalf_half(raw, a, rb, e):
-            rows = wcalf[KP * a : KP * (a + 1), KP * rb + HALF * e : KP * rb + HALF * (e + 1)]
-            nc.sync.dma_start(raw, rows.rearrange("(p j) c -> p j c", j=PACK))
-            wc_raw[a, rb, e] = raw
-
         wc_raw = {}
+
+        def load_wcalf(raw, a, rb, cols):
+            rows = wcalf[KP * a : KP * (a + 1), KP * rb + cols.start : KP * rb + cols.stop]
+            nc.sync.dma_start(raw[:], rows.rearrange("(p j) c -> p j c", j=PACK))
+            wc_raw[a, rb, cols.start] = raw
+
         gains = [held(("stage_wm0", "stage_wm1")[rb], [P, PACK], F32)[:] for rb in range(2)]
 
         def load_gains(rb):
-            nc.sync.dma_start(gains[rb], gain[KP * rb : KP * (rb + 1)].rearrange("(p t) -> p t", t=PACK))
+            with nc.allow_non_contiguous_dma(reason="512 gains dealt to their partitions and slices"):
+                dealt = gain[KP * rb : KP * (rb + 1)].rearrange("(q t i) -> i q t", t=PACK, i=RUN)
+                for i in range(RUN):
+                    nc.sync.dma_start(gains[rb][i:P:RUN, :], dealt[i])
 
+        halves = [slice(HALF * e, HALF * (e + 1)) for e in range(2)]
         for e in range(2):
-            load_wcalf_half(held("raw00_%d" % e, [P, PACK, HALF], F32)[:], 0, 0, e)
+            load_wcalf(held("raw00_%d" % e, [P, PACK, HALF], F32), 0, 0, halves[e])
         deal_scale_rows(v2_sc[0], 4, calf_rows, 0, range(0, 2))
-        wc_raw[1, 0] = load_wcalf(1, 0)
+        load_wcalf(at(8192, "raw10", [P, PACK, KP], F32), 1, 0, slice(0, KP))
         deal_scale_rows(v2_sc[0], 4, calf_rows, 0, range(2, 4))
         load_gains(0)
         nc.sync.dma_start(tab2_w[1][:], words_of(tab2_words, 1))
         deal_scale_rows(v2_sc[1], 8, calf_rows, 1, range(0, 2))
-        load_wcalf_half(held("raw01_0", [P, PACK, HALF], F32)[:], 0, 1, 0)
+        load_wcalf(held("raw01_0", [P, PACK, HALF], F32), 0, 1, halves[0])
         deal_scale_rows(v2_sc[1], 8, calf_rows, 1, range(2, 4))
-        load_wcalf_half(placed.tile([P, PACK, HALF], F32, name="raw11_0", offset=16384, align_bytes=64)[:], 1, 1, 0)
-        load_wcalf_half(held("raw01_1", [P, PACK, HALF], F32)[:], 0, 1, 1)
+        load_wcalf(at(16384, "raw11_0", [P, PACK, HALF], F32), 1, 1, halves[0])
+        load_wcalf(held("raw01_1", [P, PACK, HALF], F32), 0, 1, halves[1])
         load_gains(1)
-        load_wcalf_half(placed.tile([P, PACK, HALF], F32, name="raw11_1", offset=1536, align_bytes=64)[:], 1, 1, 1)
+        load_wcalf(at(1536, "raw11_1", [P, PACK, HALF], F32), 1, 1, halves[1])
         wm_raw = [held("tab_w%d" % rb, [P, PACK, N], F32) for rb in range(2)]
         for rb in range(2):
-            nc.sync.dma_start(wm_raw[rb][:], wmerit[KP * rb : KP * (rb + 1), :].rearrange("(p j) c -> p j c", j=PACK))
+            rows = wmerit[KP * rb : KP * (rb + 1), :].rearrange("(q t i) c -> i q t c", t=PACK, i=RUN)
+            for i in range(RUN):
+                nc.sync.dma_start(wm_raw[rb][i:P:RUN, :, :], rows[i])
 
         part = BANK // LIST_ROWS
         v1 = [gather("v1_%d" % u, tab_w[1][:].bitcast(U32), sire_list[:, part * u : part * (u + 1)], BANK, U32) for u in range(2)]
@@ -153,10 +168,11 @@ def tile_list_sire_calf_merit_kernel(
         def sire_pass(acc, s, u, a):
             rb, t = divmod(s, PACK)
             moving = v0[:, BANK * u : BANK * (u + 1)] if a == 0 else v1[u][:]
+            group = PACK * a + t
             nc.tensor.matmul_mx(
                 out=acc[:],
-                lhsT=ws[:, H * a + P * s : H * a + P * (s + 1)].bitcast(U8).bitcast(FP4X4),
-                lhsT_scale=ws_sc[rb][:, KP * a + P * t : KP * a + P * (t + 1)],
+                lhsT=ws[s, a].bitcast(U8).bitcast(FP4X4),
+                lhsT_scale=ws_sc[:, H * rb + P * group : H * rb + P * (group + 1)],
                 rhs=moving.bitcast(FP8X4),
                 rhs_scale=v_sc[a][:, BANK * u : BANK * (u + 1)],
                 start=(a == 0),
@@ -164,7 +180,7 @@ def tile_list_sire_calf_merit_kernel(
             )
 
         h = [
-            placed.tile([P, S], F32, name="h%d" % s, offset=8192 + 4096 * (s - 4), align_bytes=64) if s in (4, 5) else held("h%d" % s, [P, S], F32)
+            at(8192, "h%d" % s, [P, S], F32) if s == 5 else held("h%d" % s, [P, S], F32)
             for s in range(2 * PACK)
         ]
 
@@ -176,174 +192,169 @@ def tile_list_sire_calf_merit_kernel(
                 sire_pass(acc, s, u, 1)
                 nc.scalar.activation(h[s][:, BANK * u : BANK * (u + 1)], acc[:], COPY)
 
-        def wcalf_views(grouped, raw, order):
-            dst = grouped.rearrange("p (t m j) -> p " + order, t=PACK, j=PACK)
-            src = raw.rearrange("p j (m t) -> p " + order, t=PACK)
-            return dst, src
+        def cast_views(grouped, a, rb, first, order):
+            raw = wc_raw[a, rb, first]
+            src = raw[:].rearrange("p j (q t i) -> p " + order, t=PACK, i=RUN)
+            dst = grouped.rearrange("p (t q i j) -> p " + order, t=PACK, i=RUN, j=PACK)
+            q0 = first // (PACK * RUN)
+            return dst[:, q0 : q0 + src.shape[1]], src
 
         def cast_on_gpsimd(grouped, a, rb):
             for e in range(2):
-                dst, src = wcalf_views(grouped, wc_raw[a, rb, e], "m t j")
-                for m in range(0, P // 2, 32):
-                    nc.gpsimd.tensor_scalar(dst[:, P // 2 * e + m : P // 2 * e + m + 32], src[:, m : m + 32], 1.0, 0.0, MULT, ADD)
-
-        def cast_on_scalar(grouped, a, rb):
-            dst, src = wcalf_views(grouped, wc_raw[a, rb], "m j t")
-            nc.scalar.activation(dst, src, COPY)
-
-        def cast_half(engine, grouped, e):
-            dst, src = wcalf_views(grouped, wc_raw[1, 1, e], "m j t")
-            if engine == "scalar":
-                nc.scalar.activation(dst[:, P // 2 * e : P // 2 * (e + 1)], src, COPY)
-            else:
-                nc.vector.tensor_copy(dst[:, P // 2 * e : P // 2 * (e + 1)], src)
+                dst, src = cast_views(grouped, a, rb, HALF * e, "q t i j")
+                for q in range(0, PAIRS // 2, 16):
+                    nc.gpsimd.tensor_scalar(dst[:, q : q + 16], src[:, q : q + 16], 1.0, 0.0, MULT, ADD)
 
         def cast_wmerit(rb, grouped, cols):
             nc.scalar.activation(
-                grouped.rearrange("p (c i j) -> p c j i", i=RUN, j=PACK),
-                wm_raw[rb][:, :, cols].rearrange("p j (c i) -> p c j i", i=RUN), COPY)
+                grouped.rearrange("p (c i j) -> p c j i", i=2, j=PACK),
+                wm_raw[rb][:, :, cols].rearrange("p j (c i) -> p c j i", i=2), COPY)
             return grouped
 
-        def quantise(name, grouped, width, under=None):
-            codes = under if under is not None else held(name + "_codes", [P, width], U32)
-            scales = held(name + "_scales", [P, width], U8)
+        def quantise(name, grouped, width, offset=None):
+            codes = held(name + "_codes", [P, width], U32)
+            scales = held(name + "_scales", [P, width], U8) if offset is None else at(offset, name + "_scales", [P, width], U8)
             nc.vector.quantize_mx(out=codes[:].bitcast(FP8X4), scales=scales[:], in_=grouped)
             return codes[:], scales[:]
 
-        wc00_bf16 = held("stage00", [P, PACK * KP], BF16)[:]
+        wc00_bf16 = at(28672, "stage00", [P, PACK * KP], BF16)[:]
         cast_on_gpsimd(wc00_bf16, 0, 0)
-        wc10_bf16 = held("stage10", [P, PACK * KP], BF16)[:]
-        cast_on_scalar(wc10_bf16, 1, 0)
         sire_sums([(0, 0), (0, 1), (1, 0), (1, 1)], 0)
-        for s in range(2, 2 * PACK - 1):
+        for s in range(2, PACK + 1):
             sire_sums([(s, 0), (s, 1)], 2 * (s % 2))
+        wc10_bf16 = at(24576, "stage10", [P, PACK * KP], BF16)[:]
+        nc.scalar.copy(*cast_views(wc10_bf16, 1, 0, 0, "q t j i"))
+        sire_sums([(5, 0), (5, 1)], 2)
 
-        v2 = [gather("v2_%d" % a, tab2_w[a][:].bitcast(U32), calf_list[:], C, U32) for a in range(2)]
+        v2 = [gather("v2_0", tab2_w[0][:].bitcast(U32), calf_list[:], C, U32)]
         wc = {}
         wc[0, 0] = quantise("wc00", wc00_bf16, KP)
-        x = [held("x%d" % rb, [P, PACK, C], F32) for rb in range(2)]
         picked = {}
 
-        def pick(s, dst):
-            nc.vector.tensor_copy(dst, h[s][:].indirect(pick_list[:]))
-            picked[s] = dst
+        def pick(s, dst, calves=slice(0, C)):
+            offsets = pick_list[:, calves.start // LIST_ROWS : calves.stop // LIST_ROWS]
+            nc.vector.tensor_copy(dst, h[s][:].indirect(offsets))
+            picked.setdefault(s, []).append((calves, dst))
 
+        x0 = held("x0", [P, PACK, C], F32)
         pick(0, held("tab2_w0", [P, C], F32)[:])
         for s in range(1, PACK):
-            pick(s, x[0][:, s, :])
+            pick(s, x0[:, s, :])
+        pick(4, held("pick4", [P, C], F32)[:])
 
-        def calf_pass(acc, rb, t, a):
+        def calf_passes(sums, rb, a):
             codes, scales = wc[a, rb]
-            nc.tensor.matmul_mx(
-                out=acc[:],
-                lhsT=codes[:, P * t : P * (t + 1)].bitcast(FP8X4),
-                lhsT_scale=scales[:, P * t : P * (t + 1)],
-                rhs=v2[a][:].bitcast(FP8X4),
-                rhs_scale=v2_sc[a][4 * (a + 1) : P, :],
-                start=(a == 0),
-                stop=(a == 1),
-            )
-
-        def open_calf(rb, numbers):
-            sums = [bank(C, number) for number in numbers]
             for t in range(PACK):
-                calf_pass(sums[t], rb, t, 0)
-            return sums
+                nc.tensor.matmul_mx(
+                    out=sums[t][:],
+                    lhsT=codes[:, P * t : P * (t + 1)].bitcast(FP8X4),
+                    lhsT_scale=scales[:, P * t : P * (t + 1)],
+                    rhs=v2[a][:].bitcast(FP8X4),
+                    rhs_scale=v2_sc[a][4 * (a + 1) : P, :],
+                    start=(a == 0),
+                    stop=(a == 1),
+                )
 
-        def close_calf(rb, sums):
+        def adds(x, rb, sums):
             for t in range(PACK):
-                calf_pass(sums[t], rb, t, 1)
-                nc.vector.tensor_tensor(x[rb][:, t, :], picked[PACK * rb + t], sums[t][:], ADD)
+                for calves, values in picked[PACK * rb + t]:
+                    nc.vector.tensor_tensor(x[:, t, calves], values, sums[t][:, calves], ADD)
 
-        def factors(f, rb):
+        def factors(f, x, rb):
             for t in range(PACK):
-                nc.scalar.activation(f[:, t, :], x[rb][:, t, :], COPY, bias=1.0, scale=gains[rb][:, t : t + 1])
-            return f
+                nc.scalar.activation(f[:, t, :], x[:, t, :], COPY, bias=1.0, scale=gains[rb][:, t : t + 1])
 
-        def multiply(engine, z, rb, f, calves):
+        def multiply(engine, z, x, f, calves):
             order = "p t (c i) -> p c t i"
             engine.tensor_tensor(
-                z.rearrange("p (c i t) -> p c t i", i=RUN, t=PACK),
-                x[rb][:, :, calves].rearrange(order, i=RUN), f[:, :, calves].rearrange(order, i=RUN), MULT,
+                z.rearrange("p (c i t) -> p c t i", i=2, t=PACK),
+                x[:, :, calves].rearrange(order, i=2), f[:, :, calves].rearrange(order, i=2), MULT,
             )
 
-        b0 = open_calf(0, (4, 5, 6, 7))
-        wc[1, 0] = quantise("wc10", wc10_bf16, KP)
-        pick(4, held("tab2_w1", [P, C], F32)[:])
+        b0 = [bank(C, number) for number in (4, 5, 6, 7)]
+        calf_passes(b0, 0, 0)
+        wc[1, 0] = quantise("wc10", wc10_bf16, KP, 28672)
+        v2.append(gather("v2_1", tab2_w[1][:].bitcast(U32), calf_list[:], C, U32, 30720))
+        pick(5, held("tab2_w1", [P, HALF], F32)[:], halves[0])
         wc01_bf16 = held("stage01", [P, PACK * KP], BF16)[:]
         cast_on_gpsimd(wc01_bf16, 0, 1)
         wc11_bf16 = held("stage11", [P, PACK * KP], BF16)[:]
-        cast_half("scalar", wc11_bf16, 0)
-        close_calf(0, b0)
-        f0 = factors(placed.tile([P, PACK, C], F32, name="f0", offset=16384, align_bytes=64), 0)
-        sire_sums([(2 * PACK - 1, 0), (2 * PACK - 1, 1)], 6)
-        cast_half("vector", wc11_bf16, 1)
+        nc.scalar.copy(*cast_views(wc11_bf16, 1, 1, 0, "q t j i"))
+        calf_passes(b0, 0, 1)
+        adds(x0, 0, b0)
+        f0 = at(16384, "f0", [P, PACK, C], F32)
+        factors(f0, x0, 0)
+        for s in range(2 * PACK - 2, 2 * PACK):
+            sire_sums([(s, 0), (s, 1)], 2 * s - 8)
+        nc.vector.tensor_copy(*cast_views(wc11_bf16, 1, 1, HALF, "q t j i"))
         wc[0, 1] = quantise("wc01", wc01_bf16, KP)
-        b1 = open_calf(1, (0, 1, 2, 3))
+        b1 = [bank(C, number) for number in (0, 1, 2, 3)]
+        calf_passes(b1, 1, 0)
         wc[1, 1] = quantise("wc11", wc11_bf16, KP)
-        for s in range(5, 2 * PACK):
-            pick(s, placed.tile([P, C], F32, name="pick%d" % s, offset={5: 2048, 6: 4096, 7: 0}[s], align_bytes=64)[:])
-        z0 = held("stage11", [P, PACK * 3 * P], BF16)[:]
-        for c in range(0, 3 * P, P):
-            multiply(nc.gpsimd, z0[:, PACK * c : PACK * (c + P)], 0, f0, slice(c, c + P))
+        pick(5, at(2048, "pick5", [P, HALF], F32)[:], halves[1])
+        for s in range(6, 2 * PACK):
+            pick(s, at({6: 4096, 7: 0}[s], "pick%d" % s, [P, C], F32)[:])
+        z0 = held("stage11", [P, PACK * 3 * QUARTER], BF16)[:]
+        for c in range(0, 3 * QUARTER, QUARTER):
+            multiply(nc.gpsimd, z0[:, PACK * c : PACK * (c + QUARTER)], x0, f0, slice(c, c + QUARTER))
         wm0_bf16 = cast_wmerit(0, held("stage_wm0", [P, PACK * N], BF16)[:], slice(0, N))
-        close_calf(1, b1)
-        f1 = factors(held("tab_w0", [P, PACK, C], F32), 1)
+        calf_passes(b1, 1, 1)
+
+        x1 = held("x1", [P, PACK, C], F32)
+        adds(x1, 1, b1)
+        f1 = held("tab_w0", [P, PACK, C], F32)
+        factors(f1, x1, 1)
         stage_wm1 = held("stage_wm1", [P, 2, PACK * HALF], BF16)
-        wm1_bf16 = [cast_wmerit(1, stage_wm1[:, e, :], slice(HALF * e, HALF * (e + 1))) for e in range(2)]
-        z0_last = placed.tile([P, PACK * P], BF16, name="z0_last", offset=4096, align_bytes=64)[:]
-        multiply(nc.vector, z0_last, 0, f0, slice(3 * P, C))
-        wm0 = quantise("wm0", wm0_bf16, N)
-        z0_first = quantise("zq0_first", z0[:, 0 : PACK * HALF], HALF, held("tab2_w1", [P, HALF], U32))
-        z0_quarters = [quantise("zq0_third", z0[:, PACK * HALF : PACK * 3 * P], P, placed.tile([P, P], U32, name="zq0_third_codes", offset=0, align_bytes=64)), quantise("zq0_last", z0_last, P)]
+        wm1_bf16 = [cast_wmerit(1, stage_wm1[:, e, :], halves[e]) for e in range(2)]
 
-        def merit_pass(acc, weights, n, z_codes, z_scales, start, stop):
-            nc.tensor.matmul_mx(
-                out=acc,
-                lhsT=weights[0][:, P * n : P * (n + 1)].bitcast(FP8X4),
-                lhsT_scale=weights[1][:, P * n : P * (n + 1)],
-                rhs=z_codes.bitcast(FP8X4),
-                rhs_scale=z_scales,
-                start=start,
-                stop=stop,
-            )
+        def make_z1(name, calves):
+            z = held(name, [P, PACK * (calves.stop - calves.start)], BF16)[:]
+            multiply(nc.vector, z, x1, f1, calves)
+            return z
 
-        halves = [slice(HALF * u, HALF * (u + 1)) for u in range(2)]
-        merits = {}
-        for n in range(N // P):
-            merits[0, n] = bank(HALF, PACK + n)
-            merit_pass(merits[0, n][:], wm0, n, z0_first[0], z0_first[1], True, False)
-        for n in range(N // P):
-            merits[1, n] = bank(HALF, n)
-        for q in range(2):
+        def merit_passes(accs, weights, zq, start, stop):
             for n in range(N // P):
-                merit_pass(merits[1, n][:, P * q : P * (q + 1)], wm0, n, z0_quarters[q][0], z0_quarters[q][1], q == 0, False)
+                codes, scales = weights[n]
+                nc.tensor.matmul_mx(
+                    out=accs[n],
+                    lhsT=codes.bitcast(FP8X4),
+                    lhsT_scale=scales,
+                    rhs=zq[0].bitcast(FP8X4),
+                    rhs_scale=zq[1],
+                    start=start,
+                    stop=stop,
+                )
+
+        def columns(quantised, count):
+            return [tuple(plane[:, P * n : P * (n + 1)] for plane in quantised) for n in range(count)]
+
+        merits = [[bank(HALF, first + n) for n in range(N // P)] for first in (PACK, 0)]
 
         def store(u, n, engine):
             res = held("res%d%d" % (u, n), [P, HALF], F32)
             if engine == "vector":
-                nc.vector.tensor_copy(res[:], merits[u, n][:])
+                nc.vector.tensor_copy(res[:], merits[u][n][:])
             else:
-                nc.scalar.activation(res[:], merits[u, n][:], COPY)
+                nc.scalar.activation(res[:], merits[u][n][:], COPY)
             nc.sync.dma_start(out[P * n : P * (n + 1), halves[u]], res[:])
 
-        def make_z1(name, calves):
-            z = held(name, [P, PACK * (calves.stop - calves.start)], BF16)[:]
-            multiply(nc.vector, z, 1, f1, calves)
-            return z
-
+        z0_last = at(5120, "z0_last", [P, PACK * QUARTER], BF16)[:]
+        multiply(nc.vector, z0_last, x0, f0, slice(3 * QUARTER, C))
+        wm0 = columns(quantise("wm0", wm0_bf16, N, 4096), 4)
+        merit_passes([acc[:] for acc in merits[0]], wm0, quantise("zq0_first", z0[:, 0 : PACK * HALF], HALF, 4608), True, False)
+        z0_third = quantise("zq0_third", z0[:, PACK * HALF : PACK * 3 * QUARTER], QUARTER, 4864)
+        for e, zq in enumerate((z0_third, quantise("zq0_last", z0_last, QUARTER))):
+            merit_passes([acc[:, P * e : P * (e + 1)] for acc in merits[1]], wm0, zq, e == 0, False)
         z1_first = make_z1("z1_first", halves[0])
-        wm1 = [quantise("wm1_0", wm1_bf16[0], HALF)]
-        z_codes, z_scales = quantise("zq1_first", z1_first, HALF)
-        wm1.append(quantise("wm1_1", wm1_bf16[1], HALF))
-        for n in range(N // P):
-            merit_pass(merits[0, n][:], wm1[n // 2], n % 2, z_codes, z_scales, False, True)
-        z1_last = [make_z1("z1_last%d" % q, slice(HALF + P * q, HALF + P * (q + 1))) for q in range(2)]
+        wm1 = columns(quantise("wm1_0", wm1_bf16[0], HALF), 2)
+        zq1_first = quantise("zq1_first", z1_first, HALF)
+        wm1.extend(columns(quantise("wm1_1", wm1_bf16[1], HALF), 2))
+        merit_passes([acc[:] for acc in merits[0]], wm1, zq1_first, False, True)
+        z1_last = [make_z1("z1_last%d" % e, slice(HALF + QUARTER * e, HALF + QUARTER * (e + 1))) for e in range(2)]
         for n in range(N // P):
             store(0, n, "scalar")
-        for q in range(2):
-            z_codes, z_scales = quantise("zq1_last%d" % q, z1_last[q], P)
-            for n in range(N // P):
-                merit_pass(merits[1, n][:, P * q : P * (q + 1)], wm1[n // 2], n % 2, z_codes, z_scales, False, q == 1)
+        for e in range(2):
+            zq = quantise("zq1_last%d" % e, z1_last[e], QUARTER)
+            merit_passes([acc[:, P * e : P * (e + 1)] for acc in merits[1]], wm1, zq, False, e == 1)
         for n in range(N // P):
             store(1, n, ("scalar", "vector")[n % 2])

@@ -133,7 +133,7 @@ def tile_list_sire_calf_merit_kernel(
             nc.sync.dma_start(raw[:], rows.rearrange("(p j) c -> p j c", j=PACK))
             wc_raw[a, rb, cols.start] = raw
 
-        gains = [held(("stage_wm0", "stage_wm1")[rb], [P, PACK], F32)[:] for rb in range(2)]
+        gains = [at(32768, "gains0", [P, PACK], F32)[:], held("stage_wm1", [P, PACK], F32)[:]]
 
         def load_gains(rb):
             with nc.allow_non_contiguous_dma(reason="512 gains dealt to their partitions and slices"):
@@ -147,20 +147,20 @@ def tile_list_sire_calf_merit_kernel(
         deal_scale_rows(v2_sc[0], 4, calf_rows, 0, range(0, 2))
         load_wcalf(at(8192, "raw10", [P, PACK, KP], F32), 1, 0, slice(0, KP))
         deal_scale_rows(v2_sc[0], 4, calf_rows, 0, range(2, 4))
-        load_gains(0)
         nc.sync.dma_start(tab2_w[1][:], words_of(tab2_words, 1))
         deal_scale_rows(v2_sc[1], 8, calf_rows, 1, range(0, 2))
         load_wcalf(held("raw01_0", [P, PACK, HALF], F32), 0, 1, halves[0])
         deal_scale_rows(v2_sc[1], 8, calf_rows, 1, range(2, 4))
-        load_wcalf(at(16384, "raw11_0", [P, PACK, HALF], F32), 1, 1, halves[0])
+        load_wcalf(held("raw11_0", [P, PACK, HALF], F32), 1, 1, halves[0])
         load_wcalf(held("raw01_1", [P, PACK, HALF], F32), 0, 1, halves[1])
-        load_gains(1)
-        load_wcalf(at(1536, "raw11_1", [P, PACK, HALF], F32), 1, 1, halves[1])
+        load_wcalf(at(16384, "raw11_1", [P, PACK, HALF], F32), 1, 1, halves[1])
+        load_gains(0)
         wm_raw = [held("tab_w%d" % rb, [P, PACK, N], F32) for rb in range(2)]
         for rb in range(2):
             rows = wmerit[KP * rb : KP * (rb + 1), :].rearrange("(q t i) c -> i q t c", t=PACK, i=RUN)
             for i in range(RUN):
                 nc.sync.dma_start(wm_raw[rb][i:P:RUN, :, :], rows[i])
+        load_gains(1)
 
         part = BANK // LIST_ROWS
         v1 = [gather("v1_%d" % u, tab_w[1][:].bitcast(U32), sire_list[:, part * u : part * (u + 1)], BANK, U32) for u in range(2)]
@@ -180,7 +180,7 @@ def tile_list_sire_calf_merit_kernel(
             )
 
         h = [
-            at(8192, "h%d" % s, [P, S], F32) if s == 5 else held("h%d" % s, [P, S], F32)
+            at({5: 8192, 6: 12288, 7: 32768}[s], "h%d" % s, [P, S], F32) if s > PACK else held("h%d" % s, [P, S], F32)
             for s in range(2 * PACK)
         ]
 
@@ -224,7 +224,8 @@ def tile_list_sire_calf_merit_kernel(
             sire_sums([(s, 0), (s, 1)], 2 * (s % 2))
         wc10_bf16 = at(24576, "stage10", [P, PACK * KP], BF16)[:]
         nc.scalar.copy(*cast_views(wc10_bf16, 1, 0, 0, "q t j i"))
-        sire_sums([(5, 0), (5, 1)], 2)
+        for s in range(PACK + 1, 2 * PACK - 1):
+            sire_sums([(s, 0), (s, 1)], 2 * (s % 2))
 
         v2 = [gather("v2_0", tab2_w[0][:].bitcast(U32), calf_list[:], C, U32)]
         wc = {}
@@ -264,41 +265,42 @@ def tile_list_sire_calf_merit_kernel(
             for t in range(PACK):
                 nc.scalar.activation(f[:, t, :], x[:, t, :], COPY, bias=1.0, scale=gains[rb][:, t : t + 1])
 
-        def multiply(engine, z, x, f, calves):
+        def multiply(engine, z, x, f):
             order = "p t (c i) -> p c t i"
-            engine.tensor_tensor(
-                z.rearrange("p (c i t) -> p c t i", i=2, t=PACK),
-                x[:, :, calves].rearrange(order, i=2), f[:, :, calves].rearrange(order, i=2), MULT,
-            )
+            engine.tensor_tensor(z.rearrange("p (c i t) -> p c t i", i=2, t=PACK), x.rearrange(order, i=2), f.rearrange(order, i=2), MULT)
 
         b0 = [bank(C, number) for number in (4, 5, 6, 7)]
         calf_passes(b0, 0, 0)
         wc[1, 0] = quantise("wc10", wc10_bf16, KP, 28672)
         v2.append(gather("v2_1", tab2_w[1][:].bitcast(U32), calf_list[:], C, U32, 30720))
         pick(5, held("tab2_w1", [P, HALF], F32)[:], halves[0])
-        wc01_bf16 = held("stage01", [P, PACK * KP], BF16)[:]
-        cast_on_gpsimd(wc01_bf16, 0, 1)
-        wc11_bf16 = held("stage11", [P, PACK * KP], BF16)[:]
-        nc.scalar.copy(*cast_views(wc11_bf16, 1, 1, 0, "q t j i"))
+        wc1_bf16 = at(0, "stage_rb1", [P, 2 * PACK * KP], BF16)
+        cast_on_gpsimd(wc1_bf16[:, 0 : PACK * KP], 0, 1)
+        for half in halves:
+            nc.scalar.copy(*cast_views(wc1_bf16[:, PACK * KP : 2 * PACK * KP], 1, 1, half.start, "q t j i"))
         calf_passes(b0, 0, 1)
         adds(x0, 0, b0)
-        f0 = at(16384, "f0", [P, PACK, C], F32)
-        factors(f0, x0, 0)
-        for s in range(2 * PACK - 2, 2 * PACK):
-            sire_sums([(s, 0), (s, 1)], 2 * s - 8)
-        nc.vector.tensor_copy(*cast_views(wc11_bf16, 1, 1, HALF, "q t j i"))
-        wc[0, 1] = quantise("wc01", wc01_bf16, KP)
+        f0 = at(16384, "f0", [P, 2, PACK, HALF], F32)
+        for e in range(2):
+            factors(f0[:, e], x0[:, :, halves[e]], 0)
+        sire_sums([(2 * PACK - 1, 0), (2 * PACK - 1, 1)], 6)
+        codes, scales = quantise("wc_rb1", wc1_bf16[:], 2 * KP)
         b1 = [bank(C, number) for number in (0, 1, 2, 3)]
-        calf_passes(b1, 1, 0)
-        wc[1, 1] = quantise("wc11", wc11_bf16, KP)
-        pick(5, at(2048, "pick5", [P, HALF], F32)[:], halves[1])
+        for a in range(2):
+            wc[a, 1] = codes[:, KP * a : KP * (a + 1)], scales[:, KP * a : KP * (a + 1)]
+            calf_passes(b1, 1, a)
+        pick(5, at(3072, "pick5", [P, HALF], F32)[:], halves[1])
         for s in range(6, 2 * PACK):
-            pick(s, at({6: 4096, 7: 0}[s], "pick%d" % s, [P, C], F32)[:])
-        z0 = held("stage11", [P, PACK * 3 * QUARTER], BF16)[:]
-        for c in range(0, 3 * QUARTER, QUARTER):
-            multiply(nc.gpsimd, z0[:, PACK * c : PACK * (c + QUARTER)], x0, f0, slice(c, c + QUARTER))
+            pick(s, at(4096 + 2048 * (s - 6), "pick%d" % s, [P, C], F32)[:])
+
+        def z0_quarter(engine, z, q):
+            e, c = divmod(q, 2)
+            multiply(engine, z, x0[:, :, QUARTER * q : QUARTER * (q + 1)], f0[:, e, :, QUARTER * c : QUARTER * (c + 1)])
+
+        z0 = at(0, "z0", [P, PACK * 3 * QUARTER], BF16)[:]
+        for q in range(3):
+            z0_quarter(nc.gpsimd, z0[:, KP * q : KP * (q + 1)], q)
         wm0_bf16 = cast_wmerit(0, held("stage_wm0", [P, PACK * N], BF16)[:], slice(0, N))
-        calf_passes(b1, 1, 1)
 
         x1 = held("x1", [P, PACK, C], F32)
         adds(x1, 1, b1)
@@ -309,7 +311,7 @@ def tile_list_sire_calf_merit_kernel(
 
         def make_z1(name, calves):
             z = held(name, [P, PACK * (calves.stop - calves.start)], BF16)[:]
-            multiply(nc.vector, z, x1, f1, calves)
+            multiply(nc.vector, z, x1[:, :, calves], f1[:, :, calves])
             return z
 
         def merit_passes(accs, weights, zq, start, stop):
@@ -339,7 +341,7 @@ def tile_list_sire_calf_merit_kernel(
             nc.sync.dma_start(out[P * n : P * (n + 1), halves[u]], res[:])
 
         z0_last = at(5120, "z0_last", [P, PACK * QUARTER], BF16)[:]
-        multiply(nc.vector, z0_last, x0, f0, slice(3 * QUARTER, C))
+        z0_quarter(nc.vector, z0_last, 3)
         wm0 = columns(quantise("wm0", wm0_bf16, N, 4096), 4)
         merit_passes([acc[:] for acc in merits[0]], wm0, quantise("zq0_first", z0[:, 0 : PACK * HALF], HALF, 4608), True, False)
         z0_third = quantise("zq0_third", z0[:, PACK * HALF : PACK * 3 * QUARTER], QUARTER, 4864)

@@ -88,7 +88,7 @@ def tile_list_sire_calf_merit_kernel(
             by_slice = raw[:].rearrange("p a (q t) -> p a t q", t=PACK)
             for first, last in groups:
                 shape = [P, 2 * (last - first) * PAIRS]
-                dealt = at(24576, "ws4", shape, I32) if (rb, first) == (1, 0) else held("ws%d_%d" % (rb, first), shape, I32)
+                dealt = at(0, "ws4", shape, I32) if (rb, first) == (1, 0) else held("ws%d_%d" % (rb, first), shape, I32)
                 engine.tensor_copy(dealt[:].rearrange("p (a t q) -> p a t q", a=2, q=PAIRS), by_slice[:, :, first:last, :])
                 for t in range(first, last):
                     for a in range(2):
@@ -222,7 +222,7 @@ def tile_list_sire_calf_merit_kernel(
         sire_sums([(0, 0), (0, 1), (1, 0), (1, 1)], 0)
         for s in range(2, PACK + 1):
             sire_sums([(s, 0), (s, 1)], 2 * (s % 2))
-        wc10_bf16 = at(24576, "stage10", [P, PACK * KP], BF16)[:]
+        wc10_bf16 = at(0, "stage10", [P, PACK * KP], BF16)[:]
         nc.scalar.copy(*cast_views(wc10_bf16, 1, 0, 0, "q t j i"))
         for s in range(PACK + 1, 2 * PACK - 1):
             sire_sums([(s, 0), (s, 1)], 2 * (s % 2))

@@ -26,6 +26,7 @@ QUARTER = C // 4
 LIST_ROWS = 16
 SPREAD = 4
 RUN = 2
+LINE = 4
 PAIRS = P // RUN
 
 
@@ -207,8 +208,8 @@ def tile_list_sire_calf_merit_kernel(
 
         def cast_wmerit(rb, grouped, cols):
             nc.scalar.activation(
-                grouped.rearrange("p (c i j) -> p c j i", i=2, j=PACK),
-                wm_raw[rb][:, :, cols].rearrange("p j (c i) -> p c j i", i=2), COPY)
+                grouped.rearrange("p (c i j) -> p c j i", i=LINE, j=PACK),
+                wm_raw[rb][:, :, cols].rearrange("p j (c i) -> p c j i", i=LINE), COPY)
             return grouped
 
         def quantise(name, grouped, width, offset=None):
@@ -267,7 +268,7 @@ def tile_list_sire_calf_merit_kernel(
 
         def multiply(engine, z, x, f):
             order = "p t (c i) -> p c t i"
-            engine.tensor_tensor(z.rearrange("p (c i t) -> p c t i", i=2, t=PACK), x.rearrange(order, i=2), f.rearrange(order, i=2), MULT)
+            engine.tensor_tensor(z.rearrange("p (c i t) -> p c t i", i=LINE, t=PACK), x.rearrange(order, i=LINE), f.rearrange(order, i=LINE), MULT)
 
         b0 = [bank(C, number) for number in (4, 5, 6, 7)]
         calf_passes(b0, 0, 0)

@@ -150,11 +150,11 @@ def tile_list_sire_calf_merit_kernel(
         deal_scale_rows(v2_sc[0], 4, calf_rows, 0, range(2, 4))
         nc.sync.dma_start(tab2_w[1][:], words_of(tab2_words, 1))
         deal_scale_rows(v2_sc[1], 8, calf_rows, 1, range(0, 2))
-        load_wcalf(held("raw01_0", [P, PACK, HALF], F32), 0, 1, halves[0])
+        load_wcalf(held("raw01_0", [P, PACK, 3 * QUARTER], F32), 0, 1, slice(0, 3 * QUARTER))
         deal_scale_rows(v2_sc[1], 8, calf_rows, 1, range(2, 4))
         load_wcalf(held("raw11_0", [P, PACK, HALF], F32), 1, 1, halves[0])
-        load_wcalf(held("raw01_1", [P, PACK, HALF], F32), 0, 1, halves[1])
         load_wcalf(at(16384, "raw11_1", [P, PACK, HALF], F32), 1, 1, halves[1])
+        load_wcalf(held("raw01_1", [P, PACK, QUARTER], F32), 0, 1, slice(3 * QUARTER, KP))
         load_gains(0)
         wm_raw = [held("tab_w%d" % rb, [P, PACK, N], F32) for rb in range(2)]
         for rb in range(2):
@@ -200,10 +200,10 @@ def tile_list_sire_calf_merit_kernel(
             q0 = first // (PACK * RUN)
             return dst[:, q0 : q0 + src.shape[1]], src
 
-        def cast_on_gpsimd(grouped, a, rb):
-            for e in range(2):
-                dst, src = cast_views(grouped, a, rb, HALF * e, "q t i j")
-                for q in range(0, PAIRS // 2, 16):
+        def cast_on_gpsimd(grouped, a, rb, firsts):
+            for first in firsts:
+                dst, src = cast_views(grouped, a, rb, first, "q t i j")
+                for q in range(0, src.shape[1], 16):
                     nc.gpsimd.tensor_scalar(dst[:, q : q + 16], src[:, q : q + 16], 1.0, 0.0, MULT, ADD)
 
         def cast_wmerit(rb, grouped, cols):
@@ -219,7 +219,7 @@ def tile_list_sire_calf_merit_kernel(
             return codes[:], scales[:]
 
         wc00_bf16 = at(28672, "stage00", [P, PACK * KP], BF16)[:]
-        cast_on_gpsimd(wc00_bf16, 0, 0)
+        cast_on_gpsimd(wc00_bf16, 0, 0, [0, HALF])
         sire_sums([(0, 0), (0, 1), (1, 0), (1, 1)], 0)
         for s in range(2, PACK + 1):
             sire_sums([(s, 0), (s, 1)], 2 * (s % 2))
@@ -276,7 +276,7 @@ def tile_list_sire_calf_merit_kernel(
         v2.append(gather("v2_1", tab2_w[1][:].bitcast(U32), calf_list[:], C, U32, 30720))
         pick(5, held("tab2_w1", [P, HALF], F32)[:], halves[0])
         wc1_bf16 = at(0, "stage_rb1", [P, 2 * PACK * KP], BF16)
-        cast_on_gpsimd(wc1_bf16[:, 0 : PACK * KP], 0, 1)
+        cast_on_gpsimd(wc1_bf16[:, 0 : PACK * KP], 0, 1, [0, 3 * QUARTER])
         for half in halves:
             nc.scalar.copy(*cast_views(wc1_bf16[:, PACK * KP : 2 * PACK * KP], 1, 1, half.start, "q t j i"))
         calf_passes(b0, 0, 1)

from contextlib import ExitStack

import concourse.mybir as mybir

K, H, N, T, S, T2, C = 1024, 1024, 512, 4096, 1024, 2048, 512
FLOPS = 2 * K * H * S + 2 * K * H * C + 2 * H * N * C

F32 = mybir.dt.float32
BF16 = mybir.dt.bfloat16
I32 = mybir.dt.int32
U32 = mybir.dt.uint32
U16 = mybir.dt.uint16
U8 = mybir.dt.uint8
FP8X4 = mybir.dt.float8_e4m3fn_x4
FP4X4 = mybir.dt.float4_e2m1fn_x4
ADD = mybir.AluOpType.add
MULT = mybir.AluOpType.mult
COPY = mybir.ActivationFunctionType.Copy

P = 128
PACK = 4
KP = P * PACK
BANK = 512
HALF = C // 2
QUARTER = C // 4
LIST_ROWS = 16
SPREAD = 4
RUN = 2
LINE = 4
PAIRS = P // RUN


def tile_list_sire_calf_merit_kernel(
    tc, tab_words, tab_scales, offs, pos1, tab2_words, tab2_scales, offs2,
    wsire_words, wsire_scales, wcalf, gain, wmerit, out,
):
    nc = tc.nc
    with ExitStack() as ctx:
        keep = ctx.enter_context(tc.tile_pool(name="keep", bufs=1))
        placed = ctx.enter_context(tc.tile_pool(name="placed", bufs=1))
        psum = ctx.enter_context(tc.psum_pool(name="psum", bufs=1))

        def held(name, shape, dtype):
            return keep.tile(shape, dtype, name=name, align_bytes=64)

        def at(offset, name, shape, dtype):
            return placed.tile(shape, dtype, name=name, offset=offset, align_bytes=64)

        def bank(width, number):
            return psum.tile([P, width], F32, name="bank%d" % number)

        sire_list = held("sire_list", [P, S // LIST_ROWS], U16)
        calf_list = held("calf_list", [P, C // LIST_ROWS], U16)
        pick_list = held("pick_list", [P, C // LIST_ROWS], U16)

        tab_sc = held("tab_sc", [P, T], U8)
        ws_sc_raw = held("ws_sc_raw", [P, 2 * H], U8)
        tab2_sc = held("tab2_sc", [P, T2], U8)
        v_sc = [held("v_sc%d" % a, [P, S], U8) for a in range(2)]
        v2_sc = [held("v2_sc%d" % a, [P, C], U8) for a in range(2)]
        for scale_tile in (tab_sc, ws_sc_raw, tab2_sc, v_sc[0], v_sc[1], v2_sc[0], v2_sc[1]):
            nc.gpsimd.memset(scale_tile[:].bitcast(I32), 0)

        def words_of(table, a):
            return table[a].rearrange("p t i -> p (t i)").bitcast(I32)

        def load_part(window, table, a, cols):
            nc.sync.dma_start(window[:, cols], words_of(table, a)[:, cols])

        def load_scale_rows(window, scales):
            nc.sync.dma_start(window[0:P:SPREAD, :].bitcast(I32), scales.bitcast(I32).rearrange("a q c -> (a q) c"))

        def deal_scale_rows(plane, first, gathered, a, rows):
            for r in rows:
                start = 64 * a + SPREAD * r
                nc.sync.dma_start(plane[first + r : P : 32, :].bitcast(I32), gathered[start : 64 * (a + 1) : 16, :].bitcast(I32))

        def gather(name, window, offsets, count, dtype, offset=None):
            gathered = held(name, [P, count], dtype) if offset is None else at(offset, name, [P, count], dtype)
            nc.vector.tensor_copy(gathered[:], window.indirect(offsets))
            return gathered

        ws = {}

        def load_and_deal_wsire(rb, engine, groups):
            raw = held("ws_raw%d" % rb, [P, 2, KP // RUN], I32)
            pairs = wsire_words.bitcast(I32)[:, :, KP // RUN * rb : KP // RUN * (rb + 1)]
            nc.sync.dma_start(raw[:], pairs.rearrange("a p c -> p a c"))
            by_slice = raw[:].rearrange("p a (q t) -> p a t q", t=PACK)
            for first, last in groups:
                shape = [P, 2 * (last - first) * PAIRS]
                dealt = at(0, "ws4", shape, I32) if (rb, first) == (1, 0) else held("ws%d_%d" % (rb, first), shape, I32)
                engine.tensor_copy(dealt[:].rearrange("p (a t q) -> p a t q", a=2, q=PAIRS), by_slice[:, :, first:last, :])
                for t in range(first, last):
                    for a in range(2):
                        start = PAIRS * (a * (last - first) + t - first)
                        ws[PACK * rb + t, a] = dealt[:, start : start + PAIRS]

        lead = 3 * T // 8
        tab_w = [held("tab_w%d" % a, [P, T], I32) for a in range(2)]
        load_part(tab_w[0], tab_words, 0, slice(0, lead))
        nc.sync.dma_start(sire_list[:], offs)
        load_scale_rows(tab_sc, tab_scales)
        for q in range(4):
            nc.sync.dma_start(
                ws_sc_raw[32 * q : 32 * q + 4, :].bitcast(I32).rearrange("r (a c) -> r a c", a=2),
                wsire_scales[:, 4 * q : 4 * q + 4, :].bitcast(I32).rearrange("a r c -> r a c"),
            )
        load_part(tab_w[0], tab_words, 0, slice(lead, T))
        sire_rows = gather("sire_rows", tab_sc[:], sire_list[:], S, U8)
        ws_sc = held("ws_sc", [P, 2 * H], U8)
        nc.vector.tensor_copy(
            ws_sc[:].bitcast(U16).rearrange("p (b a t q) -> p b a t q", b=2, a=2, t=PACK),
            ws_sc_raw[:].bitcast(U16).rearrange("p (a b q t) -> p b a t q", a=2, b=2, t=PACK),
        )
        v0 = gather("v0", tab_w[0][:].bitcast(U32), sire_list[:], S, U32)
        nc.sync.dma_start(calf_list[:], offs2)
        load_and_deal_wsire(0, nc.vector, [(0, PACK)])
        load_scale_rows(tab2_sc, tab2_scales)
        calf_rows = gather("calf_rows", tab2_sc[:], calf_list[:], C, U8)
        load_part(tab_w[1], tab_words, 1, slice(0, lead))
        deal_scale_rows(v_sc[0], 0, sire_rows, 0, range(4))
        load_part(tab_w[1], tab_words, 1, slice(lead, T))
        deal_scale_rows(v_sc[1], 0, sire_rows, 1, range(4))
        tab2_w = [held("tab2_w%d" % a, [P, T2], I32) for a in range(2)]
        nc.sync.dma_start(tab2_w[0][:], words_of(tab2_words, 0))
        load_and_deal_wsire(1, nc.gpsimd, [(0, 1), (1, PACK)])
        nc.sync.dma_start(pick_list[:], pos1)

        wc_raw = {}

        def load_wcalf(raw, a, rb, cols):
            rows = wcalf[KP * a : KP * (a + 1), KP * rb + cols.start : KP * rb + cols.stop]
            nc.sync.dma_start(raw[:], rows.rearrange("(p j) c -> p j c", j=PACK))
            wc_raw[a, rb, cols.start] = raw

        gains = [at(32768, "gains0", [P, PACK], F32)[:], held("stage_wm1", [P, PACK], F32)[:]]

        def load_gains(rb):
            with nc.allow_non_contiguous_dma(reason="512 gains dealt to their partitions and slices"):
                dealt = gain[KP * rb : KP * (rb + 1)].rearrange("(q t i) -> i q t", t=PACK, i=RUN)
                for i in range(RUN):
                    nc.sync.dma_start(gains[rb][i:P:RUN, :], dealt[i])

        halves = [slice(HALF * e, HALF * (e + 1)) for e in range(2)]
        for e in range(2):
            load_wcalf(held("raw00_%d" % e, [P, PACK, HALF], F32), 0, 0, halves[e])
        deal_scale_rows(v2_sc[0], 4, calf_rows, 0, range(0, 2))
        load_wcalf(at(8192, "raw10", [P, PACK, KP], F32), 1, 0, slice(0, KP))
        deal_scale_rows(v2_sc[0], 4, calf_rows, 0, range(2, 4))
        nc.sync.dma_start(tab2_w[1][:], words_of(tab2_words, 1))
        deal_scale_rows(v2_sc[1], 8, calf_rows, 1, range(0, 2))
        load_wcalf(held("raw01_0", [P, PACK, 3 * QUARTER], F32), 0, 1, slice(0, 3 * QUARTER))
        deal_scale_rows(v2_sc[1], 8, calf_rows, 1, range(2, 4))
        load_wcalf(held("raw11_0", [P, PACK, HALF], F32), 1, 1, halves[0])
        load_wcalf(at(16384, "raw11_1", [P, PACK, HALF], F32), 1, 1, halves[1])
        load_wcalf(held("raw01_1", [P, PACK, QUARTER], F32), 0, 1, slice(3 * QUARTER, KP))
        load_gains(0)
        wm_raw = [held("tab_w%d" % rb, [P, PACK, N], F32) for rb in range(2)]
        for rb in range(2):
            rows = wmerit[KP * rb : KP * (rb + 1), :].rearrange("(q t i) c -> i q t c", t=PACK, i=RUN)
            for i in range(RUN):
                nc.sync.dma_start(wm_raw[rb][i:P:RUN, :, :], rows[i])
        load_gains(1)

        part = BANK // LIST_ROWS
        v1 = [gather("v1_%d" % u, tab_w[1][:].bitcast(U32), sire_list[:, part * u : part * (u + 1)], BANK, U32) for u in range(2)]

        def sire_pass(acc, s, u, a):
            rb, t = divmod(s, PACK)
            moving = v0[:, BANK * u : BANK * (u + 1)] if a == 0 else v1[u][:]
            group = PACK * a + t
            nc.tensor.matmul_mx(
                out=acc[:],
                lhsT=ws[s, a].bitcast(U8).bitcast(FP4X4),
                lhsT_scale=ws_sc[:, H * rb + P * group : H * rb + P * (group + 1)],
                rhs=moving.bitcast(FP8X4),
                rhs_scale=v_sc[a][:, BANK * u : BANK * (u + 1)],
                start=(a == 0),
                stop=(a == 1),
            )

        h = [
            at({5: 8192, 6: 12288, 7: 32768}[s], "h%d" % s, [P, S], F32) if s > PACK else held("h%d" % s, [P, S], F32)
            for s in range(2 * PACK)
        ]

        def sire_sums(sums, first):
            banks = [bank(BANK, first + i) for i in range(len(sums))]
            for acc, (s, u) in zip(banks, sums):
                sire_pass(acc, s, u, 0)
            for acc, (s, u) in zip(banks, sums):
                sire_pass(acc, s, u, 1)
                nc.scalar.activation(h[s][:, BANK * u : BANK * (u + 1)], acc[:], COPY)

        def cast_views(grouped, a, rb, first, order):
            raw = wc_raw[a, rb, first]
            src = raw[:].rearrange("p j (q t i) -> p " + order, t=PACK, i=RUN)
            dst = grouped.rearrange("p (t q i j) -> p " + order, t=PACK, i=RUN, j=PACK)
            q0 = first // (PACK * RUN)
            return dst[:, q0 : q0 + src.shape[1]], src

        def cast_on_gpsimd(grouped, a, rb, firsts):
            for first in firsts:
                dst, src = cast_views(grouped, a, rb, first, "q t i j")
                for q in range(0, src.shape[1], 16):
                    nc.gpsimd.tensor_scalar(dst[:, q : q + 16], src[:, q : q + 16], 1.0, 0.0, MULT, ADD)

        def cast_wmerit(rb, grouped, cols):
            nc.scalar.activation(
                grouped.rearrange("p (c i j) -> p c j i", i=LINE, j=PACK),
                wm_raw[rb][:, :, cols].rearrange("p j (c i) -> p c j i", i=LINE), COPY)
            return grouped

        def quantise(name, grouped, width, offset=None):
            codes = held(name + "_codes", [P, width], U32)
            scales = held(name + "_scales", [P, width], U8) if offset is None else at(offset, name + "_scales", [P, width], U8)
            nc.vector.quantize_mx(out=codes[:].bitcast(FP8X4), scales=scales[:], in_=grouped)
            return codes[:], scales[:]

        wc00_bf16 = at(28672, "stage00", [P, PACK * KP], BF16)[:]
        cast_on_gpsimd(wc00_bf16, 0, 0, [0, HALF])
        sire_sums([(0, 0), (0, 1), (1, 0), (1, 1)], 0)
        for s in range(2, PACK + 1):
            sire_sums([(s, 0), (s, 1)], 2 * (s % 2))
        wc10_bf16 = at(0, "stage10", [P, PACK * KP], BF16)[:]
        nc.scalar.copy(*cast_views(wc10_bf16, 1, 0, 0, "q t j i"))
        for s in range(PACK + 1, 2 * PACK - 1):
            sire_sums([(s, 0), (s, 1)], 2 * (s % 2))

        v2 = [gather("v2_0", tab2_w[0][:].bitcast(U32), calf_list[:], C, U32)]
        wc = {}
        wc[0, 0] = quantise("wc00", wc00_bf16, KP)
        picked = {}

        def pick(s, dst, calves=slice(0, C)):
            offsets = pick_list[:, calves.start // LIST_ROWS : calves.stop // LIST_ROWS]
            nc.vector.tensor_copy(dst, h[s][:].indirect(offsets))
            picked.setdefault(s, []).append((calves, dst))

        x0 = held("x0", [P, PACK, C], F32)
        pick(0, held("tab2_w0", [P, C], F32)[:])
        for s in range(1, PACK):
            pick(s, x0[:, s, :])
        pick(4, held("pick4", [P, C], F32)[:])

        def calf_passes(sums, rb, a):
            codes, scales = wc[a, rb]
            for t in range(PACK):
                nc.tensor.matmul_mx(
                    out=sums[t][:],
                    lhsT=codes[:, P * t : P * (t + 1)].bitcast(FP8X4),
                    lhsT_scale=scales[:, P * t : P * (t + 1)],
                    rhs=v2[a][:].bitcast(FP8X4),
                    rhs_scale=v2_sc[a][4 * (a + 1) : P, :],
                    start=(a == 0),
                    stop=(a == 1),
                )

        def adds(x, rb, sums):
            for t in range(PACK):
                for calves, values in picked[PACK * rb + t]:
                    nc.vector.tensor_tensor(x[:, t, calves], values, sums[t][:, calves], ADD)

        def factors(f, x, rb):
            for t in range(PACK):
                nc.scalar.activation(f[:, t, :], x[:, t, :], COPY, bias=1.0, scale=gains[rb][:, t : t + 1])

        def multiply(engine, z, x, f):
            order = "p t (c i) -> p c t i"
            engine.tensor_tensor(z.rearrange("p (c i t) -> p c t i", i=LINE, t=PACK), x.rearrange(order, i=LINE), f.rearrange(order, i=LINE), MULT)

        b0 = [bank(C, number) for number in (4, 5, 6, 7)]
        calf_passes(b0, 0, 0)
        wc[1, 0] = quantise("wc10", wc10_bf16, KP, 28672)
        v2.append(gather("v2_1", tab2_w[1][:].bitcast(U32), calf_list[:], C, U32, 30720))
        pick(5, held("tab2_w1", [P, HALF], F32)[:], halves[0])
        wc1_bf16 = at(0, "stage_rb1", [P, 2 * PACK * KP], BF16)
        cast_on_gpsimd(wc1_bf16[:, 0 : PACK * KP], 0, 1, [0, 3 * QUARTER])
        for half in halves:
            nc.scalar.copy(*cast_views(wc1_bf16[:, PACK * KP : 2 * PACK * KP], 1, 1, half.start, "q t j i"))
        calf_passes(b0, 0, 1)
        adds(x0, 0, b0)
        f0 = at(16384, "f0", [P, 2, PACK, HALF], F32)
        for e in range(2):
            factors(f0[:, e], x0[:, :, halves[e]], 0)
        sire_sums([(2 * PACK - 1, 0), (2 * PACK - 1, 1)], 6)
        codes, scales = quantise("wc_rb1", wc1_bf16[:], 2 * KP)
        b1 = [bank(C, number) for number in (0, 1, 2, 3)]
        for a in range(2):
            wc[a, 1] = codes[:, KP * a : KP * (a + 1)], scales[:, KP * a : KP * (a + 1)]
            calf_passes(b1, 1, a)
        pick(5, at(3072, "pick5", [P, HALF], F32)[:], halves[1])
        for s in range(6, 2 * PACK):
            pick(s, at(4096 + 2048 * (s - 6), "pick%d" % s, [P, C], F32)[:])

        def z0_quarter(engine, z, q):
            e, c = divmod(q, 2)
            multiply(engine, z, x0[:, :, QUARTER * q : QUARTER * (q + 1)], f0[:, e, :, QUARTER * c : QUARTER * (c + 1)])

        z0 = at(0, "z0", [P, PACK * 3 * QUARTER], BF16)[:]
        for q in range(3):
            z0_quarter(nc.gpsimd, z0[:, KP * q : KP * (q + 1)], q)
        wm0_bf16 = cast_wmerit(0, held("stage_wm0", [P, PACK * N], BF16)[:], slice(0, N))

        x1 = held("x1", [P, PACK, C], F32)
        adds(x1, 1, b1)
        f1 = held("tab_w0", [P, PACK, C], F32)
        factors(f1, x1, 1)
        stage_wm1 = held("stage_wm1", [P, 2, PACK * HALF], BF16)
        wm1_bf16 = [cast_wmerit(1, stage_wm1[:, e, :], halves[e]) for e in range(2)]

        def make_z1(name, calves):
            z = held(name, [P, PACK * (calves.stop - calves.start)], BF16)[:]
            multiply(nc.vector, z, x1[:, :, calves], f1[:, :, calves])
            return z

        def merit_passes(accs, weights, zq, start, stop):
            for n in range(N // P):
                codes, scales = weights[n]
                nc.tensor.matmul_mx(
                    out=accs[n],
                    lhsT=codes.bitcast(FP8X4),
                    lhsT_scale=scales,
                    rhs=zq[0].bitcast(FP8X4),
                    rhs_scale=zq[1],
                    start=start,
                    stop=stop,
                )

        def columns(quantised, count):
            return [tuple(plane[:, P * n : P * (n + 1)] for plane in quantised) for n in range(count)]

        merits = [[bank(HALF, first + n) for n in range(N // P)] for first in (PACK, 0)]

        def store(u, n, engine):
            res = held("res%d%d" % (u, n), [P, HALF], F32)
            if engine == "vector":
                nc.vector.tensor_copy(res[:], merits[u][n][:])
            else:
                nc.scalar.activation(res[:], merits[u][n][:], COPY)
            nc.sync.dma_start(out[P * n : P * (n + 1), halves[u]], res[:])

        z0_last = at(5120, "z0_last", [P, PACK * QUARTER], BF16)[:]
        z0_quarter(nc.vector, z0_last, 3)
        wm0 = columns(quantise("wm0", wm0_bf16, N, 4096), 4)
        merit_passes([acc[:] for acc in merits[0]], wm0, quantise("zq0_first", z0[:, 0 : PACK * HALF], HALF, 4608), True, False)
        z0_third = quantise("zq0_third", z0[:, PACK * HALF : PACK * 3 * QUARTER], QUARTER, 4864)
        for e, zq in enumerate((z0_third, quantise("zq0_last", z0_last, QUARTER))):
            merit_passes([acc[:, P * e : P * (e + 1)] for acc in merits[1]], wm0, zq, e == 0, False)
        z1_first = make_z1("z1_first", halves[0])
        wm1 = columns(quantise("wm1_0", wm1_bf16[0], HALF), 2)
        zq1_first = quantise("zq1_first", z1_first, HALF)
        wm1.extend(columns(quantise("wm1_1", wm1_bf16[1], HALF), 2))
        merit_passes([acc[:] for acc in merits[0]], wm1, zq1_first, False, True)
        z1_last = [make_z1("z1_last%d" % e, slice(HALF + QUARTER * e, HALF + QUARTER * (e + 1))) for e in range(2)]
        for n in range(N // P):
            store(0, n, "scalar")
        for e in range(2):
            zq = quantise("zq1_last%d" % e, z1_last[e], QUARTER)
            merit_passes([acc[:, P * e : P * (e + 1)] for acc in merits[1]], wm1, zq, False, e == 1)
        for n in range(N // P):
            store(1, n, ("scalar", "vector")[n % 2])
